import numpy as np, ml_dtypes
CORES = [40,41,42,43,44,45,46,47]
N = 8
BF = ml_dtypes.bfloat16
def gentries(a):
    return np.ascontiguousarray(a.reshape(8, 16, -1).transpose(0, 2, 1)).reshape(8, -1)
def gtable(e):
    e = np.asarray(e); return np.ascontiguousarray(e.reshape(8, -1, 16).transpose(0, 2, 1)).reshape(128, -1).astype(np.int32)
V, C, S, L = 2048, 1536, 48, 256
RS, RP, Q, F = 3, 3, 3, 720
H = V - (N - 1) * S
I, J = np.arange(N)[:, None, None], np.arange(8)[None, :, None]
def mixed(rng, a):
    return np.take_along_axis(a, np.argsort(rng.random(a.shape), axis=-1), axis=-1)
def make(rng, npl=0, nq=0, own=None, power=1, tip=False):
    po = rng.random((N, 8, H))
    if tip: po[..., 0] = 2
    po = np.argsort(po, axis=-1)
    key = rng.random((N, 8, V)); key[I, J, po[..., :npl + nq]] = 9
    if own is not None: key[..., H:] += 5 * own[..., None]
    if tip: key[..., V - 1] = -2; key[..., 0] = -1
    U = H - npl - nq if npl + nq else V
    pool = np.argsort(key, axis=-1)[..., :U]
    m = rng.random((N, 8, C))
    if tip: m[..., 0] = -2; m[..., C - 1] = -1
    cp = np.argsort(m, axis=-1)
    mv = np.zeros((N, 8, C), np.int64); mv[I, J, cp[..., :npl]] = po[..., :npl]; mv[I, J, cp[..., npl:]] = pool[..., :C - npl][..., ::-1]
    u = np.sort((rng.random((N, 8, C, 16)) ** power * (U - 15)).astype(np.int64), axis=-1) + np.arange(16)
    va = np.take_along_axis(pool, u.reshape(N, 8, -1), axis=-1).reshape(N, 8, C, 16)
    eq = va == mv[..., None]; j = np.where(np.any(eq, axis=-1), np.argmax(eq, axis=-1), rng.integers(0, 16, (N, 8, C)))
    np.put_along_axis(va, j[..., None], mv[..., None], axis=-1)
    if tip:
        m = (rng.random((N, 8, C)) < 0.5) & ~np.any((va == 0) | (va == V - 1), axis=-1)
        for i, z in ((1, 0), (2, V - 1)):
            q = ((j + i) & 15)[..., None]
            np.put_along_axis(va, q, np.where(m[..., None], z, np.take_along_axis(va, q, axis=-1)), axis=-1)
    va = mixed(rng, va)
    p = rng.random((N, 8, L)); p[..., 0] = -1; p[..., 1] = 2
    nl = np.take_along_axis(cp[..., :L], np.argsort(p, axis=-1), axis=-1)
    o = mv.copy(); o[I, J, cp[..., :L + C // 16]] = V
    det = np.zeros((N, 8, V + 1), bool); det[I, J, o] = True
    w = rng.integers(0, 256, (N, 8, V)); w = np.where(det[..., :V], w, np.maximum(w, rng.integers(0, 256, (N, 8, V))))
    return {"x": rng.integers(0, 256, (N, 8, 16, V)), "w": w, "va": va, "k": rng.integers(0, 256, (N, 8, 16, C)), "s": rng.integers(0, 256, (N, 8, C)), "o": o, "nl": nl,
            "cp": cp, "mv": mv, "priv": po[..., :npl], "quiet": po[..., npl:npl + nq], "det": det[..., :V]}
def pack(a):
    return {"xv": np.ascontiguousarray(a["x"].reshape(N, 128, V)).astype(np.float32).astype(BF), "wv": a["w"].astype(np.int32), "va": np.stack([gtable(q.reshape(8, -1)) for q in a["va"]]),
            "kc": np.ascontiguousarray(a["k"].reshape(N, 128, C)).astype(np.float32).astype(BF), "sc": a["s"].astype(np.int32), "ov": a["o"].astype(np.int32), "nl": np.stack([gtable(q) for q in a["nl"]])}
def setup_inputs(rng):
    a = make(rng); a["nl"] = np.where(rng.random((N, 8, L)) < 0.03, C, a["nl"])
    return pack(a)
def setup_inputs_spread(rng):
    a = make(rng, power=2)
    a["x"] = (np.exp2(8 * rng.random((N, 8, 1, V))) * rng.random((N, 8, 16, V)) * (rng.random((N, 8, 1, V)) > 0.0625)).astype(np.int64)
    b = (np.exp2(8 * rng.random((N, 8, V)))).astype(np.int64) - 1; e = rng.integers(0, 256, (N, 8, V))
    a["w"] = np.where(a["det"], b, np.maximum(b, e))
    a["s"] = 256 - np.minimum(np.exp2(8 * rng.random((N, 8, C))).astype(np.int64), 256)
    a["k"] = (np.exp2(8 * rng.random((N, 8, 1, C))) * rng.random((N, 8, 16, C))).astype(np.int64)
    a["nl"] = np.where(rng.random((N, 8, L)) < rng.choice(np.array([0.0, 0.1, 0.5]), (N, 8, 1)), C, a["nl"])
    return pack(a)
def setup_inputs_ends(rng):
    n = 24; a = make(rng, n, 64, tip=True); qv, pv, c = a["quiet"], a["priv"], a["cp"][..., :n]
    a["x"] = 255 * rng.integers(0, 2, (N, 8, 16, V)); a["k"] = 255 * rng.integers(0, 2, (N, 8, 16, C))
    share = np.array([0.06, 0.12, 0.5])[(np.arange(N)[:, None] + np.arange(8)[None, :]) % 3][..., None]
    a["w"] = 255 * (rng.random((N, 8, V)) >= share).astype(np.int64); a["s"] = 255 * (rng.random((N, 8, C)) < 0.75).astype(np.int64)
    a["x"][I, J, :, qv[..., :32]] = 255; a["x"][I, J, :, qv[..., 32:]] = 0
    a["w"][I, J, qv] = 255; a["w"][I, J, pv] = 0; a["s"][I, J, c] = 255
    z = np.argsort(rng.random((N, 8, n, 32)), axis=-1)
    hi = np.take_along_axis(np.broadcast_to(qv[..., None, :32], z.shape), z, axis=-1)[..., :15]; lo = np.take_along_axis(np.broadcast_to(qv[..., None, 32:], z.shape), z, axis=-1)[..., :15]
    sel = (np.arange(n) % 3)[:, None]
    row = np.where(sel == 0, lo, np.where(sel == 1, hi, np.where(np.arange(15) < 8, hi, lo)))
    a["va"][I, J, c] = mixed(rng, np.concatenate([pv[..., None], row], axis=-1))
    kept = np.any(a["nl"][..., None] == c[..., None, :], axis=-1)
    void = np.where((np.arange(8) & 3) == 2, 0.5, 0.06)[None, :, None]
    a["nl"] = np.where((rng.random((N, 8, L)) < void) & ~kept, C, a["nl"])
    return pack(a)
def marked(rng, a, g):
    va = a["va"][N - 1, g]; a["o"][N - 1, g] = V; sp = H + rng.permutation(S); cl = rng.permutation(C); n = C // 16
    va[cl[2 * n:], rng.integers(0, 16, C - 2 * n)] = sp[0]
    va[cl[:n]] = sp[17:][np.argsort(rng.random((n, S - 17)), axis=1)[:, :16]]
    row = np.where(np.arange(16)[None, :] < rng.integers(1, 17, n)[:, None], sp[1:17][np.argsort(rng.random((n, 16)), axis=1)], va[cl[n:2 * n]])
    va[cl[n:2 * n]] = mixed(rng, row)
    xg = a["x"][N - 1, g]; q = sp[1:17]
    xg[:, q] = a["x"][N - 2, (1 - g) & 7][:, q]; xg[15, q] = (xg[15, q] + rng.integers(1, 256, 16)) & 255
def setup_inputs_corners(rng):
    ty = (np.arange(8)[None, :] + 3 * np.arange(N)[:, None]) & 7
    a = make(rng, L, 32, own=(((ty >= 1) & (ty <= 3)) | ((ty == 0) & (np.arange(N)[:, None] >= N - 2))).astype(np.int64)); va, w, s, o, nl = a["va"], a["w"], a["s"], a["o"], a["nl"]
    cls = np.arange(L) & 15; half = cls >= 8
    for r in range(N):
        for g in range(8):
            t = int(ty[r, g]); c = a["cp"][r, g]; pv = a["priv"][r, g]; qv = a["quiet"][r, g]
            if t == 0:
                nl[r, g] = C
                if r == N - 2: o[r, g] = a["mv"][r, g]
                if r == N - 1: marked(rng, a, g)
            elif t <= 3:
                oth = np.argsort(rng.random((L, L)) + 2 * (half[:, None] != half[None, :]) + 4 * np.eye(L), axis=1)[:, :15]
                q = np.argsort(rng.random((L, 31)), axis=1)[:, :15]
                row = np.where(np.arange(15)[None, :] < cls[:, None], pv[oth], qv[q])
                xg = a["x"][r, g]; kg = a["k"][r, g]; dead = pv[8:8 + Q]
                xg[:, qv[:16]] = 255
                row[16] = np.concatenate([dead, qv[:15 - Q]]); row[32] = np.concatenate([dead[:1], qv[:14]])
                old = np.zeros(16, np.int64)
                for i in range(RP):
                    z = 48 + 16 * i; still = rng.permutation(qv[:31])[:(14 - Q if i else 15)]
                    row[z] = np.concatenate([dead, pv[z - 16:z - 15], still]) if i else still
                    new = rng.integers(0, 256, 16)
                    if i == RP - 2: new[:15] = 0; new[15] = rng.integers(1, 256)
                    if i == RP - 1: new[:] = 0
                    kg[:, c[z]] = (new + old + np.add.reduce(xg[:, still], axis=1)) & 255
                    old = new
                z = 48 + 16 * (RP - 2); row[112] = np.concatenate([pv[z:z + 1], rng.permutation(qv[:31])[:14]])
                row = mixed(rng, row)
                va[r, g, c[:L]] = np.concatenate([pv[:, None], row], axis=1)
                w[r, g] = np.maximum(w[r, g], 1); w[r, g, pv] = 0; w[r, g, qv] = 255; s[r, g, c[:L]] = rng.integers(128, 256, L)
                if t == 2:
                    e = int(c[C - 1]); i = int(np.argmax(va[r, g, e] == o[r, g, e]))
                    va[r, g, e, i] = pv[0]; va[r, g, e, (i + 1) & 15] = qv[31]; o[r, g, e] = pv[0]; w[r, g, qv[31]] = 0; s[r, g, e] = 255
                if t == 3: nl[r, g, int(rng.integers(0, L))] = C
            elif t == 4:
                if r & 1: nl[r, g, :L - 1] = C
                else: nl[r, g, 1:] = C
            elif t == 5: o[r, g] = V
            elif t == 6: s[r, g, c[:L]] = 255 * rng.integers(0, 2, L)
    return pack(a)
def counted(rng, a, r, g):
    b = r & 3; z = (r + 1 + (r >> 2)) & 3; last = (RP - 1) * F
    va = a["va"][r, g]; o = a["o"][r, g]; a["nl"][r, g] = C; o[:] = V
    p = rng.permutation(F); m = np.concatenate([p[:L + b], np.arange(F, last), last + rng.permutation(C - last)[:z]])
    va[m, rng.integers(0, 16, len(m))] = H + 1 - (r & 1)
    if r & 1: va[p[F - 1], 0] = H + 1; o[p[F - 1]] = H + 1
def crossed(rng, a, r, g):
    va = a["va"][r, g]; w = a["w"][r, g]; s = a["s"][r, g]; o = a["o"][r, g]; nl = a["nl"][r, g]; c = a["cp"][r, g]; d = N - 1 - r
    w[:] = np.maximum(w, 1); s[c[:L]] = np.maximum(s[c[:L]], 1)
    if d:
        v = H + (d - 1) * S + np.arange(S); va[c[:S], 0] = v; w[v] = 0
        nl[np.isin(nl, c[S:L])] = C
        if r & 1:
            e = int(c[C - 1]); va[e, int(np.argmax(va[e] == o[e]))] = H + 1; o[e] = H + 1
        return
    v = a["mv"][r, g, c[:L]]; u = a["quiet"][r, g]; ok = np.ones(H, bool); ok[v] = False; ok[u] = False
    rest = np.nonzero(ok)[0]
    va[c[:L]] = np.concatenate([v[:, None], rest[np.argsort(rng.random((L, len(rest))), axis=1)[:, :15]]], axis=1)
    w[v] = 0; nl[np.isin(nl, c[L - 4:L])] = C
    e = c[C - 4:]; u = u[8:22]; xg = a["x"][r, g]
    a["k"][r, g][:, e] = (xg[:, o[e]] + np.add.reduce(xg[:, u], axis=1)[:, None]) & 255
    va[e] = mixed(rng, np.concatenate([o[e][:, None], (V - 1 - np.arange(4))[:, None], np.broadcast_to(u, (4, 14))], axis=1))
def setup_inputs_crowd(rng):
    ty = (np.arange(8)[None, :] + np.arange(N)[:, None]) & 3
    a = make(rng, 0, 24, own=(ty == 3).astype(np.int64)); va, w, s, o = a["va"], a["w"], a["s"], a["o"]
    for r in range(N):
        for g in range(8):
            t = int(ty[r, g])
            if t == 3:
                if ((r + g) & 7) == N - 1: crossed(rng, a, r, g)
                else: counted(rng, a, r, g)
                continue
            c = a["nl"][r, g]; qv = a["quiet"][r, g]; i = np.arange(L)
            n = rng.integers(0, 4, L) if t == 2 else np.zeros(L, np.int64)
            p = rng.integers(0, 15, L); q = p + 1 + (rng.random(L) * (15 - p)).astype(np.int64)
            row = va[r, g, c]; keep = row.copy(); row[i, p] = qv[2 * n]; row[i, q] = qv[2 * n + 1]
            if t == 1: z = 0 if r & 1 else L - 1; row[z] = keep[z]
            va[r, g, c] = row; w[r, g] = np.maximum(w[r, g], 1); w[r, g, qv] = 0; s[r, g, c] = np.maximum(s[r, g, c], 1)
            e = int(a["cp"][r, g, C - 1]); h = int(np.argmax(va[r, g, e] == o[r, g, e]))
            va[r, g, e, h] = qv[0]
            if h == 15: h = 14; va[r, g, e, h] = qv[0]
            va[r, g, e, h + 1] = qv[1]; o[r, g, e] = qv[0]; s[r, g, e] = max(int(s[r, g, e]), 1)
    return pack(a)
def setup_inputs_calm(rng):
    a = make(rng); base = np.array([0, 1, 100, 215])[(np.arange(N)[:, None] + np.arange(8)[None, :]) & 3][..., None]
    a["w"] = base + ((a["w"] * 41) >> 8)
    low = np.min(np.take_along_axis(a["w"], a["va"].reshape(N, 8, -1), axis=-1).reshape(N, 8, C, 16), axis=-1)
    a["s"] = np.minimum(low + rng.integers(0, 4, (N, 8, C)), 255)
    return pack(a)
def check_inputs(d):
    bad = []; u = {}
    for k, lo, hi in (("xv", 0, 255), ("wv", 0, 255), ("va", 0, V - 1), ("kc", 0, 255), ("sc", 0, 255), ("ov", 0, V), ("nl", 0, C)):
        v = np.nan_to_num(np.asarray(d[k]).astype(np.float64), nan=-1.0, posinf=1e9, neginf=-1e9)
        if not np.all((v >= lo) & (v <= hi) & (v == np.floor(v))): bad.append("range of " + k)
        u[k] = np.clip(v, lo, hi).astype(np.int64)
    a = np.stack([gentries(q) for q in u["va"]]).reshape(N, 8, C, 16); n = np.stack([gentries(q) for q in u["nl"]]); o = u["ov"]
    if np.any(np.diff(np.sort(a, axis=-1), axis=-1) == 0): bad.append("va: the variables of a constraint differ")
    if np.any((o < V) & ~np.any(a == o[..., None], axis=-1)): bad.append("ov: an output is a variable of its constraint")
    for k, v, top in (("ov: outputs differ", o, V), ("nl: constraints in lanes differ", n, C)):
        z = np.sort(v, axis=-1)
        if np.any((z[..., 1:] == z[..., :-1]) & (z[..., 1:] < top)): bad.append(k)
    if np.any((n < C) & (np.take_along_axis(o, np.minimum(n, C - 1), axis=-1) < V)): bad.append("nl: constraints in lanes have no output")
    return bad
def meet(x, w, de, o, ch):
    me = np.arange(N)
    for d in range(1, N):
        pr = me ^ d; pg = (d - np.arange(8)) & 7; at = H + (d - 1) * S; cs = slice(at, at + S)
        mx, mw, md = x[..., cs].copy(), w[..., cs].copy(), de[..., cs] < C
        px, pw, pd = mx[pr][:, pg], mw[pr][:, pg], md[pr][:, pg]
        high = (me > pr)[:, None, None]
        lose = np.where(md & pd, np.where(mw == pw, high, mw < pw), np.where(md | pd, pd, high))
        r, g, i = np.nonzero(lose & md); o[r, g, de[r, g, at + i]] = V; de[r, g, at + i] = C
        ch[..., cs] |= lose & np.any(mx != px, axis=2)
        x[..., cs] = np.where(lose[:, :, None, :], px, mx); w[..., cs] = np.where(lose, pw, mw)
def raised(ch, a):
    return np.any(np.take_along_axis(ch, a.reshape(N, 8, -1), axis=-1).reshape(N, 8, C, 16), axis=-1)
def reference(xv, wv, va, kc, sc, ov, nl):
    x = xv.astype(np.float32).astype(np.int64).reshape(N, 8, 16, V); k = kc.astype(np.float32).astype(np.int64).reshape(N, 8, 16, C)
    w = wv.astype(np.int64); s = sc.astype(np.int64); o = ov.astype(np.int64)
    a = np.stack([gentries(q) for q in va]).astype(np.int64).reshape(N, 8, C, 16); ln = np.stack([gentries(q) for q in nl]).astype(np.int64)
    de = np.full((N, 8, V + 1), C, np.int64); de[I, J, o] = np.arange(C); de[..., V] = C
    fl = np.zeros((N, 8, C), bool)
    for step in range(RS):
        c = np.minimum(ln, C - 1); rows = a[I, J, c]; ww = w[I[..., None], J[..., None], rows]
        kk = np.argmin(ww, axis=-1); oo = np.take_along_axis(rows, kk[..., None], axis=-1)[..., 0]
        srt = np.sort(ww, axis=-1); st = s[I, J, c]
        live = (ln < C) & (srt[..., 0] < st); ln = np.where(live, ln, C)
        first = np.full((N, 8, V), L, np.int64); np.minimum.at(first, (I, J, oo), np.where(live, np.arange(L), L))
        act = live & (first[I, J, oo] == np.arange(L)); nw = np.minimum(st, srt[..., 1])
        r, g, j = np.nonzero(act); cc = c[r, g, j]; v = oo[r, g, j]; e = de[r, g, v]
        de[r, g, v] = cc; o[r, g, cc] = v; w[r, g, v] = nw[r, g, j]; x[r, g, :, v] = 256; fl[r, g, cc] = True
        q = e < C; o[r[q], g[q], e[q]] = V
        ln[r, g, j] = e
        ch = np.zeros((N, 8, V), bool); meet(x, w, de, o, ch); fl |= raised(ch, a)
    for t in range(RP):
        order = np.roll(np.arange(C), -t * F); ff = fl[:, :, order]
        r, g, i = np.nonzero(ff & (np.add.accumulate(ff.astype(np.int64), axis=-1) <= L)); c = order[i]
        has = o[r, g, c] < V
        fl[r[~has], g[~has], c[~has]] = False
        r, g, c = r[has], g[has], c[has]; v = o[r, g, c]; rows = a[r, g, c]; own = rows == v[:, None]
        stale = np.add.reduce(((x[r[:, None], g[:, None], 0, rows] == 256) & ~own).astype(np.int64), axis=1)
        go = stale <= Q; r, g, c, v, rows, own = r[go], g[go], c[go], v[go], rows[go], own[go]
        xs = x[r[:, None], g[:, None], :, rows]
        nx = (k[r, g, :, c] - np.add.reduce(np.where(own[:, :, None], 0, xs), axis=1)) & 255
        nw = np.minimum(s[r, g, c], np.min(np.where(own, 256, w[r[:, None], g[:, None], rows]), axis=1))
        ch = np.zeros((N, 8, V), bool); ch[r, g, v] = np.any(x[r, g, :, v] != nx, axis=1)
        x[r, g, :, v] = nx; w[r, g, v] = nw; fl[r, g, c] = False
        meet(x, w, de, o, ch); fl |= raised(ch, a)
    return {"y": x.reshape(N, 128, V).astype(np.float32).astype(BF), "yw": w.astype(np.float32), "yo": o.astype(np.float32), "yf": fl.astype(np.float32)}

@@ -1,0 +1,729 @@
+from concourse.bass import DstId, RemoteDMATransfer
+from concourse.mybir import AluOpType as OP, ActivationFunctionType as AF
+
+V_, C_, L_, H_, NR = 2048, 1536, 256, 1712, 336
+BIG = float(2 ** 25)
+F, B, I, U = "float32", "bfloat16", "int32", "uint16"
+
+
+def sb(shape, d):
+    return ("sbuf", [128] + shape, d)
+
+
+SCRATCH = {
+    "VA": sb([1544], I), "VAF": sb([1544], F), "RLI": sb([16, 96], I), "RL": sb([16, 96], U),
+    "XW": sb([2304], B), "W1": sb([2304], B), "DE": sb([3840], F), "S16": sb([1544], F),
+    "OO": sb([1856], F), "FLR": sb([1856], F), "KK": sb([1552], B), "CH": sb([2304], F),
+    "LW": sb([3072], F), "LX": sb([3072], F), "CV": sb([1536], F),
+    "NLI": sb([16], I), "OVI": sb([96], I), "W32": sb([512], I), "S32": sb([384], I), "O32": sb([384], I),
+    "W32B": sb([512], B), "S32B": sb([384], B), "O32F": sb([384], F),
+    "CI": sb([8], I), "COL": sb([24], F), "GV": sb([128], F), "VV": sb([128], F), "PV": sb([128], I),
+    "RV": sb([128], F), "ZV": sb([256], F), "Q16": sb([16], F), "JT": sb([2, 16], F), "CJ": sb([2, 96], F),
+    "JK": sb([2, 16], F), "BB": sb([128], B), "BW": sb([144], B), "BWF": sb([144], F), "IF": sb([128], F),
+    "MT": sb([24, 128], B), "REP": sb([4, 128], B), "REPF": sb([4, 128], F), "TM": sb([128], F),
+    "DGM": sb([256], B), "RS0": sb([256], B), "RS1": sb([256], B), "M0": sb([256], B), "ONE": sb([256], B),
+    "STL": sb([256], B), "D0": sb([2304], B), "DG": sb([32], B), "EL": sb([2], U), "TIE": sb([336], B),
+    "ZB": sb([256], B), "ONF": sb([256], F),
+    "LN": sb([16], U), "LNF": sb([16], F), "ROWS": sb([256], U), "RK": sb([256], F), "SG": sb([256], F),
+    "GW": sb([4096], B), "GX": sb([4096], B), "ST": sb([256], F), "SENT": sb([2, 16], F), "TT": sb([256], F),
+    "PQ": sb([2, 256], F), "ZZ": sb([256], F), "R1": sb([2, 16], I), "R2": sb([16, 3], I), "TB": sb([16, 16], B),
+    "TBT": sb([256], B), "O16": sb([256], U), "OF": sb([256], F), "NW": sb([256], B), "OF0": sb([256], F), "TC0": sb([2, 16], U),
+    "CNT": sb([2176], B), "SM": sb([12, 16], F), "TG": sb([16], U), "TC": sb([16], U), "OL": sb([16], U),
+    "CD0": sb([256], F), "CD1": sb([256], F), "MK": sb([256], F), "MX": sb([256], F), "SC": sb([256], F), "SD": sb([272], F),
+    "SND": sb([6, 7, 144], B), "LND": sb([6, 7, 144], B), "LOSE": sb([336], B),
+    "GR": sb([4, 1536], B), "ACC": sb([1536], B),
+    "FL": sb([96], B), "FK": sb([96], B), "INC": sb([96], B), "NF": sb([96], F), "RR": sb([2, 96], F), "PS": sb([96], U),
+    "OWN": sb([256], B), "P2": sb([256], B), "P2T": sb([256], B), "XO": sb([256], B), "KG": sb([256], B),
+    "NX": sb([2, 256], I), "DF": sb([256], F),
+    "OFF": sb([96], F), "OFL": sb([96], U), "YWB": sb([128], F), "YOB": sb([2, 96], F), "YFB": sb([96], F),
+}
+for _n in "ABCDEFGH":
+    SCRATCH["P" + _n] = ("psum", [128, 512], F)
+DMAS = ["nl", "ovf", "va", "w32", "s32", "o32", "xv", "kc", "rl", "y", "yw", "yo", "yf"]
+SEMAPHORES = ["sv", "sa", "sp", "sg", "ls"] + ["ar%d" % m for m in range(6)] + ["d_" + n for n in DMAS]
+M_I, M_NI, M_IB, M_B01, M_B2, M_B15, M_S00, M_S11, M_S10, M_S01, M_P, M_T0, M_T2, M_LA, M_LB, M_RS, M_A = (
+    0, 1, 2, 3, 4, 5, 6, 7, 8, 9, 10, 17, 18, 19, 20, 21, 22)
+INF = 10 ** 9
+WAITS = -15800.0
+
+
+def rank_program(g, core, T, topo):
+    rank = T.rank_of(core)
+    if rank is None:
+        return
+    Q = {"v": g.vector, "a": g.scalar, "p": g.tensor, "g": g, "s": g.sync}
+    SEM = {"v": "sv", "a": "sa", "p": "sp", "g": "sg"}
+    count = {}
+    seen = {e: {} for e in Q}
+    log = {}
+
+    def spec(a):
+        return (a, 0, INF) if isinstance(a, str) else a
+
+    def need(e, tok):
+        s, n = tok
+        if seen[e].get(s, 0) < n:
+            Q[e].wait_ge(T.sem[s], n)
+            seen[e][s] = n
+
+    def order(e, reads, writes):
+        toks = {}
+        for kind, lst in (("r", reads), ("w", writes)):
+            for a in lst:
+                name, lo, hi = spec(a)
+                ps = SCRATCH[name][0] == "psum"
+                for (l2, h2, k2, e2, tok) in log.get(name, []):
+                    if ps:
+                        hit = e2 != e or (e != "p" and (k2 == "w" or kind == "w"))
+                    elif l2 >= hi or lo >= h2:
+                        hit = False
+                    else:
+                        hit = k2 == "w" or kind == "w"
+                    if hit:
+                        toks[tok[0]] = max(toks.get(tok[0], 0), tok[1])
+        for s in toks:
+            need(e, (s, toks[s]))
+
+    def note(e, reads, writes, tok):
+        for kind, lst in (("r", reads), ("w", writes)):
+            for a in lst:
+                name, lo, hi = spec(a)
+                old = log.get(name, [])
+                if SCRATCH[name][0] == "psum":
+                    old = [r for r in old if r[3] == e and r[2] == "w" and kind == "r"]
+                    lo, hi = 0, INF
+                elif kind == "w":
+                    old = [r for r in old if not (lo <= r[0] and r[1] <= hi)]
+                else:
+                    old = [r for r in old if not (r[2] == "r" and r[3] == e and lo <= r[0] and r[1] <= hi)]
+                log[name] = old + [(lo, hi, kind, e, tok)]
+
+    def op(e, fns, reads, writes):
+        order(e, reads, writes)
+        if not isinstance(fns, list):
+            fns = [fns]
+        s = SEM[e]
+        ins = None
+        for f in fns:
+            ins = f()
+        ins.then_inc(T.sem[s], 1)
+        count[s] = count.get(s, 0) + 1
+        note(e, reads, writes, (s, count[s]))
+
+    def dma(e, name, pairs, reads, writes):
+        order(e, reads, writes)
+        s = "d_" + name
+        for o, i in pairs:
+            Q[e].dma_start(o, i).then_inc(T.sem[s], 16)
+        count[s] = 16 * len(pairs)
+        note("dma" + name, reads, writes, (s, count[s]))
+
+    v, a, pe = g.vector, g.scalar, g.tensor
+
+    def cp(out, in_, r, w):
+        op("v", lambda: v.tensor_copy(out, in_), r, w)
+
+    def tt(out, i0, i1, o, r, w):
+        op("v", lambda: v.tensor_tensor(out, i0, i1, o), r, w)
+
+    def ts(out, i0, s1, o0, r, w, s2=None, o1=None):
+        if s2 is None:
+            op("v", lambda: v.tensor_scalar(out, i0, s1, None, o0), r, w)
+        else:
+            op("v", lambda: v.tensor_scalar(out, i0, s1, s2, o0, o1), r, w)
+
+    def scan(out, d0, d1, init, o0, o1, r, w):
+        op("v", lambda: v.tensor_tensor_scan(out, d0, d1, init, o0, o1), r, w)
+
+    def tr(out, in_, r, w):
+        op("v", lambda: v.transpose(out, in_), r, w)
+
+    def ms(out, val, w):
+        op("v", lambda: v.memset(out, val), [], w)
+
+    def act(out, in_, r, w, bias=0.0, scale=1.0):
+        op("a", lambda: a.activation(out, in_, AF.Identity, bias=bias, scale=scale), r, w)
+
+    def strew(out, in_, r, w):
+        op("a", lambda: a.activation(out, in_, AF.Silu), r, w)
+
+    def mm(lst, r, w):
+        op("p", [(lambda x=x: pe.matmul(*x)) for x in lst], r, w)
+
+    def iota(out, pat, base, cm, w, fl=True):
+        if fl:
+            op("g", lambda: g.iota(out, pat, base, cm, allow_small_or_imprecise_dtypes=True), [], w)
+        else:
+            op("g", lambda: g.iota(out, pat, base, cm), [], w)
+
+    def fill(out, n, val, w):
+        iota(out, [[0, n]], val, 0, w)
+
+    def sel(out, in_, pat, cmp, val, base, cm, r, w):
+        op("g", lambda: g.affine_select(out, in_, pat, cmp, val, base, cm), r, w)
+
+    def col(k):
+        return T.COL[:, k:k + 1]
+
+    def cn(k):
+        return ("COL", k, k + 1)
+
+    def mt(k):
+        return T.MT[:, k, :]
+
+    def mn(k):
+        return ("MT", k, k + 1)
+
+    def sm(k):
+        return T.SM[:, k, :]
+
+    def sn(k):
+        return ("SM", k, k + 1)
+
+    def dsel(u):
+        return T.BW[:, 15 - u:143 - u]
+
+    def dself(u):
+        return T.BWF[:, 15 - u:143 - u]
+
+    def mark(k, pat, base, val, src=None):
+        if src is None:
+            sel(mt(k), T.ZB[:, 0:128], pat, OP.not_equal, val, base, 1, ["ZB"], [mn(k)])
+        else:
+            sel(mt(k), mt(src), pat, OP.not_equal, val, base, 1, [mn(src)], [mn(k)])
+
+    XG, WG, DG_ = T.XW[:, 0:2304], T.W1[:, 0:2304], T.DE[:, 0:2304]
+    DGP = T.PB[:, 256:512]
+    REPL = slice(H_, V_)
+    ROW = [[-16, 8], [0, 16]]
+
+    dma("a", "w32", [(T.W32[0:32, :], T.wv[:])], [], ["W32"])
+    dma("s", "nl", [(T.NLI[:], T.nl[:])], [], ["NLI"])
+    dma("a", "s32", [(T.S32[0:32, :], T.sc[:])], [], ["S32"])
+    dma("s", "ovf", [(T.OVI[:], T.ov[:])], [], ["OVI"])
+    dma("s", "va", [(T.VA[:, 0:C_], T.va[:])], [], [("VA", 0, C_)])
+    dma("s", "xv", [(T.XW[:, 0:V_], T.xv[:])], [], [("XW", 0, V_)])
+    dma("s", "o32", [(T.O32[0:32, :], T.ov[:])], [], ["O32"])
+    dma("s", "kc", [(T.KK[:, 0:C_], T.kc[:])], [], [("KK", 0, C_)])
+    dma("s", "rl", [(T.RLI[:, k, :], T.va[k::16, :]) for k in range(16)], [], ["RLI"])
+
+    iota(T.CI[:, 0:1], [[0, 1]], 0, 1, [("CI", 0, 1)], False)
+    iota(T.RV[0:32, :], [[-4, 8], [0, 16]], 0, 1, ["RV"])
+    iota(T.GV[:], [[1, 8], [0, 16]], 0, 0, ["GV"])
+    iota(T.VV[:], [[-1, 128]], 0, 1, ["VV"])
+    iota(T.PV[:], [[16, 8], [-1, 16]], 128, 1, ["PV"], False)
+    iota(T.ZV[:], [[0, 16], [1, 16]], 0, 0, ["ZV"])
+    iota(T.JT[:, 0, :], [[32, 8], [0, 2]], -2048, 0, ["JT"])
+    iota(T.Q16[:], [[16, 16]], 0, 0, ["Q16"])
+    iota(T.CJ[:, 0, :], [[1, 96]], C_, 0, ["CJ"])
+    iota(T.CV[:], [[-256, 96], [-24576, 16]], 256 * C_, 0, ["CV"])
+    fill(T.ZB[:, 0:128], 128, 0, ["ZB"])
+    for k, base, hb in ((M_S00, 0, 0), (M_S11, -16, -1000), (M_S10, 0, -1000), (M_S01, -16, 0)):
+        mark(k, [[-32, 4], [1000, 2], [-1, 16]], base + hb, 1.0)
+    mark(M_B01, ROW, 0, 1.0)
+    mark(M_B01, ROW, -1, 1.0, M_B01)
+    mark(M_B2, ROW, -2, 1.0)
+    iota(T.LW[:, 512:2056], [[-256, 1544]], 256 * C_, 0, ["LW"])
+    fill(T.STL[:], 256, 4096, ["STL"])
+    mark(M_NI, [[-1, 128]], 0, -1.0)
+    fill(T.ONE[:], 256, 1, ["ONE"])
+    fill(T.TIE[0:1, :], NR, 0, ["TIE"])
+    for d in range(1, 8):
+        if rank > (rank ^ d):
+            fill(T.TIE[0:1, 48 * (d - 1):48 * d], 48, 1, ["TIE"])
+
+    ms(T.D0[:], 1.0, ["D0"])
+    act(DG_, T.D0[:], ["D0"], ["DE"], scale=0.0)
+    ts(T.CI[:, 1:2], T.CI[:, 0:1], 15, OP.bitwise_and, ["CI"], [("CI", 1, 2)])
+    ts(T.CI[:, 2:3], T.CI[:, 0:1], 4, OP.arith_shift_right, [("CI", 0, 1)], [("CI", 2, 3)])
+    ts(T.CI[:, 3:4], T.CI[:, 0:1], 31, OP.bitwise_and, [("CI", 0, 1)], [("CI", 3, 4)])
+    for u in range(4):
+        ts(T.REP[0:32, u, :], T.RV[0:32, :], float(u), OP.is_equal, ["RV"], [("REP", u, u + 1)])
+    cp(T.COL[:, 0:3], T.CI[:, 1:4], ["CI"], [("COL", 0, 3)])
+    ms(T.VA[:, C_:1544], 0, [("VA", C_, 1544)])
+    ms(T.S16[:, C_:1544], 0.0, [("S16", C_, 1544)])
+    ms(T.W1[:, V_:2304], 0.0, [("W1", V_, 2304)])
+    ms(T.BW[:], 0.0, ["BW"])
+    ts(col(3), col(0), 96.0, OP.mult, [cn(0)], [cn(3)])
+    ts(col(4), col(0), 4096.0, OP.mult, [cn(0)], [cn(4)], -65536.0, OP.add)
+    ts(T.BB[:], T.GV[:], col(1), OP.is_equal, ["GV", cn(1)], ["BB"])
+    ts(T.IF[:], T.VV[:], 0.0, OP.is_equal, ["VV"], ["IF"])
+    ts(T.BW[:, 15:143:16], T.BB[:, 0::16], 4096.0, OP.mult, ["BB"], ["BW"])
+    cp(T.W32B[0:32, :], T.W32[0:32, :], ["W32"], ["W32B"])
+    banks = ["PA", "PB", "PC", "PD"]
+    for u in range(4):
+        mm([(T[banks[u]][:, :], T.REP[0:32, u, :], T.W32B[0:32, :], True, True)], ["REP", "W32B"], [banks[u]])
+    cp(T.S32B[0:32, :], T.S32[0:32, :], ["S32"], ["S32B"])
+    cp(T.LN[:], T.NLI[:], ["NLI"], ["LN"])
+    cp(T.LNF[:], T.NLI[:], ["NLI"], ["LNF"])
+    for u in range(4):
+        act(T.W1[:, 512 * u:512 * u + 512], T[banks[u]][:, :], [banks[u]], [("W1", 512 * u, 512 * u + 512)], bias=1.0)
+    sb_ = ["PE", "PF", "PG", "PH"]
+    for u in range(4):
+        mm([(T[sb_[u]][:, 0:384], T.REP[0:32, u, :], T.S32B[0:32, :], True, True)], ["REP", "S32B"], [sb_[u]])
+    ts(T.PV[:], T.PV[:], 127, OP.bitwise_and, ["PV"], ["PV"])
+    ts(T.RS0[:], T.ZV[:], 0.0, OP.is_equal, ["ZV"], ["RS0"], BIG, OP.mult)
+    ts(T.RS1[:], T.ZV[:], 1.0, OP.is_equal, ["ZV"], ["RS1"], BIG, OP.mult)
+    for d in range(1, 8):
+        ts(mt(M_P + d - 1), T.PV[:], float(16 * d), OP.is_equal, ["PV"], [mn(M_P + d - 1)])
+
+    def lane_lists(first=False):
+        if not first:
+            act(T.SG[:], T.S16[:].indirect(T.LN[:]), ["S16", "LN"], ["SG"])
+        cp(T.ROWS[:], T.VA[:].indirect(T.LN[:]), ["VA", "LN"], ["ROWS"])
+        ts(T.RK[:], T.VA[:].indirect(T.LN[:]), col(4), OP.add, ["VA", "LN", cn(4)], ["RK"])
+        mm([(T.PA[:, 0:256], T.IF[:], T.RK[:], True, False)], ["IF", "RK"], ["PA"])
+
+    def sentinels():
+        tr(T.ST[:], T.SG[:], ["SG"], ["ST"])
+        for f in range(2):
+            tt(T.SENT[:, f, :], T.ST[:, 0::16], T.JT[:, f, :], OP.add, ["ST", "JT"], [("SENT", f, f + 1)])
+
+    def gath(e, dn, lo, hi):
+        win, wn = (WG, "W1") if dn == "GW" else (XG, "XW")
+        if hi > lo:
+            (cp if e == "v" else act)(T[dn][:, 16 * lo:16 * hi], win.indirect(T.ROWS[:, lo:hi]), [wn, "ROWS"], [(dn, 16 * lo, 16 * hi)])
+
+    def key_mm(lo, hi, last):
+        mm([(T.PA[:, lo:hi], dsel(k), T.GW[:, 16 * lo + k:16 * hi:16], False, last and k == 15) for k in range(16)],
+           ["BW", ("GW", 16 * lo, 16 * hi)], ["PA"])
+
+    def sum_mm(lo, hi, last):
+        mm([(T.PC[:, lo:hi], mt(M_NI), T.GX[:, 16 * lo + k:16 * hi:16], False, last and k == 15) for k in range(16)],
+           [("GX", 16 * lo, 16 * hi)], ["PC"])
+
+    def rnd(dn, lo, mid, hi, last):
+        gath("v", dn, lo, mid)
+        gath("a", dn, mid, hi)
+        (key_mm if dn == "GW" else sum_mm)(lo, hi, last)
+
+    def to_list():
+        scan(T.SC[:], T.M0[:], T.MK[:], 0.0, OP.mult, OP.add, ["M0", "MK"], ["SC"])
+
+    ENDS = T.SC[:, 15::16]
+
+    peers = [T.cores[rank ^ d] for d in range(1, 8)]
+    eng = topo.engines(core, peers[0])
+    far = [p for p in peers if topo.die(p) != topo.die(core)]
+    near = [p for p in peers if topo.die(p) == topo.die(core)]
+    masks = {}
+    pool = eng[0::2] + eng[1::2]
+    per = 2
+    for k, p in enumerate(far + near):
+        masks[p] = sum(1 << e for e in pool[per * k:per * k + per])
+
+    def snd(m, f):
+        return T.SND[:, m, :, 48 * f:48 * f + 48]
+
+    def pack_x(m):
+        act(snd(m, 0), T.XW[:, REPL], ["XW"], [("SND", 3 * m, 3 * m + 1)])
+
+    def pack_w(m):
+        act(snd(m, 1), T.W1[:, REPL], ["W1"], [("SND", 3 * m + 1, 3 * m + 2)])
+
+    def owners_psum():
+        act(T.PE[:, 0:NR], T.DE[:, REPL], ["DE"], ["PE"])
+
+    def send(m):
+        tt(snd(m, 2), T.W1[:, REPL], T.PE[:, 0:NR], OP.min, ["W1", "PE"], [("SND", 3 * m + 2, 3 * m + 3)])
+        if m < 3:
+            cp(snd(m, 1), T.W1[:, REPL], ["W1"], [("SND", 3 * m + 1, 3 * m + 2)])
+        order("g", [("SND", 3 * m, 3 * m + 3)], [])
+        trs = []
+        for d in range(1, 8):
+            p = peers[d - 1]
+            rid, pid, _ = topo.addr(p)
+            trs.append(RemoteDMATransfer(dst_ids=[DstId(rid=rid, pnc=pid)], dma_engine_mask=masks[p],
+                                         remote_sem=T.sem["ar%d" % m], src=T.SND[:, m, d - 1, :], dst=T.LND[:, m, d - 1, :]))
+        g.remote_dma_fused(trs, local_sem=T.sem.ls)
+        count["ls"] = count.get("ls", 0) + 7 * per
+        sr = ("SND", 3 * m, 3 * m + 3)
+        mm([(T.PE[:, 0:NR], mt(M_NI), snd(m, 2), True, False),
+            (T.PE[:, 0:NR], T.ONE[0:1, 0:128], T.TIE[0:1, :], False, False)], [sr, mn(M_NI), "ONE", "TIE"], ["PE"])
+        mm([(T.PF[:, 0:NR], mt(M_NI), snd(m, 1), True, False)], [sr], ["PF"])
+
+    def mine_x(m):
+        mm([(T.PG[:, 0:NR], mt(M_NI), snd(m, 0), True, False)], [("SND", 3 * m, 3 * m + 3)], ["PG"])
+
+    def arrive(m, xfirst):
+        need("p", ("ar%d" % m, 7 * per))
+        for f, bank in ((2, "PE"), (0, "PG"), (1, "PF")) if xfirst else ((2, "PE"), (1, "PF"), (0, "PG")):
+            mm([(T[bank][:, 48 * d:48 * d + 48], mt(M_P + d), T.LND[:, m, d, 48 * f:48 * f + 48], False, d == 6)
+                for d in range(7)], [("MT", M_P, M_P + 7)], [bank])
+        ts(T.LOSE[:], T.PE[:, 0:NR], 0.5, OP.is_gt, ["PE"], ["LOSE"])
+
+    def upd_w():
+        tt(T.PF[:, 0:NR], T.PF[:, 0:NR], T.LOSE[:], OP.mult, ["PF", "LOSE"], ["PF"])
+        tt(T.W1[:, REPL], T.W1[:, REPL], T.PF[:, 0:NR], OP.add, ["PF", ("W1", H_, V_)], [("W1", H_, V_)])
+
+    def upd_z():
+        tt(T.PG[:, 0:NR], T.PG[:, 0:NR], T.LOSE[:], OP.mult, ["PG", "LOSE"], ["PG"])
+
+    def upd_ch():
+        tt(T.CH[:, REPL], T.PG[:, 0:NR], T.CH[:, REPL], OP.not_equal, ["PG", ("CH", H_, V_)], [("CH", H_, V_)])
+
+    def upd_xd():
+        ts(T.PE[:, 0:NR], T.PE[:, 0:NR], 0.5, OP.is_lt, ["PE"], ["PE"])
+        tt(T.XW[:, REPL], T.XW[:, REPL], T.PG[:, 0:NR], OP.add, ["PG", ("XW", H_, V_)], [("XW", H_, V_)])
+        tt(T.DE[:, REPL], T.DE[:, REPL], T.PE[:, 0:NR], OP.mult, ["PE", ("DE", H_, V_)], [("DE", H_, V_)])
+
+    def halve():
+        act(T.CH[:, REPL], T.CH[:, REPL], [("CH", H_, V_)], [("CH", H_, V_)], scale=0.5)
+
+    def consts_steal():
+        ms(T.DG[:, 16:32], 0.0, [("DG", 16, 32)])
+        ts(T.DG[:, 0:16], T.ZV[:, 0:16], col(0), OP.is_equal, ["ZV", cn(0)], [("DG", 0, 16)], float(2 ** 20), OP.mult)
+        ts(T.JT[:, 0, :], T.JT[:, 0, :], col(2), OP.add, ["JT", cn(2)], ["JT"])
+        ts(T.DG[:, 0:16], T.DG[:, 0:16], 1.0, OP.max, ["DG"], ["DG"])
+        ts(T.JT[:, 1, :], T.JT[:, 0, :], 4096.0, OP.add, ["JT"], ["JT"])
+        ms(T.TB[:], 0.0, ["TB"])
+        ts(col(9), col(0), 8.0, OP.mult, [cn(0)], [cn(9)], 24.0, OP.add)
+        ts(T.JK[:, 0, :], T.Q16[:], col(0), OP.add, ["Q16", cn(0)], [("JK", 0, 1)], 2048.0, OP.add)
+        ts(T.JK[:, 1, :], T.Q16[:], col(0), OP.add, ["Q16", cn(0)], [("JK", 1, 2)], 1600.0, OP.add)
+        ts(T.EL[:, 0:1], col(9), col(0), OP.mult, [cn(9), cn(0)], ["EL"], 15.0, OP.add)
+        ms(T.XW[:, V_:2304], 0.0, [("XW", V_, 2304)])
+
+    def owners_list():
+        ts(T.CJ[:, 0, :], T.CJ[:, 0, :], col(3), OP.add, ["CJ", cn(3)], ["CJ"])
+        cp(T.RR[:, 0, :], T.OVI[:], ["OVI"], ["RR"])
+        ts(T.CJ[:, 1, :], T.CJ[:, 0, :], 768.0, OP.add, ["CJ"], ["CJ"])
+        ts(T.NF[:], T.RR[:, 0, :], 2047.5, OP.is_gt, ["RR"], ["NF"])
+        tt(T.NF[:], T.NF[:], T.CJ[:, 1, :], OP.mult, ["NF", "CJ"], ["NF"])
+        tt(T.NF[:], T.NF[:], T.RR[:, 0, :], OP.max, ["NF", "RR"], ["NF"])
+        cp(T.PS[:], T.NF[:], ["NF"], ["PS"])
+
+    def consts_out():
+        ob = ["PE", "PF", "PA", "PH"]
+        for u in range(4):
+            mm([(T[ob[u]][:, 0:384], T.REPF[0:32, u, :], T.O32F[0:32, :], True, True)], ["REPF", "O32F"], [ob[u]])
+            if u < 3:
+                act(T.OO[:, 384 * u:384 * u + 384], T[ob[u]][:, 0:384], [ob[u]], [("OO", 384 * u, 384 * u + 384)])
+
+    def consts_plan_g():
+        mark(M_I, [[-1, 128]], 0, 1.0)
+        mark(M_IB, [[-1, 128]], 0, BIG)
+        mark(M_B15, ROW, -15, 2.0 ** -16)
+        mark(M_RS, ROW, -7, -1.0)
+        sel(mt(M_T0), T.BB[:], [[1, 128]], OP.is_gt, 0.0, 0, -1, ["BB"], [mn(M_T0)])
+        mark(M_T2, ROW, -15, 1.0, M_T0)
+        sel(mt(M_T2), mt(M_T2), [[0, 8], [1, 16]], OP.not_equal, 0.0, -15, 0, [mn(M_T2)], [mn(M_T2)])
+        fill(T.KK[:, C_:1552], 16, 0, [("KK", C_, 1552)])
+        fill(T.FK[:], 96, 0, ["FK"])
+        fill(T.SD[:, 0:16], 16, 0, [("SD", 0, 16)])
+        fill(T.LW[:, 0:256], 256, 0, ["LW"])
+        fill(T.LX[:, 0:256], 256, 0, ["LX"])
+
+    def consts_plan_v():
+        ts(col(12), col(0), 7.0, OP.is_lt, [cn(0)], [cn(12)])
+        ts(mt(M_A), T.VV[:], 0.0, OP.is_lt, ["VV"], [mn(M_A)])
+        for k, s in ((M_LA, 8.0), (M_LB, 7.0)):
+            ts(T.TM[:], T.ZV[:, 0:128], s, OP.is_lt, ["ZV", cn(12)], ["TM"], col(12), OP.subtract)
+            tt(T.TM[:], T.TM[:], mt(M_A), OP.add, ["TM", mn(M_A)], ["TM"])
+            tt(mt(k), T.TM[:], T.BB[:], OP.mult, ["TM", "BB"], [mn(k)])
+
+    CD = ["CD0", "CD1"]
+    lane_lists(True)
+    for st in range(3):
+        cd, cdn = CD[st % 2], CD[(st + 1) % 2]
+        if st == 0:
+            rnd("GW", 0, 60, 96, False)
+            for u in range(4):
+                act(T.S16[:, 384 * u:384 * u + 384], T[sb_[u]][:, 0:384], [sb_[u]], [("S16", 384 * u, 384 * u + 384)], scale=65536.0)
+            act(T.SG[:], T.S16[:].indirect(T.LN[:]), ["S16", "LN"], ["SG"])
+            consts_steal()
+            owners_list()
+            rnd("GW", 96, 156, 192, False)
+            for q in range(16):
+                at = 8 * q * (q + 1) + 16 * q
+                act(T.D0[:, at:at + 17], T.DG[:, 0:17], ["DG"], [("D0", at, at + 17)])
+            rnd("GW", 192, 230, 256, True)
+            strew(T.DE[:].indirect(T.PS[:]), T.CV[:], ["PS", "CV"], ["DE"])
+            act(T[cd][:], T.LW[:, 512:2056].indirect(T.LN[:]), ["LW", "LN"], [cd])
+            act(T.DE[:, V_:2304], T[cd][:], [cd], [("DE", V_, 2304)])
+            sentinels()
+            ts(T.DGM[:], T.ZV[:], col(0), OP.is_equal, ["ZV", cn(0)], ["DGM"])
+        else:
+            rnd("GW", 0, 48, 96, False)
+            rnd("GW", 96, 140, 192, False)
+            rnd("GW", 192, 220, 256, True)
+            upd_z()
+            upd_xd()
+            act(T.DE[:, V_:2304], T[cd][:], [cd], [("DE", V_, 2304)])
+        tr(T.PH[:, 0:256], T.PA[:, 0:256], ["PA"], ["PH"])
+        scan(T.PQ[:, 0, :], T.RS0[:], T.PH[:, 0:256], BIG, OP.add, OP.min, ["RS0", "PH"], [("PQ", 0, 1)])
+        tt(T.ZZ[:, 1:256], T.PH[:, 1:256], T.PQ[:, 0, 0:255], OP.max, ["PH", ("PQ", 0, 1)], ["ZZ"])
+        scan(T.PQ[:, 1, 1:256], T.RS1[:, 1:256], T.ZZ[:, 1:256], BIG, OP.add, OP.min, ["RS1", "ZZ"], [("PQ", 1, 2)])
+        tt(T.R1[:], T.PQ[:, :, 15::16], T.SENT[:], OP.min, ["PQ", "SENT"], ["R1"])
+        ts(T.R2[:, :, 0:1], T.R1[:, 0, :], 4032, OP.bitwise_and, ["R1"], [("R2", 0, 1)])
+        ts(T.R2[:, :, 1:2], T.R1[:, 0, :], 63, OP.bitwise_and, ["R1"], [("R2", 1, 2)])
+        ts(T.R2[:, :, 2:3], T.R1[:, 1, :], 16, OP.arith_shift_right, ["R1"], [("R2", 2, 3)])
+        cp(T.TB[:, :, 0:3], T.R2[:], ["R2"], ["TB"])
+        tr(T.TBT[:], T.TB[:], ["TB"], ["TBT"])
+        lst = []
+        for y1 in range(2):
+            for h in range(2):
+                k = {(0, 0): M_S00, (1, 1): M_S11, (1, 0): M_S10, (0, 1): M_S01}[(h, y1)]
+                for s in range(2):
+                    lst.append((T.PB[:, y1:16:2], mt(k), T.TB[:, h::2, s:s + 1], h == 0 and s == 0, h == 1 and s == 1))
+        mm(lst, ["TB", ("MT", M_S00, M_S01 + 1)], ["PB"])
+        mm([(T.PC[:, 0:256], mt(M_B01), T.TBT[:], True, True)], ["TBT", mn(M_B01)], ["PC"])
+        mm([(T.PD[:, 0:256], mt(M_B2), T.TBT[:], True, True)], ["TBT", mn(M_B2)], ["PD"])
+        if st == 0:
+            ts(T.M0[:], T.ZV[:], 0.5, OP.is_gt, ["ZV"], ["M0"])
+            cp(T.O32F[0:32, :], T.O32[0:32, :], ["O32"], ["O32F"])
+        else:
+            upd_ch()
+        cp(T.O16[:], T.PC[:, 0:256], ["PC"], ["O16"])
+        act(T.NW[:], T.PD[:, 0:256], ["PD"], ["NW"], bias=1.0)
+        if st > 0:
+            of = "DF" if st == 1 else "OF"
+            act(T[of][:], T.PC[:, 0:256], ["PC"], [of])
+            halve()
+        if st == 1:
+            consts_out()
+        for q in range(16):
+            at, n = 8 * q * (q + 1), 16 * (q + 1)
+            ts(T.GX[:, at:at + n], T.O16[:, 0:n], T.PB[:, q:q + 1], OP.is_equal, ["O16", "PB"], [("GX", at, at + n)], 2.0 ** -8, OP.mult)
+        scan(T.CNT[:], T.D0[:, 0:2176], T.GX[:, 0:2176], 0.0, OP.mult, OP.add, ["D0", "GX"], ["CNT"])
+        tt(sm(0), T.CNT[:].indirect(T.EL[:, 0:1]), T.JK[:, 0, :], OP.min, ["CNT", "EL", "JK"], [sn(0)])
+        tt(sm(1), sm(0), T.PB[:, 0:16], OP.max, [sn(0), "PB"], [sn(1)])
+        cp(T.TG[:], sm(1), [sn(1)], ["TG"])
+        act(T[cdn][:], DG_.indirect(T.TG[:]), ["DE", "TG"], [cdn])
+        strew(DG_.indirect(T.TG[:]), T[cd][:], ["TG", cd], ["DE"])
+        cp(XG.indirect(T.TG[:]), T.STL[:], ["TG", "STL"], ["XW"])
+        cp(WG.indirect(T.TG[:]), T.NW[:], ["TG", "NW"], ["W1"])
+        owners_psum()
+        pack_x(st)
+        send(st)
+        mine_x(st)
+        if st == 0:
+            fill(T.ONF[:], 256, 1, ["ONF"])
+            fill(T.OO[:, C_:1856], 320, 2048, [("OO", C_, 1856)])
+            fill(T.CH[:, H_:V_], NR, 0, [("CH", H_, V_)])
+            fill(T.FLR[:], 1856, 0, ["FLR"])
+            act(T.OF0[:], T.PC[:, 0:256], ["PC"], ["OF0"])
+            act(T.REPF[0:32], T.REP[0:32], ["REP"], ["REPF"])
+            act(T.BWF[:], T.BW[:], ["BW"], ["BWF"], scale=2.0 ** -16)
+            ts(DGP, T.ZV[:], col(0), OP.is_equal, ["ZV", cn(0)], ["PB"])
+        if st == 1:
+            act(T.OO[:, 1152:C_], T.PH[:, 0:384], ["PH"], [("OO", 1152, C_)])
+            fill(T.CH[:, 0:H_], H_, 0, [("CH", 0, H_)])
+            fill(T.CH[:, V_:2304], 256, 0, [("CH", V_, 2304)])
+            consts_plan_g()
+        ts(sm(2), sm(1), 2047.5, OP.is_gt, [sn(1)], [sn(2)])
+        if st < 2:
+            tt(T.MK[:], T[cdn][:], DGP, OP.mult, [cdn, "PB"], ["MK"])
+            ts(sm(4), T.PB[:, 0:16], 2047.5, OP.is_lt, ["PB"], [sn(4)], BIG, OP.mult)
+            to_list()
+        tt(sm(2), sm(2), T.JK[:, 1, :], OP.mult, [sn(2), "JK"], [sn(2)])
+        if st < 2:
+            tt(sm(5), ENDS, sm(4), OP.min, ["SC", sn(4)], [sn(5)])
+        tt(sm(3), sm(2), T.LNF[:], OP.max, [sn(2), "LNF"], [sn(3)])
+        if st < 2:
+            ts(T.LN[:], sm(5), -1.0 / 256, OP.mult, [sn(5)], ["LN"], C_ + 0.25, OP.add)
+        tcs = [(T.TC0[:, 0, :], ("TC0", 0, 1), "OF0"), (T.TC0[:, 1, :], ("TC0", 1, 2), "DF"), (T.TC[:], "TC", "OF")]
+        cp(tcs[st][0], sm(3), [sn(3)], [tcs[st][1]])
+        if st < 2:
+            cp(T.LNF[:], T.LN[:], ["LN"], ["LNF"])
+            lane_lists()
+            sentinels()
+        if st == 0:
+            cp(T.RL[:], T.RLI[:], ["RLI"], ["RL"])
+        for ls, ln_, of in ([], tcs[0:1], tcs[1:3])[st]:
+            cp(T.OO[:].indirect(ls), T[of][:], [ln_, of], ["OO"])
+            strew(T.FLR[:].indirect(ls), T.ONF[:], [ln_, "ONF"], ["FLR"])
+        if st == 2:
+            ms(T.DE[:, V_:V_ + 8], -1024.0, [("DE", V_, V_ + 8)])
+            consts_plan_v()
+        arrive(st, st == 2)
+        if st < 2:
+            upd_w()
+
+    def lift(nv, extra, late=None):
+        win = T.CH[:]
+        mm([(T.PH[:, 0:96], mt(M_I), T.FK[:], True, False)] +
+           [(T.PH[:, 0:96], dself(u), T.FLR[:, 96 * u:96 * u + 96], False, False) for u in range(16)],
+           [mn(M_I), "FK", "BWF", "FLR"], ["PH"])
+        full, half = nv // 2, nv % 2
+        ajobs = [(k, 0, 96) for k in range(full + half, 16)]
+        ajobs = ([(full, 48, 96)] if half else []) + ajobs[:-1] + [(15, 0, 48), (15, 48, 96)]
+        vjobs = ([(0, 0, 96)] + ([(full, 0, 48)] if half else []) + [(k, 0, 96) for k in range(1, full - 1)]
+                 + [(full - 1, 48, 96), (full - 1, 0, 48)])
+        na, nj = len(ajobs), len(vjobs)
+
+        def red(src, name, lo, hi, last):
+            mm([(T.PH[:, lo:hi], dsel(u), src(u), False, last and u == 15) for u in range(16)], ["BW", name], ["PH"])
+
+        def ajob(n):
+            k, lo, hi = ajobs[n]
+            s = n % 4
+            nm = ("GR", 96 * s + lo, 96 * s + hi)
+            act(T.GR[:, s, 16 * lo:16 * hi], win.indirect(T.RL[:, k, lo:hi]), ["CH", "RL"], [nm])
+            if n < na - 2:
+                red(lambda u: T.GR[:, s, 16 * lo + u:16 * hi:16], nm, lo, hi, False)
+
+        def vjob(n):
+            k, lo, hi = vjobs[n]
+            dst, nm = T.ACC[:, 16 * lo:16 * hi], ("ACC", 16 * lo, 16 * hi)
+            if n == 0:
+                cp(dst, win.indirect(T.RL[:, k, lo:hi]), ["CH", "RL"], [nm])
+            elif n < nj - 2:
+                tt(dst, win.indirect(T.RL[:, k, lo:hi]), dst, OP.max, ["CH", "RL", nm], [nm])
+            else:
+                s = (na - nj + n) % 4
+                tt(T.GR[:, s, 16 * lo:16 * hi], win.indirect(T.RL[:, k, lo:hi]), dst, OP.max, ["CH", "RL", nm],
+                   [("GR", 96 * s + lo, 96 * s + hi)])
+
+        extra()
+        for n in range(na - 2):
+            ajob(n)
+        for n in range(nj - 2):
+            vjob(n)
+            if n == 2 and late:
+                late()
+        for e in (2, 1):
+            s = (na - e) % 4
+            ajob(na - e)
+            vjob(nj - e)
+            red(lambda u: T.GR[:, s, u:1536:16], ("GR", 96 * s, 96 * s + 96), 0, 96, e == 1)
+
+    def after_steals():
+        mm([(T.PD[:, 0:96], dself(u), T.OO[:, 96 * u:96 * u + 96], u == 0, u == 15) for u in range(16)], ["BWF", "OO"], ["PD"])
+        upd_w()
+        upd_xd()
+        cp(T.VAF[:], T.VA[:], ["VA"], ["VAF"])
+
+    def last_outputs():
+        cp(T.OFF[:], T.PD[:, 0:96], ["PD"], ["OFF"])
+        cp(T.OFL[:], T.OFF[:], ["OFF"], ["OFL"])
+
+    def after_plan():
+        upd_w()
+        upd_xd()
+
+    def outputs():
+        upd_w()
+        upd_xd()
+        mm([(T.PD[:, 0:128], dsel(u), T.W1[:, 128 * u:128 * u + 128], u == 0, u == 15) for u in range(16)], ["BW", "W1"], ["PD"])
+        tt(T.GX[:, 0:C_], DG_.indirect(T.OFL[:]), T.CV[:], OP.subtract, ["DE", "OFL", "CV"], ["GX"])
+        mm([(T.PC[:, 0:96], dsel(u), T.GX[:, u:C_:16], u == 0, u == 15) for u in range(16)], ["BW", "GX"], ["PC"])
+        ts(T.GW[:, H_:V_], T.XW[:, REPL], 256.0, OP.min, ["XW"], [("GW", H_, V_)])
+        dma("s", "y", [(T.y[:], T.GW[:, 0:V_])], ["GW"], [])
+
+    def outputs_late():
+        ts(T.YWB[:], T.PD[:, 0:128], 2.0 ** -16, OP.mult, ["PD"], ["YWB"], -1.0, OP.add)
+        dma("s", "yw", [(T.yw[:], T.YWB[:])], ["YWB"], [])
+        ts(T.YOB[:, 0, :], T.PC[:, 0:96], 2.0 ** -16, OP.mult, ["PC"], ["YOB"])
+        tt(T.YOB[:, 0, :], T.YOB[:, 0, :], T.YOB[:, 0, :], OP.mult, ["YOB"], ["YOB"])
+        ts(T.YOB[:, 0, :], T.YOB[:, 0, :], 16384.0, OP.is_gt, ["YOB"], ["YOB"], 2048.0, OP.mult)
+        tt(T.YOB[:, 1, :], T.YOB[:, 0, :], T.OFF[:], OP.max, ["YOB", "OFF"], ["YOB"])
+        dma("s", "yo", [(T.yo[:], T.YOB[:, 1, :])], ["YOB"], [])
+
+    upd_z()
+    upd_ch()
+    lift(14, after_steals, last_outputs)
+
+    for t in range(3):
+        m = 3 + t
+        fill(T.FLR[:], 1856, 0, ["FLR"])
+        fill(T.CH[:], 2304, 0, ["CH"])
+        ts(T.FL[:], T.PH[:, 0:96], 0.0, OP.is_gt, ["PH"], ["FL"])
+        scan(T.INC[:], T.ONE[:, 0:96], T.FL[:], 0.0, OP.mult, OP.add, ["ONE", "FL"], ["INC"])
+        tot, mid = T.INC[:, 95:96], T.INC[:, 47:48]
+        if t == 1:
+            mm([(T.PC[:, 0:1], mt(M_LA), tot, True, False), (T.PC[:, 0:1], mt(M_RS), mid, False, True),
+                (T.PC[:, 1:2], mt(M_LB), tot, True, False), (T.PC[:, 1:2], mt(M_RS), mid, False, True)], ["INC", "MT"], ["PC"])
+        else:
+            mm([(T.PC[:, 0:1], mt(M_T0 if t == 0 else M_T2), tot, True, True)], ["INC", "MT"], ["PC"])
+        ts(T.NF[:], T.FL[:], -4096.0, OP.mult, ["FL"], ["NF"], 4095.0, OP.add)
+        tt(T.NF[:], T.NF[:], T.INC[:], OP.add, ["NF", "INC"], ["NF"])
+        if t == 1:
+            for hf in range(2):
+                ts(T.RR[:, 0, 48 * hf:48 * hf + 48], T.NF[:, 48 * hf:48 * hf + 48], T.PC[:, hf:hf + 1], OP.add,
+                   ["NF", "PC"], [("RR", 48 * hf, 48 * hf + 48)])
+        else:
+            ts(T.RR[:, 0, :], T.NF[:], T.PC[:, 0:1], OP.add, ["NF", "PC"], [("RR", 0, 96)])
+        tt(T.RR[:, 1, :], T.RR[:, 0, :], T.CJ[:, 0, :], OP.min, [("RR", 0, 96), "CJ"], [("RR", 96, 192)])
+        cp(T.PS[:], T.RR[:, 1, :], [("RR", 96, 192)], ["PS"])
+        strew(T.LX[:].indirect(T.PS[:, 46:96]), T.CV[:, 736:C_], ["PS", "CV"], ["LX"])
+        cp(T.LW[:].indirect(T.PS[:, 0:46]), T.CV[:, 0:736], ["PS", "CV"], ["LW"])
+        tt(T.MK[:], T.LW[:, 0:256], DGP, OP.mult, ["LW", "PB"], ["MK"])
+        tt(T.MX[:], T.LX[:, 0:256], DGP, OP.mult, ["LX", "PB"], ["MX"])
+        scan(T.SD[:, 16:272], T.MK[:], T.MX[:], 0.0, OP.add, OP.add, ["MK", "MX"], [("SD", 16, 272)])
+        tt(sm(0), T.SD[:, 31::16], T.SD[:, 15:256:16], OP.subtract, ["SD"], [sn(0)])
+        ts(T.LN[:], sm(0), -1.0 / 256, OP.mult, [sn(0)], ["LN"], C_ + 0.25, OP.add)
+        if t < 2:
+            fill(T.LW[:, 0:256], 256, 0, ["LW"])
+            fill(T.LX[:, 0:256], 256, 0, ["LX"])
+        cp(T.ROWS[:], T.VA[:].indirect(T.LN[:]), ["VA", "LN"], ["ROWS"])
+        act(T.RK[:], T.VAF[:].indirect(T.LN[:]), ["VAF", "LN"], ["RK"])
+        act(T.OF[:], T.OO[:].indirect(T.LN[:]), ["OO", "LN"], ["OF"])
+        tt(T.MK[:], T.OO[:].indirect(T.LN[:]), T.DGM[:], OP.mult, ["OO", "LN", "DGM"], ["MK"])
+        gath("a", "GW", 32, 96)
+        tt(T.OWN[:], T.RK[:], T.OF[:], OP.is_equal, ["RK", "OF"], ["OWN"])
+        to_list()
+        mm([(T.PA[:, 0:256], mt(M_IB), T.OWN[:], True, False)], ["OWN", "MT"], ["PA"])
+        cp(T.OL[:], ENDS, ["SC"], ["OL"])
+        cp(sm(1), ENDS, ["SC"], [sn(1)])
+        gath("v", "GW", 0, 32)
+        key_mm(0, 96, False)
+        rnd("GW", 96, 152, 192, False)
+        rnd("GW", 192, 224, 256, True)
+        act(T.XO[:], XG.indirect(T.OL[:]), ["XW", "OL"], ["XO"])
+        act(T.KG[:], T.KK[:].indirect(T.LN[:]), ["KK", "LN"], ["KG"])
+        mm([(T.PC[:, 0:256], mt(M_I), T.XO[:], True, False), (T.PC[:, 0:256], mt(M_I), T.KG[:], False, False)],
+           ["XO", "KG", "MT"], ["PC"])
+        rnd("GX", 0, 48, 96, False)
+        tr(T.TT[:], T.PA[:, 0:256], ["PA"], ["TT"])
+        scan(T.P2[:], T.RS0[:], T.TT[:], BIG, OP.add, OP.min, ["RS0", "TT"], ["P2"])
+        tr(T.P2T[:], T.P2[:], ["P2"], ["P2T"])
+        mm([(T.PD[:, 0:256], mt(M_B15), T.P2T[:], True, True)], ["P2T", "MT"], ["PD"])
+        tt(T.MK[:], DG_.indirect(T.OL[:]), T.DGM[:], OP.mult, ["DE", "OL", "DGM"], ["MK"])
+        act(T.SG[:], T.S16[:].indirect(T.LN[:]), ["S16", "LN"], ["SG"], bias=1.0, scale=2.0 ** -16)
+        rnd("GX", 96, 140, 192, False)
+        rnd("GX", 192, 224, 256, True)
+        owners_psum()
+        to_list()
+        tt(T.NW[:], T.PD[:, 0:256], T.SG[:], OP.min, ["PD", "SG"], ["NW"])
+        tt(sm(2), ENDS, sm(0), OP.subtract, ["SC", sn(0)], [sn(2)])
+        tt(sm(2), sm(2), sm(2), OP.mult, [sn(2)], [sn(2)])
+        ts(sm(2), sm(2), 16384.0, OP.is_gt, [sn(2)], [sn(2)])
+        tt(sm(2), sm(2), T.JK[:, 0, :], OP.mult, [sn(2), "JK"], [sn(2)])
+        tt(sm(2), sm(2), sm(1), OP.max, [sn(2), sn(1)], [sn(2)])
+        tt(T.MK[:], T.PC[:, 0:256], T.DGM[:], OP.mult, ["PC", "DGM"], ["MK"])
+        to_list()
+        ts(T.NX[:, 0, :], T.PC[:, 0:256], 65536.0, OP.add, ["PC"], [("NX", 0, 1)])
+        ts(sm(3), ENDS, WAITS, OP.is_lt, ["SC"], [sn(3)])
+        ts(T.NX[:, 1, :], T.NX[:, 0, :], 255, OP.bitwise_and, [("NX", 0, 1)], [("NX", 1, 2)])
+        tt(sm(3), sm(3), T.JK[:, 0, :], OP.mult, [sn(3), "JK"], [sn(3)])
+        tt(sm(3), sm(3), sm(2), OP.max, [sn(3), sn(2)], [sn(3)])
+        cp(T.TG[:], sm(3), [sn(3)], ["TG"])
+        cp(XG.indirect(T.TG[:]), T.NX[:, 1, :], ["TG", ("NX", 1, 2)], ["XW"])
+        cp(WG.indirect(T.TG[:]), T.NW[:], ["TG", "NW"], ["W1"])
+        pack_x(m)
+        pack_w(m)
+        send(m)
+        mine_x(m)
+        tt(T.DF[:], T.NX[:, 1, :], T.XO[:], OP.not_equal, [("NX", 1, 2), "XO"], ["DF"])
+        strew(T.CH[:].indirect(T.TG[:]), T.DF[:], ["TG", "DF"], ["CH"])
+        cp(sm(5), T.LN[:], ["LN"], [sn(5)])
+        tt(sm(4), sm(2), sm(3), OP.is_equal, [sn(2), sn(3)], [sn(4)])
+        ts(T.NF[:], T.RR[:, 1, :], 255.5, OP.is_gt, [("RR", 96, 192)], ["NF"])
+        tt(sm(4), sm(4), T.JK[:, 1, :], OP.mult, [sn(4), "JK"], [sn(4)])
+        tt(T.FK[:], T.NF[:], T.FL[:], OP.mult, ["NF", "FL"], ["FK"])
+        tt(sm(4), sm(4), sm(5), OP.max, [sn(4), sn(5)], [sn(4)])
+        cp(T.TC[:], sm(4), [sn(4)], ["TC"])
+        strew(T.FLR[:].indirect(T.TC[:]), T.ONF[:], ["TC", "ONF"], ["FLR"])
+        if t == 2:
+            ts(T.GW[:, 0:H_], T.XW[:, 0:H_], 256.0, OP.min, ["XW"], [("GW", 0, H_)])
+        arrive(m, True)
+        upd_z()
+        upd_ch()
+        if t < 2:
+            lift(15, after_plan)
+        else:
+            lift(14, outputs, outputs_late)
+    ts(T.YFB[:], T.PH[:, 0:96], 0.0, OP.is_gt, ["PH"], ["YFB"])
+    dma("s", "yf", [(T.yf[:], T.YFB[:])], ["YFB"], [])
+    for s in count:
+        need("g", (s, count[s]))

@@ -2,6 +2,8 @@ from concourse.bass import DstId, RemoteDMATransfer
 from concourse.mybir import AluOpType as OP, ActivationFunctionType as AF
 
 V_, C_, L_, H_, NR = 2048, 1536, 256, 1712, 336
+WV, WC = 2320, 1808
+DV, DC = 2064, 1552
 BIG = float(2 ** 25)
 F, B, I, U = "float32", "bfloat16", "int32", "uint16"
 
@@ -11,39 +13,39 @@ def sb(shape, d):
 
 
 SCRATCH = {
-    "VA": sb([1544], I), "VAF": sb([1544], F), "RLI": sb([16, 96], I), "RL": sb([16, 96], U),
-    "XW": sb([2304], B), "W1": sb([2304], B), "DE": sb([3840], F), "S16": sb([1544], F),
-    "OO": sb([1856], F), "FLR": sb([1856], F), "KK": sb([1552], B), "CH": sb([2304], F),
-    "LW": sb([3072], F), "LX": sb([3072], F), "CV": sb([1536], F),
-    "NLI": sb([16], I), "OVI": sb([96], I), "W32": sb([512], I), "S32": sb([384], I), "O32": sb([384], I),
-    "W32B": sb([512], B), "S32B": sb([384], B), "O32F": sb([384], F),
-    "CI": sb([8], I), "COL": sb([24], F), "GV": sb([128], F), "VV": sb([128], F), "PV": sb([128], I),
-    "RV": sb([128], F), "ZV": sb([256], F), "Q16": sb([16], F), "JT": sb([2, 16], F), "CJ": sb([2, 96], F),
-    "JK": sb([2, 16], F), "BB": sb([128], B), "BW": sb([144], B), "BWF": sb([144], F), "IF": sb([128], F),
-    "MT": sb([24, 128], B), "REP": sb([4, 128], B), "REPF": sb([4, 128], F), "TM": sb([128], F),
-    "DGM": sb([256], B), "RS0": sb([256], B), "RS1": sb([256], B), "M0": sb([256], B), "ONE": sb([256], B),
-    "STL": sb([256], B), "D0": sb([2304], B), "DG": sb([32], B), "EL": sb([2], U), "TIE": sb([336], B),
-    "ZB": sb([256], B), "ONF": sb([256], F),
-    "LN": sb([16], U), "LNF": sb([16], F), "ROWS": sb([256], U), "RK": sb([256], F), "SG": sb([256], F),
-    "GW": sb([4096], B), "GX": sb([4096], B), "ST": sb([256], F), "SENT": sb([2, 16], F), "TT": sb([256], F),
-    "PQ": sb([2, 256], F), "ZZ": sb([256], F), "R1": sb([2, 16], I), "R2": sb([16, 3], I), "TB": sb([16, 16], B),
-    "TBT": sb([256], B), "O16": sb([256], U), "OF": sb([256], F), "NW": sb([256], B), "OF0": sb([256], F), "TC0": sb([2, 16], U),
-    "CNT": sb([2176], B), "SM": sb([12, 16], F), "TG": sb([16], U), "TC": sb([16], U), "OL": sb([16], U),
-    "CD0": sb([256], F), "CD1": sb([256], F), "MK": sb([256], F), "MX": sb([256], F), "SC": sb([256], F), "SD": sb([272], F),
-    "SND": sb([6, 7, 144], B), "LND": sb([6, 7, 144], B), "LOSE": sb([336], B),
-    "GR": sb([4, 1536], B), "ACC": sb([1536], B),
-    "FL": sb([96], B), "FK": sb([96], B), "INC": sb([96], B), "NF": sb([96], F), "RR": sb([2, 96], F), "PS": sb([96], U),
-    "OWN": sb([256], B), "P2": sb([256], B), "P2T": sb([256], B), "XO": sb([256], B), "KG": sb([256], B),
+    "VA": sb([1544], I), "VHI": sb([4, 192], I), "VH": sb([4, 192], U), "VU": sb([768], U), "VB": sb([1544], I), "RS4": sb([1024], B), "XW": sb([WV], B), "ST": sb([WV + C_], B),
+    "W0": sb([V_], B), "CS": sb([WC], B), "FLR": sb([WC], B), "KK": sb([1552], B), "CH": sb([WV], F),
+    "LW": sb([4624], F), "LX": sb([4624], F), "CV": sb([C_], F), "CV2": sb([C_], B),
+    "NLI": sb([16], I), "OVI": sb([96], I), "W32": sb([512], I), "S32": sb([384], I), "S32B": sb([384], B),
+    "CI": sb([8], I), "COL": sb([40], F), "EYE": sb([16], F), "GV": sb([128], F), "VV": sb([128], F), "ZV": sb([256], B),
+    "Q16": sb([16], F), "JT": sb([2, 16], F), "CJ": sb([5, 96], F), "JK": sb([2, 16], F), "BB": sb([128], B),
+    "BW": sb([6, 144], B), "MT": sb([16, 8, 16], B), "CF": sb([WC], F), "KC": sb([512], B), "KM": sb([7, 8, 16], B), "RU": sb([4, 8, 16], B),
+    "BD": sb([6, 10, 16], B), "PW": sb([4, 15, 16], B), "TM": sb([128], F), "DGM": sb([256], B), "RS0": sb([256], B),
+    "RS1": sb([256], B), "M0": sb([256], B), "ONE": sb([272], B), "D0": sb([2192], B), "DG": sb([32], B), "EL": sb([2], U),
+    "TIE": sb([NR], B),
+    "LN": sb([16], U), "CO": sb([2, 16], F), "TP": sb([32], F), "TQ": sb([32], F), "ROWS": sb([256], U), "CSG": sb([256], B),
+    "GW": sb([4096], B), "GX": sb([4096], B), "SENT": sb([2, 16], F), "TT": sb([256], F),
+    "PQ": sb([2, 272], F), "ZZ": sb([256], F), "R1": sb([2, 16], I), "R2": sb([16, 6], I), "TB": sb([16, 16], B),
+    "TBT": sb([16, 16], B), "O16": sb([256], U), "OF": sb([16], F), "OU": sb([16], U), "EG": sb([256], B),
+    "NW": sb([256], B), "NC": sb([256], F), "CNT": sb([2176], B), "SM": sb([12, 16], F), "TG": sb([16], U), "TC": sb([16], U),
+    "MK": sb([256], F), "MX": sb([256], F), "SC": sb([256], F), "SD": sb([272], F),
+    "LNX": sb([4, 7, 48], B), "LNS": sb([6, 7, 48], B), "CHB": sb([NR], B),
+    "LOSE": sb([2, NR], B), "NE": sb([NR], B), "GR": sb([5, 1536], B), "ACC": sb([1024], B),
+    "FL": sb([96], B), "FK": sb([96], B), "INC": sb([96], B), "NF": sb([96], F), "RR": sb([96], F), "PS": sb([96], U),
+    "OWN": sb([256], B), "OR": sb([256], F), "P2": sb([256], B), "P2T": sb([256], B), "XO": sb([256], B), "KG": sb([256], B),
     "NX": sb([2, 256], I), "DF": sb([256], F),
     "OFF": sb([96], F), "OFL": sb([96], U), "YWB": sb([128], F), "YOB": sb([2, 96], F), "YFB": sb([96], F),
 }
 for _n in "ABCDEFGH":
-    SCRATCH["P" + _n] = ("psum", [128, 512], F)
-DMAS = ["nl", "ovf", "va", "w32", "s32", "o32", "xv", "kc", "rl", "y", "yw", "yo", "yf"]
-SEMAPHORES = ["sv", "sa", "sp", "sg", "ls"] + ["ar%d" % m for m in range(6)] + ["d_" + n for n in DMAS]
-M_I, M_NI, M_IB, M_B01, M_B2, M_B15, M_S00, M_S11, M_S10, M_S01, M_P, M_T0, M_T2, M_LA, M_LB, M_RS, M_A = (
-    0, 1, 2, 3, 4, 5, 6, 7, 8, 9, 10, 17, 18, 19, 20, 21, 22)
+    SCRATCH["P" + _n] = ("psum", [128, 32, 16] if _n in "CDH" else [128, 512], F)
+DMAS = ["nl", "ovf", "va", "w32", "s32", "xr", "xv", "kc", "vh", "y", "yw", "yo", "yf"]
+SEMAPHORES = ["sv", "sa", "sp", "sg", "ls", "lx"] + ["ar%d" % m for m in range(10)] + ["d_" + n for n in DMAS]
+M_134, M_N1, M_N2, M_I, M_NI, M_IB, M_SB, M_B0, M_OB, M_T0, M_T2, M_LA, M_LB, M_RS, M_OW, M_NO = range(16)
+W_KEY, W_W, W_OWN, W_OUT, W_ALL, W_7 = range(6)
+P_X, P_SCORE, P_ST, P_STALE = range(4)
+SHARE = (704, 736, 736, 688)
 INF = 10 ** 9
+NO_OUTPUT = -100000.0
 WAITS = -15800.0
 
 
@@ -162,14 +164,20 @@ def rank_program(g, core, T, topo):
     def sel(out, in_, pat, cmp, val, base, cm, r, w):
         op("g", lambda: g.affine_select(out, in_, pat, cmp, val, base, cm), r, w)
 
+    def mark(view, name, pat, base, val):
+        sel(view, view, pat, OP.not_equal, val, base, 1, [name], [name])
+
     def col(k):
         return T.COL[:, k:k + 1]
 
     def cn(k):
         return ("COL", k, k + 1)
 
+    def eye(k):
+        return T.EYE[:, k:k + 1]
+
     def mt(k):
-        return T.MT[:, k, :]
+        return T.MT[:, k]
 
     def mn(k):
         return ("MT", k, k + 1)
@@ -180,127 +188,138 @@ def rank_program(g, core, T, topo):
     def sn(k):
         return ("SM", k, k + 1)
 
-    def dsel(u):
-        return T.BW[:, 15 - u:143 - u]
+    def pb(name, n, at=0):
+        return T[name][:, at // 16:(at + n) // 16, :] if len(SCRATCH[name][1]) == 3 else T[name][:, at:at + n]
 
-    def dself(u):
-        return T.BWF[:, 15 - u:143 - u]
+    def pick(kind, u):
+        return T.BW[:, kind, 15 - u:143 - u]
 
-    def mark(k, pat, base, val, src=None):
-        if src is None:
-            sel(mt(k), T.ZB[:, 0:128], pat, OP.not_equal, val, base, 1, ["ZB"], [mn(k)])
-        else:
-            sel(mt(k), mt(src), pat, OP.not_equal, val, base, 1, [mn(src)], [mn(k)])
+    def to_psum_list(bank, at, kind, src, name, first=True, last=True):
+        mm([(pb(bank, 16, at), pick(kind, i), src(i), first and i == 0, last and i == 15) for i in range(16)], ["BW", name], [bank])
 
-    XG, WG, DG_ = T.XW[:, 0:2304], T.W1[:, 0:2304], T.DE[:, 0:2304]
-    DGP = T.PB[:, 256:512]
+    XG, SG = T.XW[:, 0:WV], T.ST[:, 0:WV]
+    DGP = pb("PB", 256, 256)
     REPL = slice(H_, V_)
+    SR, XR, CR = ("ST", H_, V_), ("XW", H_, V_), ("CH", H_, V_)
     ROW = [[-16, 8], [0, 16]]
+    (K_I, K_G, K_96, K_P0, K_P1, K_56, K_DEF, K_KEY, K_OWN, K_OUT, K_BST, K_BCS, K_EL, K_CV, K_CS, K_WRAP) = (
+        0, 1, 3, 4, 5, 6, 7, 8, 9, 10, 11, 12, 13, 16, 20, 24)
 
+    dma("s", "ovf", [(T.OVI[:], T.ov[:])], [], ["OVI"])
     dma("a", "w32", [(T.W32[0:32, :], T.wv[:])], [], ["W32"])
     dma("s", "nl", [(T.NLI[:], T.nl[:])], [], ["NLI"])
-    dma("a", "s32", [(T.S32[0:32, :], T.sc[:])], [], ["S32"])
-    dma("s", "ovf", [(T.OVI[:], T.ov[:])], [], ["OVI"])
     dma("s", "va", [(T.VA[:, 0:C_], T.va[:])], [], [("VA", 0, C_)])
-    dma("s", "xv", [(T.XW[:, 0:V_], T.xv[:])], [], [("XW", 0, V_)])
-    dma("s", "o32", [(T.O32[0:32, :], T.ov[:])], [], ["O32"])
-    dma("s", "kc", [(T.KK[:, 0:C_], T.kc[:])], [], [("KK", 0, C_)])
-    dma("s", "rl", [(T.RLI[:, k, :], T.va[k::16, :]) for k in range(16)], [], ["RLI"])
+    dma("s", "xr", [(T.XW[:, REPL], T.xv[:, REPL])], [], [XR])
+    dma("s", "s32", [(T.S32[0:32, :], T.sc[:]), (T.S32[32:64, :], T.ov[:]), (T.S32[64:96, :], T.ov[:])], [], ["S32"])
 
     iota(T.CI[:, 0:1], [[0, 1]], 0, 1, [("CI", 0, 1)], False)
-    iota(T.RV[0:32, :], [[-4, 8], [0, 16]], 0, 1, ["RV"])
-    iota(T.GV[:], [[1, 8], [0, 16]], 0, 0, ["GV"])
-    iota(T.VV[:], [[-1, 128]], 0, 1, ["VV"])
-    iota(T.PV[:], [[16, 8], [-1, 16]], 128, 1, ["PV"], False)
-    iota(T.ZV[:], [[0, 16], [1, 16]], 0, 0, ["ZV"])
-    iota(T.JT[:, 0, :], [[32, 8], [0, 2]], -2048, 0, ["JT"])
-    iota(T.Q16[:], [[16, 16]], 0, 0, ["Q16"])
-    iota(T.CJ[:, 0, :], [[1, 96]], C_, 0, ["CJ"])
-    iota(T.CV[:], [[-256, 96], [-24576, 16]], 256 * C_, 0, ["CV"])
-    fill(T.ZB[:, 0:128], 128, 0, ["ZB"])
-    for k, base, hb in ((M_S00, 0, 0), (M_S11, -16, -1000), (M_S10, 0, -1000), (M_S01, -16, 0)):
-        mark(k, [[-32, 4], [1000, 2], [-1, 16]], base + hb, 1.0)
-    mark(M_B01, ROW, 0, 1.0)
-    mark(M_B01, ROW, -1, 1.0, M_B01)
-    mark(M_B2, ROW, -2, 1.0)
-    iota(T.LW[:, 512:2056], [[-256, 1544]], 256 * C_, 0, ["LW"])
-    fill(T.STL[:], 256, 4096, ["STL"])
-    mark(M_NI, [[-1, 128]], 0, -1.0)
-    fill(T.ONE[:], 256, 1, ["ONE"])
-    fill(T.TIE[0:1, :], NR, 0, ["TIE"])
-    for d in range(1, 8):
-        if rank > (rank ^ d):
-            fill(T.TIE[0:1, 48 * (d - 1):48 * d], 48, 1, ["TIE"])
+    iota(T.EYE[:], [[1, 16]], 0, 0, ["EYE"])
+    need("g", ("sg", count["sg"]))
+    iota(T.KC[64:96, :], [[1, 32], [0, 16]], 0, 0, [("KC", 2, 3)])
+    need("g", ("sg", count["sg"]))
+    iota(T.KC[96:128, :], [[0, 32], [1, 16]], 0, 0, [("KC", 3, 4)])
+    need("g", ("sg", count["sg"]))
+    iota(T.CJ[:, 0, :], [[1, 96]], 0, 0, [("CJ", 0, 1)])
+    ms(T.ACC[:, 0:1024], 0.0, ["ACC"])
+    ms(T.KM[:], 0.0, ["KM"])
+    ms(T.RU[:], 0.0, ["RU"])
 
-    ms(T.D0[:], 1.0, ["D0"])
-    act(DG_, T.D0[:], ["D0"], ["DE"], scale=0.0)
+    def blank(out, n, w, val=0.0):
+        act(out, T.ACC[:, 0:n], ["ACC"], w, bias=val)
+
+    blank(T.ST[:, 0:1024], 1024, [("ST", 0, 1024)])
+    blank(T.ST[:, 1024:V_], 1024, [("ST", 1024, V_)])
+    blank(T.BD[:], 960, ["BD"])
     ts(T.CI[:, 1:2], T.CI[:, 0:1], 15, OP.bitwise_and, ["CI"], [("CI", 1, 2)])
     ts(T.CI[:, 2:3], T.CI[:, 0:1], 4, OP.arith_shift_right, [("CI", 0, 1)], [("CI", 2, 3)])
-    ts(T.CI[:, 3:4], T.CI[:, 0:1], 31, OP.bitwise_and, [("CI", 0, 1)], [("CI", 3, 4)])
-    for u in range(4):
-        ts(T.REP[0:32, u, :], T.RV[0:32, :], float(u), OP.is_equal, ["RV"], [("REP", u, u + 1)])
+    ts(T.CI[:, 3:4], T.CI[:, 0:1], 4, OP.arith_shift_right, [("CI", 0, 1)], [("CI", 3, 4)], 1, OP.bitwise_and)
+    for view, val in ((T.KM[64:65, 5, :, 4], -1.0), (T.KM[96:97, 5, :, 3], -96.0), (T.KM[64:65, 0:4, :, 5], 16.0),
+                      (T.KM[96:97, 0:4, :, 6], 1.0), (T.KM[32:33, 0:4, :, 1], -255.0),
+                      (T.KM[32:33, 1, :, 5], 512.0), (T.KM[32:33, 2, :, 5], 1024.0), (T.KM[32:33, 3, :, 5], 1536.0),
+                      (T.KM[64:65, 4, :, 3], -16.0), (T.KM[96:97, 4, :, 4], -1.0)):
+        op("v", lambda: v.memset(view, val), ["KM"], [("KM", -1, -1)])
     cp(T.COL[:, 0:3], T.CI[:, 1:4], ["CI"], [("COL", 0, 3)])
-    ms(T.VA[:, C_:1544], 0, [("VA", C_, 1544)])
-    ms(T.S16[:, C_:1544], 0.0, [("S16", C_, 1544)])
-    ms(T.W1[:, V_:2304], 0.0, [("W1", V_, 2304)])
-    ms(T.BW[:], 0.0, ["BW"])
-    ts(col(3), col(0), 96.0, OP.mult, [cn(0)], [cn(3)])
-    ts(col(4), col(0), 4096.0, OP.mult, [cn(0)], [cn(4)], -65536.0, OP.add)
-    ts(T.BB[:], T.GV[:], col(1), OP.is_equal, ["GV", cn(1)], ["BB"])
-    ts(T.IF[:], T.VV[:], 0.0, OP.is_equal, ["VV"], ["IF"])
-    ts(T.BW[:, 15:143:16], T.BB[:, 0::16], 4096.0, OP.mult, ["BB"], ["BW"])
-    cp(T.W32B[0:32, :], T.W32[0:32, :], ["W32"], ["W32B"])
-    banks = ["PA", "PB", "PC", "PD"]
+    ms(T.KM[0:1, 6], 4096.0, ["KM"])
+    ms(T.KC[32:64, :], 1.0, [("KC", 1, 2)])
+    ts(T.EYE[:], T.EYE[:], col(K_I), OP.is_equal, ["EYE", cn(K_I)], ["EYE"])
+    ts(col(K_96), col(K_I), 96.0, OP.mult, [cn(K_I)], [cn(K_96)])
+    ts(col(K_DEF), eye(1), 256.0, OP.mult, ["EYE"], [cn(K_DEF)])
+    ts(col(K_P0), col(2), -1.0, OP.mult, [cn(2)], [cn(K_P0)], 1.0, OP.add)
+    ts(col(K_DEF), eye(3), 1440.0, OP.mult, ["EYE", cn(K_DEF)], [cn(K_DEF)], col(K_DEF), OP.add)
     for u in range(4):
-        mm([(T[banks[u]][:, :], T.REP[0:32, u, :], T.W32B[0:32, :], True, True)], ["REP", "W32B"], [banks[u]])
-    cp(T.S32B[0:32, :], T.S32[0:32, :], ["S32"], ["S32B"])
-    cp(T.LN[:], T.NLI[:], ["NLI"], ["LN"])
-    cp(T.LNF[:], T.NLI[:], ["NLI"], ["LNF"])
+        ts(col(K_CV + u), eye(4), 96.0 - 24 * u, OP.mult, ["EYE", cn(K_DEF)], [cn(K_CV + u)], col(K_DEF), OP.add)
     for u in range(4):
-        act(T.W1[:, 512 * u:512 * u + 512], T[banks[u]][:, :], [banks[u]], [("W1", 512 * u, 512 * u + 512)], bias=1.0)
-    sb_ = ["PE", "PF", "PG", "PH"]
+        mark(T.KM[0:32, u, :, 0:2], ("KM", u, u + 1), [[-4, 8], [0, 2]], -u, 1.0)
+    mm([(pb("PA", 384), T.KM[64:128, 5], T.KC[64:128, 0:384], True, True)], [("KM", 5, 6), ("KC", 2, 4)], ["PA"])
     for u in range(4):
-        mm([(T[sb_[u]][:, 0:384], T.REP[0:32, u, :], T.S32B[0:32, :], True, True)], ["REP", "S32B"], [sb_[u]])
-    ts(T.PV[:], T.PV[:], 127, OP.bitwise_and, ["PV"], ["PV"])
-    ts(T.RS0[:], T.ZV[:], 0.0, OP.is_equal, ["ZV"], ["RS0"], BIG, OP.mult)
-    ts(T.RS1[:], T.ZV[:], 1.0, OP.is_equal, ["ZV"], ["RS1"], BIG, OP.mult)
-    for d in range(1, 8):
-        ts(mt(M_P + d - 1), T.PV[:], float(16 * d), OP.is_equal, ["PV"], [mn(M_P + d - 1)])
+        act(T.CV2[:, 384 * u:384 * u + 384], pb("PA", 384), ["PA", cn(K_CV + u)], [("CV2", u, u + 1)], bias=col(K_CV + u))
+    cp(T.KC[0:32, :], T.W32[0:32, :], ["W32"], [("KC", 0, 1)])
+    ts(T.CJ[:, 0, :], T.CJ[:, 0, :], col(K_96), OP.add, [("CJ", 0, 1), cn(K_96)], [("CJ", 0, 1)])
+    ts(T.NF[:], T.OVI[:], 2047.5, OP.is_gt, ["OVI"], ["NF"])
+    ts(T.CJ[:, 1, :], T.CJ[:, 0, :], float(WV), OP.add, [("CJ", 0, 1)], [("CJ", 1, 2)])
+    ts(T.CO[:, 0, :], T.NLI[:], -1.0, OP.mult, ["NLI"], [("CO", 0, 1)], float(C_), OP.add)
+    tt(T.NF[:], T.NF[:], T.CJ[:, 1, :], OP.mult, ["NF", ("CJ", 1, 2)], ["NF"])
+    ms(T.ST[:, V_:V_ + 1], -1.0, [("ST", V_, V_ + 1)])
+    ms(T.ST[:, V_ + 1:DV], 255.0, [("ST", V_ + 1, DV)])
+    tt(T.NF[:], T.NF[:], T.OVI[:], OP.max, ["NF", "OVI"], ["NF"])
+    ms(T.ST[:, DV:WV], 0.0, [("ST", DV, WV)])
+    cp(T.PS[:], T.NF[:], ["NF"], ["PS"])
+    wb = ["PE", "PF", "PG", "PH"]
 
-    def lane_lists(first=False):
-        if not first:
-            act(T.SG[:], T.S16[:].indirect(T.LN[:]), ["S16", "LN"], ["SG"])
+    def state_mm(u, last):
+        return [(pb(wb[u], 512), T.KM[:, u], T.KC[:], True, last)]
+
+    for u in range(4):
+        mm(state_mm(u, True), [("KM", u, u + 1), "KC"], [wb[u]])
+        act(T.W0[:, 512 * u:512 * u + 512], pb(wb[u], 512), [wb[u]], [("W0", u, u + 1)])
+
+    def state_build(u, part):
+        piece, nm = T.ST[:, 512 * u:512 * u + 512], ("ST", 512 * u, 512 * u + 512)
+        if part == 0:
+            mm(state_mm(u, False), ["KM", "KC"], [wb[u]])
+        if part == 1:
+            mm([(pb(wb[u], 512), mt(M_134), piece, False, True)], [mn(M_134), nm], [wb[u]])
+        if part == 2:
+            op("a", lambda: a.activation(piece, pb(wb[u], 512), AF.Relu), [wb[u]], [nm])
+
+    def turn_list(k):
+        ts(T.TP[:, 0:16], T.CO[:, k, :], col(K_P0), OP.mult, [("CO", k, k + 1), cn(K_P0)], [("TP", 0, 1)])
+        ts(T.TP[:, 16:32], T.CO[:, k, :], col(2), OP.mult, [("CO", k, k + 1), cn(2)], [("TP", 1, 2)])
+        tr(T.TQ[:], T.TP[:], ["TP"], ["TQ"])
+        tt(sm(9), T.TQ[:, 0:16], T.TQ[:, 16:32], OP.add, ["TQ"], [sn(9)])
+        ts(T.LN[:], sm(9), -1.0, OP.mult, [sn(9)], ["LN"], float(C_), OP.add)
+
+    def owners(u):
+        cp(T.ST[:].indirect(T.PS[:, 24 * u:24 * u + 24]), T.CV2[:, 384 * u:384 * u + 384], ["PS", ("CV2", u, u + 1)], ["ST"])
+
+    def lane_rows():
         cp(T.ROWS[:], T.VA[:].indirect(T.LN[:]), ["VA", "LN"], ["ROWS"])
-        ts(T.RK[:], T.VA[:].indirect(T.LN[:]), col(4), OP.add, ["VA", "LN", cn(4)], ["RK"])
-        mm([(T.PA[:, 0:256], T.IF[:], T.RK[:], True, False)], ["IF", "RK"], ["PA"])
 
-    def sentinels():
-        tr(T.ST[:], T.SG[:], ["SG"], ["ST"])
-        for f in range(2):
-            tt(T.SENT[:, f, :], T.ST[:, 0::16], T.JT[:, f, :], OP.add, ["ST", "JT"], [("SENT", f, f + 1)])
-
-    def gath(e, dn, lo, hi):
-        win, wn = (WG, "W1") if dn == "GW" else (XG, "XW")
-        if hi > lo:
-            (cp if e == "v" else act)(T[dn][:, 16 * lo:16 * hi], win.indirect(T.ROWS[:, lo:hi]), [wn, "ROWS"], [(dn, 16 * lo, 16 * hi)])
-
-    def key_mm(lo, hi, last):
-        mm([(T.PA[:, lo:hi], dsel(k), T.GW[:, 16 * lo + k:16 * hi:16], False, last and k == 15) for k in range(16)],
-           ["BW", ("GW", 16 * lo, 16 * hi)], ["PA"])
-
-    def sum_mm(lo, hi, last):
-        mm([(T.PC[:, lo:hi], mt(M_NI), T.GX[:, 16 * lo + k:16 * hi:16], False, last and k == 15) for k in range(16)],
-           [("GX", 16 * lo, 16 * hi)], ["PC"])
-
-    def rnd(dn, lo, mid, hi, last):
-        gath("v", dn, lo, mid)
-        gath("a", dn, mid, hi)
-        (key_mm if dn == "GW" else sum_mm)(lo, hi, last)
-
-    def to_list():
-        scan(T.SC[:], T.M0[:], T.MK[:], 0.0, OP.mult, OP.add, ["M0", "MK"], ["SC"])
-
-    ENDS = T.SC[:, 15::16]
+    ms(T.VA[:, C_:1544], 0, [("VA", C_, 1544)])
+    turn_list(0)
+    iota(T.GV[:], [[1, 8], [0, 16]], 0, 0, ["GV"])
+    iota(T.ZV[:], [[0, 16], [1, 16]], 0, 0, ["ZV"])
+    iota(T.Q16[:], [[16, 16]], 0, 0, ["Q16"])
+    blank(T.PW[:], 960, ["PW"])
+    ms(T.MT[:, 0:3], 0.0, [("MT", 0, 3)])
+    for u in range(4):
+        mark(T.RU[0:32, u, :, 0:2], ("RU", u, u + 1), [[-4, 8], [0, 2]], -u, 1.0)
+        mark(T.RU[0:96, u, :, 8:10], ("RU", u, u + 1), [[-4, 8], [-32, 2]], -u - 32, 1.0)
+    mark(T.MT[:, M_134, :, 1], mn(M_134), [[-16, 8]], -1, 1.0)
+    mark(T.MT[:, M_134, :, 3:5], mn(M_134), [[-16, 8], [-1, 2]], -3, 1.0)
+    owners(0)
+    ms(T.BW[:], 0.0, ["BW"])
+    ts(T.BB[:], T.GV[:], col(K_G), OP.is_equal, ["GV", cn(K_G)], ["BB"])
+    ts(col(K_56), eye(5), eye(6), OP.add, ["EYE"], [cn(K_56)])
+    ts(col(K_OWN), eye(3), eye(4), OP.add, ["EYE"], [cn(K_OWN)])
+    ts(col(K_OUT), eye(8), eye(9), OP.add, ["EYE"], [cn(K_OUT)])
+    ts(col(K_KEY), eye(0), 65536.0, OP.mult, ["EYE", cn(K_56)], [cn(K_KEY)], col(K_56), OP.add)
+    ts(col(K_CS), eye(3), float(C_), OP.mult, ["EYE"], [cn(K_CS)], eye(1), OP.add)
+    lane_rows()
+    ts(col(K_CS), col(K_CS), 64.0, OP.mult, [cn(K_CS)], [cn(K_CS)])
+    for kind, wc in ((W_W, eye(0)), (W_OWN, col(K_OWN)), (W_OUT, col(K_OUT)), (W_ALL, 1.0), (W_7, eye(7)), (W_KEY, col(K_KEY))):
+        op("v", lambda: v.tensor_scalar(T.BW[:, kind, 15:143:16], T.BB[:, 0::16], wc, None, OP.mult), ["BB", "COL", "EYE", "BW"],
+           ["BW" if kind == W_KEY else ("BW", -1, -1)])
 
     peers = [T.cores[rank ^ d] for d in range(1, 8)]
     eng = topo.engines(core, peers[0])
@@ -312,339 +331,477 @@ def rank_program(g, core, T, topo):
     for k, p in enumerate(far + near):
         masks[p] = sum(1 << e for e in pool[per * k:per * k + per])
 
-    def snd(m, f):
-        return T.SND[:, m, :, 48 * f:48 * f + 48]
-
-    def pack_x(m):
-        act(snd(m, 0), T.XW[:, REPL], ["XW"], [("SND", 3 * m, 3 * m + 1)])
-
-    def pack_w(m):
-        act(snd(m, 1), T.W1[:, REPL], ["W1"], [("SND", 3 * m + 1, 3 * m + 2)])
-
-    def owners_psum():
-        act(T.PE[:, 0:NR], T.DE[:, REPL], ["DE"], ["PE"])
-
-    def send(m):
-        tt(snd(m, 2), T.W1[:, REPL], T.PE[:, 0:NR], OP.min, ["W1", "PE"], [("SND", 3 * m + 2, 3 * m + 3)])
-        if m < 3:
-            cp(snd(m, 1), T.W1[:, REPL], ["W1"], [("SND", 3 * m + 1, 3 * m + 2)])
-        order("g", [("SND", 3 * m, 3 * m + 3)], [])
+    def send(m, src, dst, reads):
+        order("g", reads, [])
         trs = []
-        for d in range(1, 8):
-            p = peers[d - 1]
-            rid, pid, _ = topo.addr(p)
-            trs.append(RemoteDMATransfer(dst_ids=[DstId(rid=rid, pnc=pid)], dma_engine_mask=masks[p],
-                                         remote_sem=T.sem["ar%d" % m], src=T.SND[:, m, d - 1, :], dst=T.LND[:, m, d - 1, :]))
-        g.remote_dma_fused(trs, local_sem=T.sem.ls)
-        count["ls"] = count.get("ls", 0) + 7 * per
-        sr = ("SND", 3 * m, 3 * m + 3)
-        mm([(T.PE[:, 0:NR], mt(M_NI), snd(m, 2), True, False),
-            (T.PE[:, 0:NR], T.ONE[0:1, 0:128], T.TIE[0:1, :], False, False)], [sr, mn(M_NI), "ONE", "TIE"], ["PE"])
-        mm([(T.PF[:, 0:NR], mt(M_NI), snd(m, 1), True, False)], [sr], ["PF"])
+        for d in range(7):
+            rid, pid, _ = topo.addr(peers[d])
+            trs.append(RemoteDMATransfer(dst_ids=[DstId(rid=rid, pnc=pid)], dma_engine_mask=masks[peers[d]],
+                                         remote_sem=T.sem["ar%d" % m], src=src(d), dst=dst(d)))
+        ls = "ls" if m < 6 else "lx"
+        g.remote_dma_fused(trs, local_sem=T.sem[ls])
+        count[ls] = count.get(ls, 0) + 7 * per
+        note("remote", reads, [], (ls, count[ls]))
 
-    def mine_x(m):
-        mm([(T.PG[:, 0:NR], mt(M_NI), snd(m, 0), True, False)], [("SND", 3 * m, 3 * m + 3)], ["PG"])
+    def mine(src, reads):
+        mm([(pb("PE", NR), mt(M_N1), src, True, False), (pb("PE", NR), T.ONE[0:1, 0:128], T.TIE[0:1, :], False, False)],
+           reads + [mn(M_N1), "ONE", "TIE"], ["PE"])
+        mm([(pb("PF", NR), mt(M_N2), src, True, False)], reads + [mn(M_N2)], ["PF"])
 
-    def arrive(m, xfirst):
+    def theirs(m, bank, kind, land, first=False):
         need("p", ("ar%d" % m, 7 * per))
-        for f, bank in ((2, "PE"), (0, "PG"), (1, "PF")) if xfirst else ((2, "PE"), (1, "PF"), (0, "PG")):
-            mm([(T[bank][:, 48 * d:48 * d + 48], mt(M_P + d), T.LND[:, m, d, 48 * f:48 * f + 48], False, d == 6)
-                for d in range(7)], [("MT", M_P, M_P + 7)], [bank])
-        ts(T.LOSE[:], T.PE[:, 0:NR], 0.5, OP.is_gt, ["PE"], ["LOSE"])
+        mm([(pb(bank, 48, 48 * d), T.PW[:, kind, 6 - d:14 - d, :], land(d), first and d == 0, d == 6) for d in range(7)],
+           [("PW", kind, kind + 1)], [bank])
 
-    def upd_w():
-        tt(T.PF[:, 0:NR], T.PF[:, 0:NR], T.LOSE[:], OP.mult, ["PF", "LOSE"], ["PF"])
-        tt(T.W1[:, REPL], T.W1[:, REPL], T.PF[:, 0:NR], OP.add, ["PF", ("W1", H_, V_)], [("W1", H_, V_)])
+    def lose(k):
+        ts(T.LOSE[:, k, :], pb("PE", NR), 0.0, OP.is_gt, ["PE"], [("LOSE", k, k + 1)])
 
-    def upd_z():
-        tt(T.PG[:, 0:NR], T.PG[:, 0:NR], T.LOSE[:], OP.mult, ["PG", "LOSE"], ["PG"])
+    def taken(bank, k):
+        tt(pb(bank, NR), pb(bank, NR), T.LOSE[:, k, :], OP.mult, [bank, ("LOSE", k, k + 1)], [bank])
 
-    def upd_ch():
-        tt(T.CH[:, REPL], T.PG[:, 0:NR], T.CH[:, REPL], OP.not_equal, ["PG", ("CH", H_, V_)], [("CH", H_, V_)])
+    def upd_st():
+        tt(T.ST[:, REPL], T.ST[:, REPL], pb("PF", NR), OP.add, ["PF", SR], [SR])
 
-    def upd_xd():
-        ts(T.PE[:, 0:NR], T.PE[:, 0:NR], 0.5, OP.is_lt, ["PE"], ["PE"])
-        tt(T.XW[:, REPL], T.XW[:, REPL], T.PG[:, 0:NR], OP.add, ["PG", ("XW", H_, V_)], [("XW", H_, V_)])
-        tt(T.DE[:, REPL], T.DE[:, REPL], T.PE[:, 0:NR], OP.mult, ["PE", ("DE", H_, V_)], [("DE", H_, V_)])
+    def upd_x():
+        tt(T.XW[:, REPL], T.XW[:, REPL], pb("PG", NR), OP.add, ["PG", XR], [XR])
 
-    def halve():
-        act(T.CH[:, REPL], T.CH[:, REPL], [("CH", H_, V_)], [("CH", H_, V_)], scale=0.5)
+    def upd_ch(bank):
+        tt(T.CH[:, REPL], pb(bank, NR), T.CH[:, REPL], OP.not_equal, [bank, CR], [CR])
+
+    def rows_consts(k, spec_):
+        for qp in range(2):
+            for lo, hi, step, s in spec_:
+                mark(T.BD[:, 2 * k + qp, 1 + qp:9:2, lo:hi], ("BD", 2 * k + qp, 2 * k + qp + 1), [[-32, 4], [-step, hi - lo]], -16 * qp - s, 1.0)
+
+    def rows_mm(bank, k):
+        lst = []
+        for qp in range(2):
+            for gp in range(2):
+                at = 1 + qp - gp
+                lst.append((T[bank][:, qp:16:2, :], T.BD[:, 2 * k + qp, at:at + 8, :], T.TBT[:, gp::2, :], gp == 0, gp == 1))
+        mm(lst, ["TBT", ("BD", 2 * k, 2 * k + 2)], [bank])
+
+    def partner_consts(kind, lo, hi, step, s, src_step):
+        for base in (-112, -240):
+            mark(T.PW[:, kind, :, lo:hi:step], ("PW", kind, kind + 1), [[16, 15], [-src_step, len(range(lo, hi, step))]], base - s, 1.0)
+
+    def send_x(m):
+        send(6 + m, lambda d: T.XW[:, H_ + 48 * d:H_ + 48 * d + 48], lambda d: T.LNX[:, m, d, :], [XR])
+
+    def send_state(m):
+        send(m, lambda d: T.ST[:, H_ + 48 * d:H_ + 48 * d + 48], lambda d: T.LNS[:, m, d, :], [SR])
+
+    def x_gap(m):
+        mm([(pb("PG", NR), mt(M_NI), T.XW[:, REPL], True, False)], [XR, mn(M_NI)], ["PG"])
+        theirs(6 + m, "PG", P_X, lambda d: T.LNX[:, m, d, :])
+
+
+    def gath(e, dn, win, wn, lo, hi):
+        if hi > lo:
+            (cp if e == "v" else act)(T[dn][:, 16 * lo:16 * hi], win.indirect(T.ROWS[:, lo:hi]), [wn, "ROWS"], [(dn, 16 * lo, 16 * hi)])
+
+    def key_start():
+        mm([(pb("PA", 256), T.KM[0:1, 6], T.ZV[0:1, :], True, False)], ["KM", "ZV"], ["PA"])
+
+    def key_blocks(lo, hi, last):
+        mm([(pb("PA", 256), pick(W_KEY, i), T.GW[:, 256 * i:256 * i + 256], False, last and i == hi - 1) for i in range(lo, hi)],
+           ["BW", ("GW", 256 * lo, 256 * hi)], ["PA"])
+
+    def strengths():
+        act(T.CSG[:], T.CF[:].indirect(T.LN[:]), ["CF", "LN"], ["CSG"], scale=1.0 / 64)
+        to_psum_list("PB", 16, W_KEY, lambda i: T.CSG[:, 16 * i:16 * i + 16], "CSG")
+
+    def lane_fields(k):
+        cp(T.R2[:, :, 5], T.CO[:, k, :], [("CO", k, k + 1)], [("R2", 5, 6)])
+        for f in range(2):
+            tt(T.SENT[:, f, :], pb("PB", 16, 16), T.JT[:, f, :], OP.add, ["PB", "JT"], [("SENT", f, f + 1)])
+        ts(T.R2[:, :, 3], T.R2[:, :, 5], 4080, OP.bitwise_and, [("R2", 5, 6)], [("R2", 3, 4)])
+        ts(T.R2[:, :, 4], T.R2[:, :, 5], 15, OP.bitwise_and, [("R2", 5, 6)], [("R2", 4, 5)])
+        ts(T.TB[:, :, 5], pb("PB", 16, 16), 2.0 ** -16, OP.mult, ["PB"], [("TB", 5, 6)])
+        cp(T.TB[:, :, 3:5], T.R2[:, :, 3:5], [("R2", 3, 5)], [("TB", 3, 5)])
 
     def consts_steal():
         ms(T.DG[:, 16:32], 0.0, [("DG", 16, 32)])
-        ts(T.DG[:, 0:16], T.ZV[:, 0:16], col(0), OP.is_equal, ["ZV", cn(0)], [("DG", 0, 16)], float(2 ** 20), OP.mult)
-        ts(T.JT[:, 0, :], T.JT[:, 0, :], col(2), OP.add, ["JT", cn(2)], ["JT"])
-        ts(T.DG[:, 0:16], T.DG[:, 0:16], 1.0, OP.max, ["DG"], ["DG"])
-        ts(T.JT[:, 1, :], T.JT[:, 0, :], 4096.0, OP.add, ["JT"], ["JT"])
+        ts(T.DG[:, 0:16], T.EYE[:], float(2 ** 20), OP.mult, ["EYE"], [("DG", 0, 16)], 1.0, OP.max)
         ms(T.TB[:], 0.0, ["TB"])
-        ts(col(9), col(0), 8.0, OP.mult, [cn(0)], [cn(9)], 24.0, OP.add)
-        ts(T.JK[:, 0, :], T.Q16[:], col(0), OP.add, ["Q16", cn(0)], [("JK", 0, 1)], 2048.0, OP.add)
-        ts(T.JK[:, 1, :], T.Q16[:], col(0), OP.add, ["Q16", cn(0)], [("JK", 1, 2)], 1600.0, OP.add)
-        ts(T.EL[:, 0:1], col(9), col(0), OP.mult, [cn(9), cn(0)], ["EL"], 15.0, OP.add)
-        ms(T.XW[:, V_:2304], 0.0, [("XW", V_, 2304)])
+        ms(T.PQ[:, 0, 0:1], 0.0, ["PQ"])
+        ts(col(K_EL), col(K_I), 8.0, OP.mult, [cn(K_I)], [cn(K_EL)], 24.0, OP.add)
+        ts(T.JK[:, 0, :], T.Q16[:], col(K_I), OP.add, ["Q16", cn(K_I)], [("JK", 0, 1)], float(DV), OP.add)
+        ts(T.JK[:, 1, :], T.Q16[:], col(K_I), OP.add, ["Q16", cn(K_I)], [("JK", 1, 2)], float(DC), OP.add)
+        ts(T.EL[:, 0:1], col(K_EL), col(K_I), OP.mult, [cn(K_EL), cn(K_I)], ["EL"], 15.0, OP.add)
+        ts(T.JT[:, 0, :], T.JK[:, 0, :], -4096.0, OP.add, ["JK"], [("JT", 0, 1)])
+        ts(T.JT[:, 1, :], T.JK[:, 0, :], 0.0, OP.add, ["JK"], [("JT", 1, 2)])
+        ts(T.RS0[:], T.ZV[:], 0.0, OP.is_equal, ["ZV"], ["RS0"], BIG, OP.mult)
+        ts(T.RS1[:], T.ZV[:], 1.0, OP.is_equal, ["ZV"], ["RS1"], BIG, OP.mult)
+        ts(col(K_BST), eye(2), 4096.0, OP.mult, ["EYE"], [cn(K_BST)], eye(1), OP.add)
+        ts(col(K_BCS), eye(7), eye(1), OP.add, ["EYE"], [cn(K_BCS)], 64.0, OP.mult)
 
-    def owners_list():
-        ts(T.CJ[:, 0, :], T.CJ[:, 0, :], col(3), OP.add, ["CJ", cn(3)], ["CJ"])
-        cp(T.RR[:, 0, :], T.OVI[:], ["OVI"], ["RR"])
-        ts(T.CJ[:, 1, :], T.CJ[:, 0, :], 768.0, OP.add, ["CJ"], ["CJ"])
-        ts(T.NF[:], T.RR[:, 0, :], 2047.5, OP.is_gt, ["RR"], ["NF"])
-        tt(T.NF[:], T.NF[:], T.CJ[:, 1, :], OP.mult, ["NF", "CJ"], ["NF"])
-        tt(T.NF[:], T.NF[:], T.RR[:, 0, :], OP.max, ["NF", "RR"], ["NF"])
-        cp(T.PS[:], T.NF[:], ["NF"], ["PS"])
+    def cs_sources():
+        ts(T.S32[32:64, :], T.S32[32:64, :], 4080, OP.bitwise_and, ["S32"], [("S32", 1, 2)])
+        ts(T.S32[64:96, :], T.S32[64:96, :], 15, OP.bitwise_and, [("S32", 2, 3)], [("S32", 2, 3)])
+        for u in range(1, 4):
+            ts(col(K_CS + u), eye(3), -384.0 * 64 * u, OP.mult, ["EYE", cn(K_CS)], [cn(K_CS + u)], col(K_CS), OP.add)
+        cp(T.S32B[0:96, :], T.S32[0:96, :], ["S32"], ["S32B"])
+        ms(T.ONE[:], 1.0, ["ONE"])
+        for lo, hi in ((1, 2), (2, 4), (4, 8)):
+            ms(T.TIE[0:1, 48 * (lo - 1):48 * (hi - 1)], 0.5 if rank > (rank ^ lo) else -0.5, [("TIE", lo, hi)])
+        ts(T.CF[:, C_:WC], T.ONE[:], eye(8), OP.mult, ["ONE", "EYE"], [("CF", C_, WC)], 2048.0 * 64, OP.mult)
 
-    def consts_out():
-        ob = ["PE", "PF", "PA", "PH"]
-        for u in range(4):
-            mm([(T[ob[u]][:, 0:384], T.REPF[0:32, u, :], T.O32F[0:32, :], True, True)], ["REPF", "O32F"], [ob[u]])
-            if u < 3:
-                act(T.OO[:, 384 * u:384 * u + 384], T[ob[u]][:, 0:384], [ob[u]], [("OO", 384 * u, 384 * u + 384)])
+    def cs_build(u):
+        bk = ["PB", "PC", "PD", "PC"][u]
+        mm([(pb(bk, 384), T.RU[0:96, u], T.S32B[0:96, :], True, False),
+            (pb(bk, 384), T.KM[64:128, 4], T.KC[64:128, 0:384], False, True)], ["RU", "S32B", "KM", "KC"], [bk])
+        act(T.CF[:, 384 * u:384 * u + 384], pb(bk, 384), [bk, cn(K_CS + u)], [("CF", 384 * u, 384 * u + 384)], bias=col(K_CS + u), scale=64.0)
+
+    def consts_meet():
+        mark(mt(M_N1), mn(M_N1), ROW, -1, -1.0)
+        mark(T.MT[:, M_N2, :, 0:5], mn(M_N2), [[-16, 8], [-1, 5]], 0, -1.0)
+        mark(T.MT[:, M_N2, :, 7], mn(M_N2), [[-16, 8]], -2, -1.0)
+        partner_consts(P_SCORE, 0, 16, 1, 1, 0)
+        partner_consts(P_ST, 0, 3, 2, 0, 2)
+        partner_consts(P_ST, 7, 8, 1, 2, 0)
+
+    def consts_later_g():
+        partner_consts(P_X, 0, 16, 1, 0, 1)
+        mark(mt(M_NI), mn(M_NI), [[-1, 128]], 0, -1.0)
+        partner_consts(P_STALE, 0, 16, 1, 2, 0)
+        fill(T.CH[:, REPL], NR, 0, [CR])
+        iota(T.RS4[:], [[0, 64], [-256, 16]], 256, 0, ["RS4"])
 
     def consts_plan_g():
-        mark(M_I, [[-1, 128]], 0, 1.0)
-        mark(M_IB, [[-1, 128]], 0, BIG)
-        mark(M_B15, ROW, -15, 2.0 ** -16)
-        mark(M_RS, ROW, -7, -1.0)
+        mark(mt(M_SB), mn(M_SB), ROW, -2, 1.0)
+        mark(mt(M_I), mn(M_I), [[-1, 128]], 0, 1.0)
+        mark(mt(M_IB), mn(M_IB), [[-1, 128]], 0, BIG)
+        mark(T.MT[:, M_B0, :, 0:2], mn(M_B0), [[-16, 8], [0, 2]], 0, 1.0)
+        mark(mt(M_OW), mn(M_OW), ROW, -3, 1.0)
+        mark(mt(M_OW), mn(M_OW), ROW, -4, 1.0)
+        mark(mt(M_NO), mn(M_NO), [[-1, 128]], 0, -131072.0)
+        mark(mt(M_OB), mn(M_OB), ROW, -8, 1.0)
+        mark(mt(M_OB), mn(M_OB), ROW, -9, 1.0)
+        mark(mt(M_RS), mn(M_RS), ROW, -7, -1.0)
         sel(mt(M_T0), T.BB[:], [[1, 128]], OP.is_gt, 0.0, 0, -1, ["BB"], [mn(M_T0)])
-        mark(M_T2, ROW, -15, 1.0, M_T0)
+        sel(mt(M_T2), mt(M_T0), ROW, OP.not_equal, 1.0, -15, 1, [mn(M_T0)], [mn(M_T2)])
         sel(mt(M_T2), mt(M_T2), [[0, 8], [1, 16]], OP.not_equal, 0.0, -15, 0, [mn(M_T2)], [mn(M_T2)])
+        fill(T.CH[:, 0:H_], H_, 0, [("CH", 0, H_)])
+        fill(T.CH[:, V_:WV], WV - V_, 0, [("CH", V_, WV)])
+
+    def consts_lift_g():
         fill(T.KK[:, C_:1552], 16, 0, [("KK", C_, 1552)])
-        fill(T.FK[:], 96, 0, ["FK"])
         fill(T.SD[:, 0:16], 16, 0, [("SD", 0, 16)])
         fill(T.LW[:, 0:256], 256, 0, ["LW"])
-        fill(T.LX[:, 0:256], 256, 0, ["LX"])
+        fill(T.XW[:, V_:WV], WV - V_, 0, [("XW", V_, WV)])
+        iota(T.CV[:], [[-256, 96], [-24576, 16]], 256 * C_, 0, ["CV"])
+        for k, s in ((M_LA, 8), (M_LB, 7)):
+            sel(T.MT[:, k, :, s:16], T.MT[:, M_T0, :, s:16], [[-16, 8], [0, 16 - s]], OP.is_ge, 0.0, -7, 1, [mn(M_T0)], [mn(k)])
+            sel(T.MT[:, k, :, 0:s], T.MT[:, M_T0, :, 0:s], [[16, 8], [0, s]], OP.is_gt, 1.0, 7, -1, [mn(M_T0)], [mn(k)])
+            sel(T.MT[:, k, :, 0:s], T.MT[:, k, :, 0:s], [[16, 8], [0, s]], OP.is_ge, 0.0, 15, -1, [mn(k)], [mn(k)])
 
-    def consts_plan_v():
-        ts(col(12), col(0), 7.0, OP.is_lt, [cn(0)], [cn(12)])
-        ts(mt(M_A), T.VV[:], 0.0, OP.is_lt, ["VV"], [mn(M_A)])
-        for k, s in ((M_LA, 8.0), (M_LB, 7.0)):
-            ts(T.TM[:], T.ZV[:, 0:128], s, OP.is_lt, ["ZV", cn(12)], ["TM"], col(12), OP.subtract)
-            tt(T.TM[:], T.TM[:], mt(M_A), OP.add, ["TM", mn(M_A)], ["TM"])
-            tt(mt(k), T.TM[:], T.BB[:], OP.mult, ["TM", "BB"], [mn(k)])
+    def consts_order(part):
+        if part == 0:
+            for j, s in enumerate((8.0, 7.0, 15.0)):
+                ts(col(K_WRAP + j), col(K_I), s, OP.is_lt, [cn(K_I)], [cn(K_WRAP + j)], float(C_), OP.mult)
+            ms(T.KM[0:1, 5], BIG, [("KM", 5, 6)])
+            ts(T.DGM[:], T.ZV[:], col(K_I), OP.is_equal, ["ZV", cn(K_I)], ["DGM"])
+            ms(T.KM[0:1, 5, :, 0], 0.0, [("KM", 5, 6)])
+            ms(T.KM[0:1, 5, :, 1], 1.0, [("KM", 5, 6)])
+            return
+        act(T.CJ[:, 1, :], T.CJ[:, 0, :], [("CJ", 0, 1)], [("CJ", 1, 2)], bias=float(C_), scale=-1.0)
+        for t in range(3):
+            act(T.CJ[:, 2 + t, :], T.CJ[:, 0, :], [("CJ", 0, 1)], [("CJ", 2 + t, 3 + t)], bias=C_ + 1.0 - 720 * t)
+        for j, (t, lo, hi) in enumerate(((1, 0, 48), (1, 48, 96), (2, 0, 96))):
+            act(T.CJ[:, 2 + t, lo:hi], T.CJ[:, 2 + t, lo:hi], [("CJ", 2 + t, 3 + t), cn(K_WRAP + j)], [("CJ", 2 + t, 3 + t)], bias=col(K_WRAP + j))
+        act(DGP, T.DGM[:], ["DGM"], ["PB"])
+        op("a", lambda: a.activation(T.M0[:], T.ZV[:], AF.Sign), ["ZV"], ["M0"])
 
-    CD = ["CD0", "CD1"]
-    lane_lists(True)
+    def inputs_only(lo, hi, bank, part):
+        n = hi - lo
+        if part == 0:
+            mm([(pb(bank, n), mt(M_OB), T.CS[:, lo:hi], True, True)], ["CS", mn(M_OB)], [bank])
+            tt(pb(bank, n), T.VA[:, lo:hi], pb(bank, n), OP.is_equal, ["VA", bank], [bank])
+        elif part == 1:
+            act(pb(bank, n), pb(bank, n), [bank], [bank], scale=V_ + 1.0)
+        else:
+            tt(T.VB[:, lo:hi], T.VA[:, lo:hi], pb(bank, n), OP.max, ["VA", bank], [("VB", lo, hi)])
+
+    def stale_x(lo, hi, bank):
+        mm([(pb(bank, hi - lo), mt(M_SB), T.ST[:, lo:hi], True, True)], [("ST", lo, hi), mn(M_SB)], [bank])
+        tt(T.XW[:, lo:hi], T.XW[:, lo:hi], pb(bank, hi - lo), OP.max, [bank, ("XW", lo, hi)], [("XW", lo, hi)])
+
+    rows_consts(0, [(0, 16, 0, 0), (0, 16, 0, 1)])
+    send_x(0)
+    rows_consts(1, [(0, 2, 0, 2), (3, 5, 1, 3), (5, 7, 1, 0)])
+    consts_meet()
+    rows_consts(2, [(0, 2, 0, 5), (3, 5, 1, 3), (8, 10, 1, 0)])
     for st in range(3):
-        cd, cdn = CD[st % 2], CD[(st + 1) % 2]
+        co, cx = st % 2, (st + 1) % 2
         if st == 0:
-            rnd("GW", 0, 60, 96, False)
             for u in range(4):
-                act(T.S16[:, 384 * u:384 * u + 384], T[sb_[u]][:, 0:384], [sb_[u]], [("S16", 384 * u, 384 * u + 384)], scale=65536.0)
-            act(T.SG[:], T.S16[:].indirect(T.LN[:]), ["S16", "LN"], ["SG"])
-            consts_steal()
-            owners_list()
-            rnd("GW", 96, 156, 192, False)
+                state_build(u, 0)
+            key_start()
+            for lo, hi in ((0, 4), (4, 8), (8, 11), (11, 14), (14, 16)):
+                gath("a", "GW", T.W0[:], "W0", 16 * lo, 16 * hi)
+                if lo == 4:
+                    for u in range(4):
+                        cs_build(u)
+                    strengths()
+                key_blocks(lo, hi, hi == 16)
+                if lo == 0:
+                    cs_sources()
+                    owners(1)
+                    owners(2)
+                    owners(3)
+                    consts_steal()
+                if lo == 4:
+                    lane_fields(0)
+            ms(T.D0[:], 1.0, ["D0"])
+            for u in range(4):
+                state_build(u, 1)
+                state_build(u, 2)
             for q in range(16):
                 at = 8 * q * (q + 1) + 16 * q
                 act(T.D0[:, at:at + 17], T.DG[:, 0:17], ["DG"], [("D0", at, at + 17)])
-            rnd("GW", 192, 230, 256, True)
-            strew(T.DE[:].indirect(T.PS[:]), T.CV[:], ["PS", "CV"], ["DE"])
-            act(T[cd][:], T.LW[:, 512:2056].indirect(T.LN[:]), ["LW", "LN"], [cd])
-            act(T.DE[:, V_:2304], T[cd][:], [cd], [("DE", V_, 2304)])
-            sentinels()
-            ts(T.DGM[:], T.ZV[:], col(0), OP.is_equal, ["ZV", cn(0)], ["DGM"])
         else:
-            rnd("GW", 0, 48, 96, False)
-            rnd("GW", 96, 140, 192, False)
-            rnd("GW", 192, 220, 256, True)
-            upd_z()
-            upd_xd()
-            act(T.DE[:, V_:2304], T[cd][:], [cd], [("DE", V_, 2304)])
-        tr(T.PH[:, 0:256], T.PA[:, 0:256], ["PA"], ["PH"])
-        scan(T.PQ[:, 0, :], T.RS0[:], T.PH[:, 0:256], BIG, OP.add, OP.min, ["RS0", "PH"], [("PQ", 0, 1)])
-        tt(T.ZZ[:, 1:256], T.PH[:, 1:256], T.PQ[:, 0, 0:255], OP.max, ["PH", ("PQ", 0, 1)], ["ZZ"])
-        scan(T.PQ[:, 1, 1:256], T.RS1[:, 1:256], T.ZZ[:, 1:256], BIG, OP.add, OP.min, ["RS1", "ZZ"], [("PQ", 1, 2)])
-        tt(T.R1[:], T.PQ[:, :, 15::16], T.SENT[:], OP.min, ["PQ", "SENT"], ["R1"])
-        ts(T.R2[:, :, 0:1], T.R1[:, 0, :], 4032, OP.bitwise_and, ["R1"], [("R2", 0, 1)])
-        ts(T.R2[:, :, 1:2], T.R1[:, 0, :], 63, OP.bitwise_and, ["R1"], [("R2", 1, 2)])
-        ts(T.R2[:, :, 2:3], T.R1[:, 1, :], 16, OP.arith_shift_right, ["R1"], [("R2", 2, 3)])
-        cp(T.TB[:, :, 0:3], T.R2[:], ["R2"], ["TB"])
+            for lo, mid, hi in ((0, 1, 2), (2, 4, 6), (6, 8, 11), (11, 13, 15), (15, 15, 16)):
+                gath("v", "GW", SG, "ST", 16 * lo, 16 * mid)
+                gath("a", "GW", SG, "ST", 16 * mid, 16 * hi)
+                if mid > lo:
+                    key_blocks(lo, mid, False)
+                key_blocks(mid, hi, hi == 16)
+            upd_ch("PF")
+            if st == 1:
+                cp(T.VU[:], T.VA[:, 768:C_], ["VA"], ["VU"])
+            else:
+                ts(T.NE[:], pb("PG", NR), 0.0, OP.not_equal, ["PG"], ["NE"])
+                upd_x()
+                mm([(pb("PE", NR), pick(W_ALL, 7), T.NE[:], True, True)], ["NE", "BW"], ["PE"])
+        scan(T.PQ[:, 0, 1:257], T.RS0[:], pb("PA", 256), BIG, OP.add, OP.min, ["RS0", "PA"], [("PQ", 0, 1)])
+        tt(T.ZZ[:], pb("PA", 256), T.PQ[:, 0, 0:256], OP.max, ["PA", ("PQ", 0, 1)], ["ZZ"])
+        scan(T.PQ[:, 1, 1:257], T.RS1[:], T.ZZ[:], BIG, OP.add, OP.min, ["RS1", "ZZ"], [("PQ", 1, 2)])
+        tt(T.R1[:], T.PQ[:, :, 16:257:16], T.SENT[:], OP.min, ["PQ", "SENT"], ["R1"])
+        ts(T.R2[:, :, 0], T.R1[:, 0, :], 4080, OP.bitwise_and, ["R1"], [("R2", 0, 1)])
+        ts(T.R2[:, :, 1], T.R1[:, 0, :], 15, OP.bitwise_and, ["R1"], [("R2", 1, 2)])
+        ts(T.R2[:, :, 2], T.R1[:, 1, :], 16, OP.arith_shift_right, ["R1"], [("R2", 2, 3)])
+        cp(T.TB[:, :, 0:3], T.R2[:, :, 0:3], [("R2", 0, 3)], [("TB", 0, 3)])
         tr(T.TBT[:], T.TB[:], ["TB"], ["TBT"])
-        lst = []
-        for y1 in range(2):
-            for h in range(2):
-                k = {(0, 0): M_S00, (1, 1): M_S11, (1, 0): M_S10, (0, 1): M_S01}[(h, y1)]
-                for s in range(2):
-                    lst.append((T.PB[:, y1:16:2], mt(k), T.TB[:, h::2, s:s + 1], h == 0 and s == 0, h == 1 and s == 1))
-        mm(lst, ["TB", ("MT", M_S00, M_S01 + 1)], ["PB"])
-        mm([(T.PC[:, 0:256], mt(M_B01), T.TBT[:], True, True)], ["TBT", mn(M_B01)], ["PC"])
-        mm([(T.PD[:, 0:256], mt(M_B2), T.TBT[:], True, True)], ["TBT", mn(M_B2)], ["PD"])
-        if st == 0:
-            ts(T.M0[:], T.ZV[:], 0.5, OP.is_gt, ["ZV"], ["M0"])
-            cp(T.O32F[0:32, :], T.O32[0:32, :], ["O32"], ["O32F"])
+        rows_mm("PC", 0)
+        rows_mm("PD", 1)
+        if st:
+            rows_mm("PH", 2)
+        tt(T.OF[:], T.R2[:, :, 0], T.R2[:, :, 1], OP.add, [("R2", 0, 2)], ["OF"])
+        if st < 2:
+            cp(T.OU[:], T.OF[:], ["OF"], ["OU"])
         else:
-            upd_ch()
-        cp(T.O16[:], T.PC[:, 0:256], ["PC"], ["O16"])
-        act(T.NW[:], T.PD[:, 0:256], ["PD"], ["NW"], bias=1.0)
-        if st > 0:
-            of = "DF" if st == 1 else "OF"
-            act(T[of][:], T.PC[:, 0:256], ["PC"], [of])
-            halve()
+            tt(T.CH[:, REPL], pb("PE", NR), T.CH[:, REPL], OP.max, ["PE", CR], [CR])
+        cp(T.O16[:], pb("PC", 256), ["PC"], ["O16"])
+        act(T.NW[:], pb("PD", 256), ["PD", cn(K_BST)], ["NW"], bias=col(K_BST))
+        if st < 2:
+            act(T.EG[:], SG.indirect(T.OU[:]), ["ST", "OU"], ["EG"])
+        if st == 0:
+            rows_mm("PC", 2)
+        act(T.NC[:], pb("PH" if st else "PC", 256), ["PH" if st else "PC", cn(K_BCS)], ["NC"], bias=col(K_BCS), scale=64.0)
+        if st < 2:
+            to_psum_list("PB", 0, W_OWN, lambda i: T.EG[:, i::16], "EG")
+        if st == 0:
+            act(T.MT[:, 3:16], T.GW[:, 0:1664], ["GW"], [("MT", 3, 16)], scale=0.0)
         if st == 1:
-            consts_out()
+            consts_order(1)
+            blank(T.LX[:, 0:256], 256, ["LX"])
         for q in range(16):
             at, n = 8 * q * (q + 1), 16 * (q + 1)
-            ts(T.GX[:, at:at + n], T.O16[:, 0:n], T.PB[:, q:q + 1], OP.is_equal, ["O16", "PB"], [("GX", at, at + n)], 2.0 ** -8, OP.mult)
+            ts(T.GX[:, at:at + n], T.O16[:, 0:n], T.OF[:, q:q + 1], OP.is_equal, ["O16", "OF"], [("GX", at, at + n)], 2.0 ** -8, OP.mult)
         scan(T.CNT[:], T.D0[:, 0:2176], T.GX[:, 0:2176], 0.0, OP.mult, OP.add, ["D0", "GX"], ["CNT"])
         tt(sm(0), T.CNT[:].indirect(T.EL[:, 0:1]), T.JK[:, 0, :], OP.min, ["CNT", "EL", "JK"], [sn(0)])
-        tt(sm(1), sm(0), T.PB[:, 0:16], OP.max, [sn(0), "PB"], [sn(1)])
+        tt(sm(1), sm(0), T.OF[:], OP.max, [sn(0), "OF"], [sn(1)])
         cp(T.TG[:], sm(1), [sn(1)], ["TG"])
-        act(T[cdn][:], DG_.indirect(T.TG[:]), ["DE", "TG"], [cdn])
-        strew(DG_.indirect(T.TG[:]), T[cd][:], ["TG", cd], ["DE"])
-        cp(XG.indirect(T.TG[:]), T.STL[:], ["TG", "STL"], ["XW"])
-        cp(WG.indirect(T.TG[:]), T.NW[:], ["TG", "NW"], ["W1"])
-        owners_psum()
-        pack_x(st)
-        send(st)
-        mine_x(st)
+        cp(SG.indirect(T.TG[:]), T.NW[:], ["TG", "NW"], ["ST"])
+        send_state(st)
+        mine(T.ST[:, REPL], [SR])
         if st == 0:
-            fill(T.ONF[:], 256, 1, ["ONF"])
-            fill(T.OO[:, C_:1856], 320, 2048, [("OO", C_, 1856)])
-            fill(T.CH[:, H_:V_], NR, 0, [("CH", H_, V_)])
-            fill(T.FLR[:], 1856, 0, ["FLR"])
-            act(T.OF0[:], T.PC[:, 0:256], ["PC"], ["OF0"])
-            act(T.REPF[0:32], T.REP[0:32], ["REP"], ["REPF"])
-            act(T.BWF[:], T.BW[:], ["BW"], ["BWF"], scale=2.0 ** -16)
-            ts(DGP, T.ZV[:], col(0), OP.is_equal, ["ZV", cn(0)], ["PB"])
+            consts_later_g()
         if st == 1:
-            act(T.OO[:, 1152:C_], T.PH[:, 0:384], ["PH"], [("OO", 1152, C_)])
-            fill(T.CH[:, 0:H_], H_, 0, [("CH", 0, H_)])
-            fill(T.CH[:, V_:2304], 256, 0, [("CH", V_, 2304)])
+            x_gap(0)
+            theirs(0, "PH", P_STALE, lambda d: T.LNS[:, 0, d, :], True)
             consts_plan_g()
+        if st == 2:
+            consts_lift_g()
+        if st < 2:
+            ts(sm(3), sm(1), 2047.5, OP.is_lt, [sn(1)], [sn(3)])
+            ts(sm(4), T.OF[:], 2047.5, OP.is_lt, ["OF"], [sn(4)])
+            tt(sm(5), sm(3), pb("PB", 16), OP.mult, [sn(3), "PB"], [sn(5)])
+            tt(sm(4), sm(4), sm(3), OP.subtract, [sn(3), sn(4)], [sn(4)])
         ts(sm(2), sm(1), 2047.5, OP.is_gt, [sn(1)], [sn(2)])
         if st < 2:
-            tt(T.MK[:], T[cdn][:], DGP, OP.mult, [cdn, "PB"], ["MK"])
-            ts(sm(4), T.PB[:, 0:16], 2047.5, OP.is_lt, ["PB"], [sn(4)], BIG, OP.mult)
-            to_list()
+            tt(sm(4), sm(4), T.CO[:, co, :], OP.mult, [sn(4), ("CO", co, co + 1)], [sn(4)])
+        act(sm(6), T.CO[:, co, :], [("CO", co, co + 1)], [sn(6)], bias=float(C_), scale=-1.0)
         tt(sm(2), sm(2), T.JK[:, 1, :], OP.mult, [sn(2), "JK"], [sn(2)])
         if st < 2:
-            tt(sm(5), ENDS, sm(4), OP.min, ["SC", sn(4)], [sn(5)])
-        tt(sm(3), sm(2), T.LNF[:], OP.max, [sn(2), "LNF"], [sn(3)])
+            tt(T.CO[:, cx, :], sm(4), sm(5), OP.add, [sn(4), sn(5)], [("CO", cx, cx + 1)])
+        tt(sm(2), sm(2), sm(6), OP.max, [sn(2), sn(6)], [sn(2)])
         if st < 2:
-            ts(T.LN[:], sm(5), -1.0 / 256, OP.mult, [sn(5)], ["LN"], C_ + 0.25, OP.add)
-        tcs = [(T.TC0[:, 0, :], ("TC0", 0, 1), "OF0"), (T.TC0[:, 1, :], ("TC0", 1, 2), "DF"), (T.TC[:], "TC", "OF")]
-        cp(tcs[st][0], sm(3), [sn(3)], [tcs[st][1]])
-        if st < 2:
-            cp(T.LNF[:], T.LN[:], ["LN"], ["LNF"])
-            lane_lists()
-            sentinels()
+            turn_list(cx)
+            lane_rows()
+            strengths()
+            key_start()
+        cp(T.TC[:], sm(2), [sn(2)], ["TC"])
+        strew(T.CF[:].indirect(T.TC[:]), T.NC[:], ["TC", "NC"], ["CF"])
         if st == 0:
-            cp(T.RL[:], T.RLI[:], ["RLI"], ["RL"])
-        for ls, ln_, of in ([], tcs[0:1], tcs[1:3])[st]:
-            cp(T.OO[:].indirect(ls), T[of][:], [ln_, of], ["OO"])
-            strew(T.FLR[:].indirect(ls), T.ONF[:], [ln_, "ONF"], ["FLR"])
-        if st == 2:
-            ms(T.DE[:, V_:V_ + 8], -1024.0, [("DE", V_, V_ + 8)])
-            consts_plan_v()
-        arrive(st, st == 2)
+            consts_order(0)
+        if st == 1:
+            tt(T.LOSE[:, 0, :], T.LOSE[:, 0, :], pb("PH", NR), OP.is_gt, ["PH", ("LOSE", 0, 1)], [("LOSE", 0, 1)])
+            taken("PG", 0)
         if st < 2:
-            upd_w()
+            lane_fields(cx)
+        if st == 2:
+            act(T.CS[:], T.CF[:], ["CF"], ["CS"], scale=1.0 / 64)
+            cp(T.VH[:], T.VHI[:], ["VHI"], ["VH"])
+            for j, bank in enumerate(("PA", "PC", "PD")):
+                stale_x(512 * j, 512 * j + 512, bank)
+        k = min(st, 1)
+        theirs(st, "PE", P_SCORE, lambda d: T.LNS[:, st, d, :])
+        theirs(st, "PF", P_ST, lambda d: T.LNS[:, st, d, :])
+        lose(k)
+        taken("PF", k)
+        if st < 2:
+            upd_st()
+        if st == 0:
+            dma("s", "vh", [(T.VHI[j % 4::4, j // 4, :], T.va[j::16, 0:768]) for j in range(16)], ["LOSE"], ["VHI"])
+        if st == 1:
+            dma("s", "xv", [(T.XW[:, 0:H_], T.xv[:, 0:H_])], ["LOSE"], [("XW", 0, H_)])
+            dma("s", "kc", [(T.KK[:, 0:C_], T.kc[:])], [], [("KK", 0, C_)])
 
-    def lift(nv, extra, late=None):
+    def lift(nv, kind, start, extra, late=None):
         win = T.CH[:]
-        mm([(T.PH[:, 0:96], mt(M_I), T.FK[:], True, False)] +
-           [(T.PH[:, 0:96], dself(u), T.FLR[:, 96 * u:96 * u + 96], False, False) for u in range(16)],
-           [mn(M_I), "FK", "BWF", "FLR"], ["PH"])
-        full, half = nv // 2, nv % 2
-        ajobs = [(k, 0, 96) for k in range(full + half, 16)]
-        ajobs = ([(full, 48, 96)] if half else []) + ajobs[:-1] + [(15, 0, 48), (15, 48, 96)]
-        vjobs = ([(0, 0, 96)] + ([(full, 0, 48)] if half else []) + [(k, 0, 96) for k in range(1, full - 1)]
-                 + [(full - 1, 48, 96), (full - 1, 0, 48)])
-        na, nj = len(ajobs), len(vjobs)
+        over = 768 - nv
+        cuts, back = [max(over - 64, 0), 64], max(64 - over, 0)
+        ajobs = ([("fold", 0, 0, cuts[0])] if cuts[0] else []) + [("plain", u, back if u == 8 else 0, 96) for u in range(8, 16)]
+        vjobs = [(h, j, cuts[h] if j == 1 else 0, 96) for h in range(2) for j in range(4)][:-1]
 
-        def red(src, name, lo, hi, last):
-            mm([(T.PH[:, lo:hi], dsel(u), src(u), False, last and u == 15) for u in range(16)], ["BW", name], ["PH"])
+        def red(s, form, u, lo, hi, last=False):
+            mm([(pb("PH", hi - lo, lo), pick(kind, u if form == "plain" else 2 * (k // 4) + u), T.GR[:, s, 16 * lo + k:16 * hi:16],
+                 False, last and k == 15) for k in range(16)], ["BW", ("GR", 96 * s + lo, 96 * s + hi)], ["PH"])
 
-        def ajob(n):
-            k, lo, hi = ajobs[n]
-            s = n % 4
-            nm = ("GR", 96 * s + lo, 96 * s + hi)
-            act(T.GR[:, s, 16 * lo:16 * hi], win.indirect(T.RL[:, k, lo:hi]), ["CH", "RL"], [nm])
-            if n < na - 2:
-                red(lambda u: T.GR[:, s, 16 * lo + u:16 * hi:16], nm, lo, hi, False)
+        def ajob(s, form, u, lo, hi):
+            ls = T.VU[:, 96 * (u - 8) + lo:96 * (u - 8) + hi] if form == "plain" else T.VH[:, 1, 96 * u + lo:96 * u + hi]
+            op("a", lambda: a.activation(T.GR[:, s, 16 * lo:16 * hi], win.indirect(ls), AF.Relu), ["CH", "VU", "VH"],
+               [("GR", 96 * s + lo, 96 * s + hi)])
 
-        def vjob(n):
-            k, lo, hi = vjobs[n]
-            dst, nm = T.ACC[:, 16 * lo:16 * hi], ("ACC", 16 * lo, 16 * hi)
-            if n == 0:
-                cp(dst, win.indirect(T.RL[:, k, lo:hi]), ["CH", "RL"], [nm])
-            elif n < nj - 2:
-                tt(dst, win.indirect(T.RL[:, k, lo:hi]), dst, OP.max, ["CH", "RL", nm], [nm])
+        def vjob(h, j, lo, hi, s=None):
+            acc, nm = T.GR[:, 3 + h, 16 * lo:16 * hi], ("GR", 96 * (3 + h) + lo, 96 * (3 + h) + hi)
+            src = win.indirect(T.VH[:, j, 96 * h + lo:96 * h + hi])
+            if j == 0:
+                ts(acc, src, 0.0, OP.max, ["CH", "VH"], [nm])
+            elif s is None:
+                tt(acc, src, acc, OP.max, ["CH", "VH", nm], [nm])
             else:
-                s = (na - nj + n) % 4
-                tt(T.GR[:, s, 16 * lo:16 * hi], win.indirect(T.RL[:, k, lo:hi]), dst, OP.max, ["CH", "RL", nm],
-                   [("GR", 96 * s + lo, 96 * s + hi)])
+                tt(T.GR[:, s, 16 * lo:16 * hi], src, acc, OP.max, ["CH", "VH", nm], [("GR", 96 * s + lo, 96 * s + hi)])
 
+        ends = []
+        for e, at, jobs in (("a", 0, ajobs), ("v", C_ - 2 * nv + 48, vjobs)):
+            for n, job in enumerate(jobs):
+                at += job[3] - job[2]
+                ends.append((at, e, n))
+        ajob(0, *ajobs[0])
+        start()
         extra()
-        for n in range(na - 2):
-            ajob(n)
-        for n in range(nj - 2):
-            vjob(n)
-            if n == 2 and late:
-                late()
-        for e in (2, 1):
-            s = (na - e) % 4
-            ajob(na - e)
-            vjob(nj - e)
-            red(lambda u: T.GR[:, s, u:1536:16], ("GR", 96 * s, 96 * s + 96), 0, 96, e == 1)
+        if back:
+            ts(T.GR[:, 0, 0:16 * back], win.indirect(T.VU[:, 0:back]), 0.0, OP.max, ["CH", "VU"], [("GR", 0, back)])
+        for at, e, n in sorted(ends):
+            if e == "a":
+                if n:
+                    ajob(n % 3, *ajobs[n])
+                red(n % 3, ajobs[n][0], ajobs[n][1], 0, ajobs[n][3])
+                if n == 2 and kind == W_7:
+                    for j, bank in enumerate(("PA", "PC", "PD")):
+                        inputs_only(512 * j, 512 * j + 512, bank, 1)
+            else:
+                h, j, lo, hi = vjobs[n]
+                vjob(h, j, lo, hi)
+                if j == 3:
+                    red(3 + h, "fold", h, lo, hi)
+                if n == 2 and late:
+                    late()
+        s = len(ajobs) % 3
+        ajob(s, "fold", 1, 0, 32)
+        vjob(1, 3, 32, 96, s)
+        red(s, "fold", 1, 0, 96)
+        ajob(3, "fold", 1, 32, 64)
+        vjob(1, 3, 0, 32, 3)
+        red(3, "fold", 1, 0, 64, True)
+
+    def stolen_flags():
+        mm([(pb("PH", 96), pick(W_7, u), T.CS[:, 96 * u:96 * u + 96], u == 0, False) for u in range(16)], ["BW", "CS"], ["PH"])
+
+    def kept_flags():
+        mm([(pb("PH", 96), mt(M_I), T.FK[:], True, False)] +
+           [(pb("PH", 96), pick(W_W, u), T.FLR[:, 96 * u:96 * u + 96], False, False) for u in range(16)],
+           [mn(M_I), "FK", "BW", "FLR"], ["PH"])
 
     def after_steals():
-        mm([(T.PD[:, 0:96], dself(u), T.OO[:, 96 * u:96 * u + 96], u == 0, u == 15) for u in range(16)], ["BWF", "OO"], ["PD"])
-        upd_w()
-        upd_xd()
-        cp(T.VAF[:], T.VA[:], ["VA"], ["VAF"])
+        upd_st()
+        ms(T.VB[:, C_:1544], 0, [("VB", C_, 1544)])
+        stale_x(1536, V_, "PE")
+        for j, bank in enumerate(("PA", "PC", "PD")):
+            inputs_only(512 * j, 512 * j + 512, bank, 0)
+        mm([(pb("PG", 96), pick(W_OUT, u), T.CS[:, 96 * u:96 * u + 96], u == 0, u == 15) for u in range(16)], ["BW", "CS"], ["PG"])
 
     def last_outputs():
-        cp(T.OFF[:], T.PD[:, 0:96], ["PD"], ["OFF"])
+        for j, bank in enumerate(("PA", "PC", "PD")):
+            inputs_only(512 * j, 512 * j + 512, bank, 2)
+        cp(T.OFF[:], pb("PG", 96), ["PG"], ["OFF"])
         cp(T.OFL[:], T.OFF[:], ["OFF"], ["OFL"])
 
     def after_plan():
-        upd_w()
-        upd_xd()
+        lose(1)
+        taken("PG", 1)
+        taken("PF", 1)
+        upd_x()
+        upd_st()
 
     def outputs():
-        upd_w()
-        upd_xd()
-        mm([(T.PD[:, 0:128], dsel(u), T.W1[:, 128 * u:128 * u + 128], u == 0, u == 15) for u in range(16)], ["BW", "W1"], ["PD"])
-        tt(T.GX[:, 0:C_], DG_.indirect(T.OFL[:]), T.CV[:], OP.subtract, ["DE", "OFL", "CV"], ["GX"])
-        mm([(T.PC[:, 0:96], dsel(u), T.GX[:, u:C_:16], u == 0, u == 15) for u in range(16)], ["BW", "GX"], ["PC"])
+        after_plan()
+        mm([(pb("PD", 128), pick(W_W, u), T.ST[:, 128 * u:128 * u + 128], u == 0, u == 15) for u in range(16)], ["BW", "ST"], ["PD"])
         ts(T.GW[:, H_:V_], T.XW[:, REPL], 256.0, OP.min, ["XW"], [("GW", H_, V_)])
         dma("s", "y", [(T.y[:], T.GW[:, 0:V_])], ["GW"], [])
+        cp(T.GX[:, 0:C_], SG.indirect(T.OFL[:]), ["ST", "OFL"], ["GX"])
 
     def outputs_late():
-        ts(T.YWB[:], T.PD[:, 0:128], 2.0 ** -16, OP.mult, ["PD"], ["YWB"], -1.0, OP.add)
+        mm([(pb("PC", 96), pick(W_OWN, u), T.GX[:, u:C_:16], u == 0, u == 15) for u in range(16)], ["BW", "GX"], ["PC"])
+        cp(T.YWB[:], pb("PD", 128), ["PD"], ["YWB"])
         dma("s", "yw", [(T.yw[:], T.YWB[:])], ["YWB"], [])
-        ts(T.YOB[:, 0, :], T.PC[:, 0:96], 2.0 ** -16, OP.mult, ["PC"], ["YOB"])
-        tt(T.YOB[:, 0, :], T.YOB[:, 0, :], T.YOB[:, 0, :], OP.mult, ["YOB"], ["YOB"])
-        ts(T.YOB[:, 0, :], T.YOB[:, 0, :], 16384.0, OP.is_gt, ["YOB"], ["YOB"], 2048.0, OP.mult)
+        tt(T.YOB[:, 0, :], pb("PC", 96), T.CJ[:, 1, :], OP.not_equal, ["PC", "CJ"], ["YOB"])
+        ts(T.YOB[:, 0, :], T.YOB[:, 0, :], 2048.0, OP.mult, ["YOB"], ["YOB"])
         tt(T.YOB[:, 1, :], T.YOB[:, 0, :], T.OFF[:], OP.max, ["YOB", "OFF"], ["YOB"])
         dma("s", "yo", [(T.yo[:], T.YOB[:, 1, :])], ["YOB"], [])
 
-    upd_z()
-    upd_ch()
-    lift(14, after_steals, last_outputs)
+    upd_ch("PF")
+    lift(SHARE[0], W_7, stolen_flags, after_steals, last_outputs)
+
+    def least(lo, hi):
+        scan(T.GX[:, 16 * lo:16 * hi], T.RS4[:, 0:16 * (hi - lo)], T.GW[:, 16 * lo:16 * hi], 0.0, OP.max, OP.min,
+             ["RS4", ("GW", 16 * lo, 16 * hi)], [("GX", 16 * lo, 16 * hi)])
+
+    def sum_mm(lo, hi, last):
+        mm([(pb("PC", hi - lo, lo), mt(M_NI), T.GX[:, 16 * lo + k:16 * hi:16], False, last and k == 15) for k in range(16)],
+           [("GX", 16 * lo, 16 * hi)], ["PC"])
+
+    ENDS = T.SC[:, 15::16]
 
     for t in range(3):
-        m = 3 + t
-        fill(T.FLR[:], 1856, 0, ["FLR"])
-        fill(T.CH[:], 2304, 0, ["CH"])
-        ts(T.FL[:], T.PH[:, 0:96], 0.0, OP.is_gt, ["PH"], ["FL"])
+        fill(T.FLR[:], WC, 0, ["FLR"])
+        fill(T.CH[:], WV, 0, ["CH"])
+        ts(T.FL[:], pb("PH", 96), 0.0, OP.is_gt, ["PH"], ["FL"])
         scan(T.INC[:], T.ONE[:, 0:96], T.FL[:], 0.0, OP.mult, OP.add, ["ONE", "FL"], ["INC"])
         tot, mid = T.INC[:, 95:96], T.INC[:, 47:48]
         if t == 1:
-            mm([(T.PC[:, 0:1], mt(M_LA), tot, True, False), (T.PC[:, 0:1], mt(M_RS), mid, False, True),
-                (T.PC[:, 1:2], mt(M_LB), tot, True, False), (T.PC[:, 1:2], mt(M_RS), mid, False, True)], ["INC", "MT"], ["PC"])
+            mm([(T.PC[:, 0, 0:1], mt(M_LA), tot, True, False), (T.PC[:, 0, 0:1], mt(M_RS), mid, False, True),
+                (T.PC[:, 0, 1:2], mt(M_LB), tot, True, False), (T.PC[:, 0, 1:2], mt(M_RS), mid, False, True)], ["INC", "MT"], ["PC"])
         else:
-            mm([(T.PC[:, 0:1], mt(M_T0 if t == 0 else M_T2), tot, True, True)], ["INC", "MT"], ["PC"])
-        ts(T.NF[:], T.FL[:], -4096.0, OP.mult, ["FL"], ["NF"], 4095.0, OP.add)
-        tt(T.NF[:], T.NF[:], T.INC[:], OP.add, ["NF", "INC"], ["NF"])
-        if t == 1:
-            for hf in range(2):
-                ts(T.RR[:, 0, 48 * hf:48 * hf + 48], T.NF[:, 48 * hf:48 * hf + 48], T.PC[:, hf:hf + 1], OP.add,
-                   ["NF", "PC"], [("RR", 48 * hf, 48 * hf + 48)])
-        else:
-            ts(T.RR[:, 0, :], T.NF[:], T.PC[:, 0:1], OP.add, ["NF", "PC"], [("RR", 0, 96)])
-        tt(T.RR[:, 1, :], T.RR[:, 0, :], T.CJ[:, 0, :], OP.min, [("RR", 0, 96), "CJ"], [("RR", 96, 192)])
-        cp(T.PS[:], T.RR[:, 1, :], [("RR", 96, 192)], ["PS"])
+            mm([(T.PC[:, 0, 0:1], mt(M_T0 if t == 0 else M_T2), tot, True, True)], ["INC", "MT"], ["PC"])
+        ts(pb("PD", 96), pb("PH", 96), 0.0, OP.is_le, ["PH"], ["PD"])
+        tt(pb("PD", 96), pb("PD", 96), T.CJ[:, 2 + t, :], OP.mult, ["PD", "CJ"], ["PD"])
+        tt(T.RR[:], pb("PD", 96), T.INC[:], OP.add, ["PD", "INC"], ["RR"])
+        for lo, hi, hf in (((0, 48, 0), (48, 96, 1)) if t == 1 else ((0, 96, 0),)):
+            ts(T.PS[:, lo:hi], T.RR[:, lo:hi], T.PC[:, 0, hf:hf + 1], OP.add, ["RR", "PC"], [("PS", lo, hi)], -1.0, OP.add)
         strew(T.LX[:].indirect(T.PS[:, 46:96]), T.CV[:, 736:C_], ["PS", "CV"], ["LX"])
         cp(T.LW[:].indirect(T.PS[:, 0:46]), T.CV[:, 0:736], ["PS", "CV"], ["LW"])
         tt(T.MK[:], T.LW[:, 0:256], DGP, OP.mult, ["LW", "PB"], ["MK"])
@@ -655,75 +812,82 @@ def rank_program(g, core, T, topo):
         if t < 2:
             fill(T.LW[:, 0:256], 256, 0, ["LW"])
             fill(T.LX[:, 0:256], 256, 0, ["LX"])
-        cp(T.ROWS[:], T.VA[:].indirect(T.LN[:]), ["VA", "LN"], ["ROWS"])
-        act(T.RK[:], T.VAF[:].indirect(T.LN[:]), ["VAF", "LN"], ["RK"])
-        act(T.OF[:], T.OO[:].indirect(T.LN[:]), ["OO", "LN"], ["OF"])
-        tt(T.MK[:], T.OO[:].indirect(T.LN[:]), T.DGM[:], OP.mult, ["OO", "LN", "DGM"], ["MK"])
-        gath("a", "GW", 32, 96)
-        tt(T.OWN[:], T.RK[:], T.OF[:], OP.is_equal, ["RK", "OF"], ["OWN"])
-        to_list()
-        mm([(T.PA[:, 0:256], mt(M_IB), T.OWN[:], True, False)], ["OWN", "MT"], ["PA"])
-        cp(T.OL[:], ENDS, ["SC"], ["OL"])
-        cp(sm(1), ENDS, ["SC"], [sn(1)])
-        gath("v", "GW", 0, 32)
-        key_mm(0, 96, False)
-        rnd("GW", 96, 152, 192, False)
-        rnd("GW", 192, 224, 256, True)
-        act(T.XO[:], XG.indirect(T.OL[:]), ["XW", "OL"], ["XO"])
+        cp(T.ROWS[:], T.VB[:].indirect(T.LN[:]), ["VB", "LN"], ["ROWS"])
+        act(T.CSG[:], T.CS[:].indirect(T.LN[:]), ["CS", "LN"], ["CSG"])
+        to_psum_list("PH", 0, W_OUT, lambda i: T.CSG[:, i::16], "CSG")
         act(T.KG[:], T.KK[:].indirect(T.LN[:]), ["KK", "LN"], ["KG"])
-        mm([(T.PC[:, 0:256], mt(M_I), T.XO[:], True, False), (T.PC[:, 0:256], mt(M_I), T.KG[:], False, False)],
-           ["XO", "KG", "MT"], ["PC"])
-        rnd("GX", 0, 48, 96, False)
-        tr(T.TT[:], T.PA[:, 0:256], ["PA"], ["TT"])
-        scan(T.P2[:], T.RS0[:], T.TT[:], BIG, OP.add, OP.min, ["RS0", "TT"], ["P2"])
-        tr(T.P2T[:], T.P2[:], ["P2"], ["P2T"])
-        mm([(T.PD[:, 0:256], mt(M_B15), T.P2T[:], True, True)], ["P2T", "MT"], ["PD"])
-        tt(T.MK[:], DG_.indirect(T.OL[:]), T.DGM[:], OP.mult, ["DE", "OL", "DGM"], ["MK"])
-        act(T.SG[:], T.S16[:].indirect(T.LN[:]), ["S16", "LN"], ["SG"], bias=1.0, scale=2.0 ** -16)
-        rnd("GX", 96, 140, 192, False)
-        rnd("GX", 192, 224, 256, True)
-        owners_psum()
-        to_list()
-        tt(T.NW[:], T.PD[:, 0:256], T.SG[:], OP.min, ["PD", "SG"], ["NW"])
-        tt(sm(2), ENDS, sm(0), OP.subtract, ["SC", sn(0)], [sn(2)])
-        tt(sm(2), sm(2), sm(2), OP.mult, [sn(2)], [sn(2)])
-        ts(sm(2), sm(2), 16384.0, OP.is_gt, [sn(2)], [sn(2)])
-        tt(sm(2), sm(2), T.JK[:, 0, :], OP.mult, [sn(2), "JK"], [sn(2)])
-        tt(sm(2), sm(2), sm(1), OP.max, [sn(2), sn(1)], [sn(2)])
-        tt(T.MK[:], T.PC[:, 0:256], T.DGM[:], OP.mult, ["PC", "DGM"], ["MK"])
-        to_list()
-        ts(T.NX[:, 0, :], T.PC[:, 0:256], 65536.0, OP.add, ["PC"], [("NX", 0, 1)])
-        ts(sm(3), ENDS, WAITS, OP.is_lt, ["SC"], [sn(3)])
+        mm([(pb("PC", 256), mt(M_I), T.KG[:], True, False)], ["KG", "MT"], ["PC"])
+        mm([(pb("PE", 256), mt(M_OW), T.CSG[:], True, False)], ["CSG", "MT"], ["PE"])
+        gath("v", "GX", XG, "XW", 0, 40)
+        cp(T.OU[:], pb("PH", 16), ["PH"], ["OU"])
+        gath("a", "GX", XG, "XW", 40, 64)
+        sum_mm(0, 64, False)
+        act(T.EG[:], SG.indirect(T.OU[:]), ["ST", "OU"], ["EG"], scale=-1.0)
+        mm([(pb("PE", 256), mt(M_OW), T.EG[:], False, True)], ["EG", "MT"], ["PE"])
+        gath("v", "GX", XG, "XW", 64, 104)
+        gath("a", "GX", XG, "XW", 104, 128)
+        op("a", lambda: a.activation(T.OWN[:], pb("PE", 256), AF.Abs), ["PE"], ["OWN"])
+        sum_mm(64, 128, False)
+        gath("v", "GX", XG, "XW", 128, 160)
+        gath("a", "GX", XG, "XW", 160, 192)
+        mm([(pb("PC", 256), mt(M_NO), T.OWN[:], False, False)], ["OWN", "MT"], ["PC"])
+        sum_mm(128, 192, False)
+        gath("v", "GX", XG, "XW", 192, 224)
+        gath("a", "GX", XG, "XW", 224, 256)
+        sum_mm(192, 256, True)
+        mm([(pb("PD", 256), T.KM[0:1, 5], T.ONE[0:1, 0:256], True, False)], ["KM", "ONE"], ["PD"])
+        act(T.XO[:], XG.indirect(T.OU[:]), ["XW", "OU"], ["XO"])
+        gath("v", "GW", SG, "ST", 0, 56)
+        gath("a", "GW", SG, "ST", 56, 128)
+        tt(T.MK[:], pb("PC", 256), T.DGM[:], OP.mult, ["PC", "DGM"], ["MK"])
+        scan(T.SC[:], T.M0[:], T.MK[:], 0.0, OP.mult, OP.add, ["M0", "MK"], ["SC"])
+        ts(T.NX[:, 0, :], pb("PC", 256), 65536.0, OP.add, ["PC"], [("NX", 0, 1)])
+        ts(sm(2), ENDS, WAITS, OP.is_lt, ["SC"], [sn(2)])
         ts(T.NX[:, 1, :], T.NX[:, 0, :], 255, OP.bitwise_and, [("NX", 0, 1)], [("NX", 1, 2)])
-        tt(sm(3), sm(3), T.JK[:, 0, :], OP.mult, [sn(3), "JK"], [sn(3)])
-        tt(sm(3), sm(3), sm(2), OP.max, [sn(3), sn(2)], [sn(3)])
+        tt(sm(3), sm(2), T.JK[:, 0, :], OP.mult, [sn(2), "JK"], [sn(3)])
+        gath("a", "GW", SG, "ST", 128, 192)
+        tt(sm(3), sm(3), pb("PH", 16), OP.max, [sn(3), "PH"], [sn(3)])
         cp(T.TG[:], sm(3), [sn(3)], ["TG"])
         cp(XG.indirect(T.TG[:]), T.NX[:, 1, :], ["TG", ("NX", 1, 2)], ["XW"])
-        cp(WG.indirect(T.TG[:]), T.NW[:], ["TG", "NW"], ["W1"])
-        pack_x(m)
-        pack_w(m)
-        send(m)
-        mine_x(m)
+        send_x(1 + t)
+        gath("a", "GW", SG, "ST", 192, 232)
+        least(0, 64)
+        least(64, 128)
+        gath("a", "GW", SG, "ST", 232, 256)
+        least(128, 192)
+        least(192, 232)
+        least(232, 256)
+        mm([(pb("PD", 256), mt(M_B0), T.GX[:, 15::16], False, True)], ["GX", "MT"], ["PD"])
+        tt(T.NW[:], pb("PD", 256), T.CSG[:], OP.min, ["PD", "CSG"], ["NW"])
+        cp(SG.indirect(T.TG[:]), T.NW[:], ["TG", "NW"], ["ST"])
+        send_state(3 + t)
+        mine(T.ST[:, REPL], [SR])
         tt(T.DF[:], T.NX[:, 1, :], T.XO[:], OP.not_equal, [("NX", 1, 2), "XO"], ["DF"])
         strew(T.CH[:].indirect(T.TG[:]), T.DF[:], ["TG", "DF"], ["CH"])
+        act(T.CHB[:], T.CH[:, REPL], [CR], ["CHB"])
+        x_gap(1 + t)
+        mm([(pb("PA", NR), mt(M_N1), T.ST[:, REPL], True, False), (pb("PA", NR), T.ONE[0:1, 0:128], T.TIE[0:1, :], False, False),
+            (pb("PA", NR), mt(M_IB), T.CHB[:], False, False)], [SR, "MT", "CHB"], ["PA"])
         cp(sm(5), T.LN[:], ["LN"], [sn(5)])
-        tt(sm(4), sm(2), sm(3), OP.is_equal, [sn(2), sn(3)], [sn(4)])
-        ts(T.NF[:], T.RR[:, 1, :], 255.5, OP.is_gt, [("RR", 96, 192)], ["NF"])
+        ts(sm(4), ENDS, NO_OUTPUT, OP.is_lt, ["SC"], [sn(4)])
+        ts(T.NF[:], T.PS[:], 255.5, OP.is_gt, ["PS"], ["NF"])
+        tt(sm(4), sm(2), sm(4), OP.is_equal, [sn(2), sn(4)], [sn(4)])
         tt(sm(4), sm(4), T.JK[:, 1, :], OP.mult, [sn(4), "JK"], [sn(4)])
         tt(T.FK[:], T.NF[:], T.FL[:], OP.mult, ["NF", "FL"], ["FK"])
         tt(sm(4), sm(4), sm(5), OP.max, [sn(4), sn(5)], [sn(4)])
         cp(T.TC[:], sm(4), [sn(4)], ["TC"])
-        strew(T.FLR[:].indirect(T.TC[:]), T.ONF[:], ["TC", "ONF"], ["FLR"])
+        cp(T.FLR[:].indirect(T.TC[:]), T.ONE[:, 0:256], ["TC", "ONE"], ["FLR"])
         if t == 2:
             ts(T.GW[:, 0:H_], T.XW[:, 0:H_], 256.0, OP.min, ["XW"], [("GW", 0, H_)])
-        arrive(m, True)
-        upd_z()
-        upd_ch()
+        tt(T.NE[:], pb("PG", NR), T.CH[:, REPL], OP.not_equal, ["PG", CR], ["NE"])
+        for bank, kind in (("PA", P_SCORE), ("PE", P_SCORE), ("PF", P_ST)):
+            theirs(3 + t, bank, kind, lambda d: T.LNS[:, 3 + t, d, :])
+        tt(T.CH[:, REPL], pb("PA", NR), T.NE[:], OP.min, ["PA", "NE"], [CR])
         if t < 2:
-            lift(15, after_plan)
+            lift(SHARE[1 + t], W_ALL, kept_flags, after_plan)
         else:
-            lift(14, outputs, outputs_late)
-    ts(T.YFB[:], T.PH[:, 0:96], 0.0, OP.is_gt, ["PH"], ["YFB"])
+            lift(SHARE[3], W_ALL, kept_flags, outputs, outputs_late)
+    ts(T.YFB[:], pb("PH", 96), 0.0, OP.is_gt, ["PH"], ["YFB"])
     dma("s", "yf", [(T.yf[:], T.YFB[:])], ["YFB"], [])
     for s in count:
         need("g", (s, count[s]))

@@ -4,6 +4,8 @@ from concourse.mybir import AluOpType as OP, ActivationFunctionType as AF
 V_, C_, L_, H_, NR = 2048, 1536, 256, 1712, 336
 WV, WC = 2320, 1808
 DV, DC = 2064, 1552
+NB = 4
+NP = 2
 BIG = float(2 ** 25)
 F, B, I, U = "float32", "bfloat16", "int32", "uint16"
 
@@ -15,11 +17,11 @@ def sb(shape, d):
 SCRATCH = {
     "VA": sb([1544], I), "VHI": sb([4, 192], I), "VH": sb([4, 192], U), "VU": sb([768], U), "VB": sb([1544], I), "RS4": sb([1024], B), "XW": sb([WV], B), "ST": sb([WV + C_], B),
     "W0": sb([V_], B), "CS": sb([WC], B), "FLR": sb([WC], B), "KK": sb([1552], B), "CH": sb([WV], F),
-    "LW": sb([4624], F), "LX": sb([4624], F), "CV": sb([C_], F), "CV2": sb([C_], B),
+    "LW": sb([4688], F), "LX": sb([4688], F), "CV": sb([C_], F), "CV2": sb([C_], B),
     "NLI": sb([16], I), "OVI": sb([96], I), "W32": sb([512], I), "S32": sb([384], I), "S32B": sb([384], B),
     "CI": sb([8], I), "COL": sb([40], F), "EYE": sb([16], F), "GV": sb([128], F), "VV": sb([128], F), "ZV": sb([256], B),
     "Q16": sb([16], F), "JT": sb([2, 16], F), "CJ": sb([5, 96], F), "JK": sb([2, 16], F), "BB": sb([128], B),
-    "BW": sb([6, 144], B), "MT": sb([16, 8, 16], B), "CF": sb([WC], F), "KC": sb([512], B), "KM": sb([7, 8, 16], B), "RU": sb([4, 8, 16], B),
+    "BW": sb([6, 144], B), "MT": sb([17, 8, 16], B), "CF": sb([WC], F), "KC": sb([512], B), "KM": sb([7, 8, 16], B), "RU": sb([4, 8, 16], B),
     "BD": sb([6, 10, 16], B), "PW": sb([4, 15, 16], B), "TM": sb([128], F), "DGM": sb([256], B), "RS0": sb([256], B),
     "RS1": sb([256], B), "M0": sb([256], B), "ONE": sb([272], B), "D0": sb([2192], B), "DG": sb([32], B), "EL": sb([2], U),
     "TIE": sb([NR], B),
@@ -34,16 +36,18 @@ SCRATCH = {
     "FL": sb([96], B), "FK": sb([96], B), "INC": sb([96], B), "NF": sb([96], F), "RR": sb([96], F), "PS": sb([96], U),
     "OWN": sb([256], B), "OR": sb([256], F), "P2": sb([256], B), "P2T": sb([256], B), "XO": sb([256], B), "KG": sb([256], B),
     "NX": sb([2, 256], I), "DF": sb([256], F),
+    "POW": sb([NR], B), "E16": sb([128], B), "HN": sb([21], F), "HW": sb([2, 21], F), "GB": sb([1536 * NB], B),
+    "MI": sb([2, 96 * NB], I), "MS": sb([2, 96 * NB], I), "HB": sb([2, 96 * NB], B),
     "OFF": sb([96], F), "OFL": sb([96], U), "YWB": sb([128], F), "YOB": sb([2, 96], F), "YFB": sb([96], F),
 }
 for _n in "ABCDEFGH":
     SCRATCH["P" + _n] = ("psum", [128, 32, 16] if _n in "CDH" else [128, 512], F)
 DMAS = ["nl", "ovf", "va", "w32", "s32", "xr", "xv", "kc", "vh", "y", "yw", "yo", "yf"]
 SEMAPHORES = ["sv", "sa", "sp", "sg", "ls", "lx"] + ["ar%d" % m for m in range(10)] + ["d_" + n for n in DMAS]
-M_134, M_N1, M_N2, M_I, M_NI, M_IB, M_SB, M_B0, M_OB, M_T0, M_T2, M_LA, M_LB, M_RS, M_OW, M_NO = range(16)
+M_134, M_N1, M_N2, M_I, M_NI, M_IB, M_SB, M_B0, M_OB, M_T0, M_T2, M_LA, M_LB, M_RS, M_OW, M_NO, M_B15 = range(17)
 W_KEY, W_W, W_OWN, W_OUT, W_ALL, W_7 = range(6)
 P_X, P_SCORE, P_ST, P_STALE = range(4)
-SHARE = (704, 736, 736, 688)
+SHARE = (448, 640, 640, 576)
 INF = 10 ** 9
 NO_OUTPUT = -100000.0
 WAITS = -15800.0
@@ -300,13 +304,13 @@ def rank_program(g, core, T, topo):
     iota(T.GV[:], [[1, 8], [0, 16]], 0, 0, ["GV"])
     iota(T.ZV[:], [[0, 16], [1, 16]], 0, 0, ["ZV"])
     iota(T.Q16[:], [[16, 16]], 0, 0, ["Q16"])
-    blank(T.PW[:], 960, ["PW"])
     ms(T.MT[:, 0:3], 0.0, [("MT", 0, 3)])
     for u in range(4):
         mark(T.RU[0:32, u, :, 0:2], ("RU", u, u + 1), [[-4, 8], [0, 2]], -u, 1.0)
         mark(T.RU[0:96, u, :, 8:10], ("RU", u, u + 1), [[-4, 8], [-32, 2]], -u - 32, 1.0)
     mark(T.MT[:, M_134, :, 1], mn(M_134), [[-16, 8]], -1, 1.0)
     mark(T.MT[:, M_134, :, 3:5], mn(M_134), [[-16, 8], [-1, 2]], -3, 1.0)
+    lane_rows()
     owners(0)
     ms(T.BW[:], 0.0, ["BW"])
     ts(T.BB[:], T.GV[:], col(K_G), OP.is_equal, ["GV", cn(K_G)], ["BB"])
@@ -315,10 +319,9 @@ def rank_program(g, core, T, topo):
     ts(col(K_OUT), eye(8), eye(9), OP.add, ["EYE"], [cn(K_OUT)])
     ts(col(K_KEY), eye(0), 65536.0, OP.mult, ["EYE", cn(K_56)], [cn(K_KEY)], col(K_56), OP.add)
     ts(col(K_CS), eye(3), float(C_), OP.mult, ["EYE"], [cn(K_CS)], eye(1), OP.add)
-    lane_rows()
     ts(col(K_CS), col(K_CS), 64.0, OP.mult, [cn(K_CS)], [cn(K_CS)])
     for kind, wc in ((W_W, eye(0)), (W_OWN, col(K_OWN)), (W_OUT, col(K_OUT)), (W_ALL, 1.0), (W_7, eye(7)), (W_KEY, col(K_KEY))):
-        op("v", lambda: v.tensor_scalar(T.BW[:, kind, 15:143:16], T.BB[:, 0::16], wc, None, OP.mult), ["BB", "COL", "EYE", "BW"],
+        op("v", lambda: v.tensor_scalar(T.BW[:, kind, 15:143:16], T.BB[:, 0::16], wc, 8192.0 if kind in (W_ALL, W_7) else 1.0, OP.mult, OP.mult), ["BB", "COL", "EYE", "BW"],
            ["BW" if kind == W_KEY else ("BW", -1, -1)])
 
     peers = [T.cores[rank ^ d] for d in range(1, 8)]
@@ -401,7 +404,7 @@ def rank_program(g, core, T, topo):
             (cp if e == "v" else act)(T[dn][:, 16 * lo:16 * hi], win.indirect(T.ROWS[:, lo:hi]), [wn, "ROWS"], [(dn, 16 * lo, 16 * hi)])
 
     def key_start():
-        mm([(pb("PA", 256), T.KM[0:1, 6], T.ZV[0:1, :], True, False)], ["KM", "ZV"], ["PA"])
+        mm([(pb("PA", 256), T.KM[0:1, 6], T.ZV[0:1, :], True, False)], [("KM", 6, 7), "ZV"], ["PA"])
 
     def key_blocks(lo, hi, last):
         mm([(pb("PA", 256), pick(W_KEY, i), T.GW[:, 256 * i:256 * i + 256], False, last and i == hi - 1) for i in range(lo, hi)],
@@ -421,20 +424,79 @@ def rank_program(g, core, T, topo):
         cp(T.TB[:, :, 3:5], T.R2[:, :, 3:5], [("R2", 3, 5)], [("TB", 3, 5)])
 
     def consts_steal():
-        ms(T.DG[:, 16:32], 0.0, [("DG", 16, 32)])
-        ts(T.DG[:, 0:16], T.EYE[:], float(2 ** 20), OP.mult, ["EYE"], [("DG", 0, 16)], 1.0, OP.max)
         ms(T.TB[:], 0.0, ["TB"])
         ms(T.PQ[:, 0, 0:1], 0.0, ["PQ"])
-        ts(col(K_EL), col(K_I), 8.0, OP.mult, [cn(K_I)], [cn(K_EL)], 24.0, OP.add)
         ts(T.JK[:, 0, :], T.Q16[:], col(K_I), OP.add, ["Q16", cn(K_I)], [("JK", 0, 1)], float(DV), OP.add)
-        ts(T.JK[:, 1, :], T.Q16[:], col(K_I), OP.add, ["Q16", cn(K_I)], [("JK", 1, 2)], float(DC), OP.add)
-        ts(T.EL[:, 0:1], col(K_EL), col(K_I), OP.mult, [cn(K_EL), cn(K_I)], ["EL"], 15.0, OP.add)
+        ts(T.RS0[:], T.ZV[:], 0.0, OP.is_equal, ["ZV"], ["RS0"], BIG, OP.mult)
         ts(T.JT[:, 0, :], T.JK[:, 0, :], -4096.0, OP.add, ["JK"], [("JT", 0, 1)])
         ts(T.JT[:, 1, :], T.JK[:, 0, :], 0.0, OP.add, ["JK"], [("JT", 1, 2)])
-        ts(T.RS0[:], T.ZV[:], 0.0, OP.is_equal, ["ZV"], ["RS0"], BIG, OP.mult)
         ts(T.RS1[:], T.ZV[:], 1.0, OP.is_equal, ["ZV"], ["RS1"], BIG, OP.mult)
+        ms(T.DG[:, 16:32], 0.0, [("DG", 16, 32)])
+        ts(T.DG[:, 0:16], T.EYE[:], float(2 ** 20), OP.mult, ["EYE"], [("DG", 0, 16)], 1.0, OP.max)
+
+    def consts_act():
+        ts(col(K_EL), col(K_I), 8.0, OP.mult, [cn(K_I)], [cn(K_EL)], 24.0, OP.add)
         ts(col(K_BST), eye(2), 4096.0, OP.mult, ["EYE"], [cn(K_BST)], eye(1), OP.add)
         ts(col(K_BCS), eye(7), eye(1), OP.add, ["EYE"], [cn(K_BCS)], 64.0, OP.mult)
+        ts(T.EL[:, 0:1], col(K_EL), col(K_I), OP.mult, [cn(K_EL), cn(K_I)], ["EL"], 15.0, OP.add)
+        ts(T.JK[:, 1, :], T.Q16[:], col(K_I), OP.add, ["Q16", cn(K_I)], [("JK", 1, 2)], float(DC), OP.add)
+
+    def mask_consts():
+        fill(T.POW[0:16], NR, 0, ["POW"])
+        fill(T.E16[0:16], 128, 0, ["E16"])
+        mark(T.E16[0:16], "E16", [[0, 8], [-1, 16]], 0, 1.0)
+        for j in range(21):
+            mark(T.POW[0:16, j::21], "POW", [[-1, 16]], 0, float(4 ** (10 - j) if j < 11 else 2 * 4 ** (20 - j)))
+        fill(T.HN[:], 21, 4, ["HN"])
+        fill(T.HN[:, 11:12], 1, 0, ["HN"])
+
+    def mask_table(part):
+        if part == 0:
+            blank(T.W0[:, 0:1024], 1024, ["W0"])
+            blank(T.W0[:, 1024:H_], H_ - 1024, ["W0"])
+        else:
+            mm([(pb("PG", NR), T.E16[0:16], T.POW[0:16], True, True)], ["E16", "POW"], ["PG"])
+            act(T.W0[:, REPL], pb("PG", NR), ["PG"], ["W0"])
+
+    def mask_gather(n):
+        lo = 48 * n
+        act(T.GB[:, 16 * lo:16 * lo + 768], T.W0[:].indirect(T.VU[:, lo:lo + 48]), ["W0", "VU"], [("GB", n, n + 1)])
+
+    def mask_sum(b):
+        mm([(pb("PG", 96, 96 * b), mt(M_I), T.GB[:, 1536 * b + k:1536 * b + 1536:16], k == 0, k == 15) for k in range(16)],
+           [("GB", 2 * b, 2 * b + 2), mn(M_I)], ["PG"])
+
+    def mask_test(part, nb, kind, bank):
+        n = 96 * nb
+        if part == 0:
+            op("a", lambda: a.activation(T.CHB[:], T.CH[:, REPL], AF.Relu), [CR], ["CHB"])
+            mm([(T[bank][:, 0:21], pick(kind, i), T.CHB[:, 21 * i:21 * i + 21], i == 0, i == 15) for i in range(16)], ["BW", "CHB"], [bank])
+            return
+        if part == 2:
+            mm([(pb("PH", 96), pick(W_ALL, 8 + b), T.HB[:, e, 96 * b:96 * b + 96], False, False) for b in range(nb) for e in range(2)],
+               ["BW", "HB"], ["PH"])
+            return
+        if kind == W_7:
+            cp(T.MI[:, 0, :], pb("PG", n), ["PG"], [("MI", 0, 1)])
+        ts(T.HW[:, 0, :], T[bank][:, 0:21], 0.0, OP.is_gt, [bank], [("HW", 0, 1)])
+        if kind == W_7:
+            ts(T.MI[:, 1, :], T.MI[:, 0, :], 1, OP.arith_shift_right, [("MI", 0, 1)], [("MI", 1, 2)], 0x155555, OP.bitwise_and)
+        scan(T.HW[:, 1, :], T.HN[:], T.HW[:, 0, :], 0.0, OP.mult, OP.add, ["HN", ("HW", 0, 1)], [("HW", 1, 2)])
+        if kind == W_7:
+            ts(T.MI[:, 0, :], T.MI[:, 0, :], 0x155555, OP.bitwise_and, [("MI", 0, 1)], [("MI", 0, 1)])
+        for e, at in ((0, 10), (1, 20)):
+            ts(T.MS[:, e, 0:n], T.MI[:, e, 0:n], T.HW[:, 1, at:at + 1], OP.add, [("MI", e, e + 1), ("HW", 1, 2)], [("MS", e, e + 1)])
+        ts(T.MS[:, :, 0:n], T.MS[:, :, 0:n], 0x2AAAAA, OP.bitwise_and, ["MS"], ["MS"])
+        cp(T.HB[:, :, 0:n], T.MS[:, :, 0:n], ["MS"], ["HB"])
+
+    def early_blocks(part):
+        for b in (range(NP), range(1), range(1, NP))[part]:
+            tile, nm = T.GB[:, 1536 * b:1536 * b + 1536], ("GB", 2 * b, 2 * b + 2)
+            if part == 0:
+                op("a", lambda: a.activation(tile, T.CH[:].indirect(T.VU[:, 96 * b:96 * b + 96]), AF.Relu), ["CH", "VU"], [nm])
+            else:
+                mm([(pb("PH", 96), pick(W_ALL, 8 + b), T.GB[:, 1536 * b + k:1536 * b + 1536:16], b == 0 and k == 0, False) for k in range(16)],
+                   ["BW", nm], ["PH"])
 
     def cs_sources():
         ts(T.S32[32:64, :], T.S32[32:64, :], 4080, OP.bitwise_and, ["S32"], [("S32", 1, 2)])
@@ -462,10 +524,11 @@ def rank_program(g, core, T, topo):
         partner_consts(P_ST, 7, 8, 1, 2, 0)
 
     def consts_later_g():
+        fill(T.CH[:, REPL], NR, 0, [CR])
+        mask_consts()
         partner_consts(P_X, 0, 16, 1, 0, 1)
         mark(mt(M_NI), mn(M_NI), [[-1, 128]], 0, -1.0)
         partner_consts(P_STALE, 0, 16, 1, 2, 0)
-        fill(T.CH[:, REPL], NR, 0, [CR])
         iota(T.RS4[:], [[0, 64], [-256, 16]], 256, 0, ["RS4"])
 
     def consts_plan_g():
@@ -473,6 +536,7 @@ def rank_program(g, core, T, topo):
         mark(mt(M_I), mn(M_I), [[-1, 128]], 0, 1.0)
         mark(mt(M_IB), mn(M_IB), [[-1, 128]], 0, BIG)
         mark(T.MT[:, M_B0, :, 0:2], mn(M_B0), [[-16, 8], [0, 2]], 0, 1.0)
+        mark(T.MT[:, M_B15, :, 0:2], mn(M_B15), [[-16, 8], [0, 2]], -15, 1.0)
         mark(mt(M_OW), mn(M_OW), ROW, -3, 1.0)
         mark(mt(M_OW), mn(M_OW), ROW, -4, 1.0)
         mark(mt(M_NO), mn(M_NO), [[-1, 128]], 0, -131072.0)
@@ -507,7 +571,7 @@ def rank_program(g, core, T, topo):
             return
         act(T.CJ[:, 1, :], T.CJ[:, 0, :], [("CJ", 0, 1)], [("CJ", 1, 2)], bias=float(C_), scale=-1.0)
         for t in range(3):
-            act(T.CJ[:, 2 + t, :], T.CJ[:, 0, :], [("CJ", 0, 1)], [("CJ", 2 + t, 3 + t)], bias=C_ + 1.0 - 720 * t)
+            act(T.CJ[:, 2 + t, :], T.CJ[:, 0, :], [("CJ", 0, 1)], [("CJ", 2 + t, 3 + t)], bias=C_ + 65.0 - 720 * t)
         for j, (t, lo, hi) in enumerate(((1, 0, 48), (1, 48, 96), (2, 0, 96))):
             act(T.CJ[:, 2 + t, lo:hi], T.CJ[:, 2 + t, lo:hi], [("CJ", 2 + t, 3 + t), cn(K_WRAP + j)], [("CJ", 2 + t, 3 + t)], bias=col(K_WRAP + j))
         act(DGP, T.DGM[:], ["DGM"], ["PB"])
@@ -530,7 +594,7 @@ def rank_program(g, core, T, topo):
     rows_consts(0, [(0, 16, 0, 0), (0, 16, 0, 1)])
     send_x(0)
     rows_consts(1, [(0, 2, 0, 2), (3, 5, 1, 3), (5, 7, 1, 0)])
-    consts_meet()
+    fill(T.D0[:], 2192, 1, ["D0"])
     rows_consts(2, [(0, 2, 0, 5), (3, 5, 1, 3), (8, 10, 1, 0)])
     for st in range(3):
         co, cx = st % 2, (st + 1) % 2
@@ -540,6 +604,9 @@ def rank_program(g, core, T, topo):
             key_start()
             for lo, hi in ((0, 4), (4, 8), (8, 11), (11, 14), (14, 16)):
                 gath("a", "GW", T.W0[:], "W0", 16 * lo, 16 * hi)
+                if lo == 14:
+                    blank(T.PW[:], 960, ["PW"])
+                    consts_meet()
                 if lo == 4:
                     for u in range(4):
                         cs_build(u)
@@ -553,7 +620,6 @@ def rank_program(g, core, T, topo):
                     consts_steal()
                 if lo == 4:
                     lane_fields(0)
-            ms(T.D0[:], 1.0, ["D0"])
             for u in range(4):
                 state_build(u, 1)
                 state_build(u, 2)
@@ -570,10 +636,15 @@ def rank_program(g, core, T, topo):
             upd_ch("PF")
             if st == 1:
                 cp(T.VU[:], T.VA[:, 768:C_], ["VA"], ["VU"])
+                strew(T.CF[:].indirect(T.TC[:]), T.NC[:], ["TC", "NC"], ["CF"])
+                mask_table(1)
+                mask_gather(0)
             else:
                 ts(T.NE[:], pb("PG", NR), 0.0, OP.not_equal, ["PG"], ["NE"])
                 upd_x()
                 mm([(pb("PE", NR), pick(W_ALL, 7), T.NE[:], True, True)], ["NE", "BW"], ["PE"])
+                for n in (3, 4, 5):
+                    mask_gather(n)
         scan(T.PQ[:, 0, 1:257], T.RS0[:], pb("PA", 256), BIG, OP.add, OP.min, ["RS0", "PA"], [("PQ", 0, 1)])
         tt(T.ZZ[:], pb("PA", 256), T.PQ[:, 0, 0:256], OP.max, ["PA", ("PQ", 0, 1)], ["ZZ"])
         scan(T.PQ[:, 1, 1:257], T.RS1[:], T.ZZ[:], BIG, OP.add, OP.min, ["RS1", "ZZ"], [("PQ", 1, 2)])
@@ -587,7 +658,12 @@ def rank_program(g, core, T, topo):
         rows_mm("PD", 1)
         if st:
             rows_mm("PH", 2)
+        if st == 2:
+            mask_sum(0)
+            mask_sum(1)
         tt(T.OF[:], T.R2[:, :, 0], T.R2[:, :, 1], OP.add, [("R2", 0, 2)], ["OF"])
+        if st == 0:
+            consts_act()
         if st < 2:
             cp(T.OU[:], T.OF[:], ["OF"], ["OU"])
         else:
@@ -602,10 +678,15 @@ def rank_program(g, core, T, topo):
         if st < 2:
             to_psum_list("PB", 0, W_OWN, lambda i: T.EG[:, i::16], "EG")
         if st == 0:
-            act(T.MT[:, 3:16], T.GW[:, 0:1664], ["GW"], [("MT", 3, 16)], scale=0.0)
+            act(T.MT[:, 3:17], T.GW[:, 0:1792], ["GW"], [("MT", 3, 17)], scale=0.0)
+        act(sm(6), T.CO[:, co, :], [("CO", co, co + 1)], [sn(6)], bias=float(C_), scale=-1.0)
         if st == 1:
             consts_order(1)
             blank(T.LX[:, 0:256], 256, ["LX"])
+            mask_gather(1)
+        if st == 2:
+            mask_gather(6)
+            mask_gather(7)
         for q in range(16):
             at, n = 8 * q * (q + 1), 16 * (q + 1)
             ts(T.GX[:, at:at + n], T.O16[:, 0:n], T.OF[:, q:q + 1], OP.is_equal, ["O16", "OF"], [("GX", at, at + n)], 2.0 ** -8, OP.mult)
@@ -632,7 +713,6 @@ def rank_program(g, core, T, topo):
         ts(sm(2), sm(1), 2047.5, OP.is_gt, [sn(1)], [sn(2)])
         if st < 2:
             tt(sm(4), sm(4), T.CO[:, co, :], OP.mult, [sn(4), ("CO", co, co + 1)], [sn(4)])
-        act(sm(6), T.CO[:, co, :], [("CO", co, co + 1)], [sn(6)], bias=float(C_), scale=-1.0)
         tt(sm(2), sm(2), T.JK[:, 1, :], OP.mult, [sn(2), "JK"], [sn(2)])
         if st < 2:
             tt(T.CO[:, cx, :], sm(4), sm(5), OP.add, [sn(4), sn(5)], [("CO", cx, cx + 1)])
@@ -643,10 +723,13 @@ def rank_program(g, core, T, topo):
             strengths()
             key_start()
         cp(T.TC[:], sm(2), [sn(2)], ["TC"])
-        strew(T.CF[:].indirect(T.TC[:]), T.NC[:], ["TC", "NC"], ["CF"])
         if st == 0:
+            mask_table(0)
             consts_order(0)
+        else:
+            strew(T.CF[:].indirect(T.TC[:]), T.NC[:], ["TC", "NC"], ["CF"])
         if st == 1:
+            mask_gather(2)
             tt(T.LOSE[:, 0, :], T.LOSE[:, 0, :], pb("PH", NR), OP.is_gt, ["PH", ("LOSE", 0, 1)], [("LOSE", 0, 1)])
             taken("PG", 0)
         if st < 2:
@@ -669,19 +752,24 @@ def rank_program(g, core, T, topo):
             dma("s", "xv", [(T.XW[:, 0:H_], T.xv[:, 0:H_])], ["LOSE"], [("XW", 0, H_)])
             dma("s", "kc", [(T.KK[:, 0:C_], T.kc[:])], [], [("KK", 0, C_)])
 
-    def lift(nv, kind, start, extra, late=None):
+    def lift(nv, kind, start, extra, late=None, skip=0):
         win = T.CH[:]
         over = 768 - nv
-        cuts, back = [max(over - 64, 0), 64], max(64 - over, 0)
-        ajobs = ([("fold", 0, 0, cuts[0])] if cuts[0] else []) + [("plain", u, back if u == 8 else 0, 96) for u in range(8, 16)]
-        vjobs = [(h, j, cuts[h] if j == 1 else 0, 96) for h in range(2) for j in range(4)][:-1]
+        left, ajobs, rest = over - 96, [], []
+        for h, j, lo, hi in ((0, 1, 0, 96), (0, 2, 0, 96), (1, 2, 0, 32), (1, 2, 64, 96), (1, 1, 64, 96)):
+            mid = lo + min(hi - lo, left)
+            left -= mid - lo
+            ajobs += [(j, h, lo, mid)] if mid > lo else []
+            rest += [(h, j, mid, hi)] if hi > mid else []
+        ajobs += [("plain", u, 0, 96) for u in range(8 + skip, 16)]
+        vjobs = sorted([(0, 0, 0, 96), (0, 3, 0, 96), (1, 0, 0, 96)] + rest)
 
         def red(s, form, u, lo, hi, last=False):
             mm([(pb("PH", hi - lo, lo), pick(kind, u if form == "plain" else 2 * (k // 4) + u), T.GR[:, s, 16 * lo + k:16 * hi:16],
                  False, last and k == 15) for k in range(16)], ["BW", ("GR", 96 * s + lo, 96 * s + hi)], ["PH"])
 
         def ajob(s, form, u, lo, hi):
-            ls = T.VU[:, 96 * (u - 8) + lo:96 * (u - 8) + hi] if form == "plain" else T.VH[:, 1, 96 * u + lo:96 * u + hi]
+            ls = T.VU[:, 96 * (u - 8) + lo:96 * (u - 8) + hi] if form == "plain" else T.VH[:, form, 96 * u + lo:96 * u + hi]
             op("a", lambda: a.activation(T.GR[:, s, 16 * lo:16 * hi], win.indirect(ls), AF.Relu), ["CH", "VU", "VH"],
                [("GR", 96 * s + lo, 96 * s + hi)])
 
@@ -696,76 +784,89 @@ def rank_program(g, core, T, topo):
                 tt(T.GR[:, s, 16 * lo:16 * hi], src, acc, OP.max, ["CH", "VH", nm], [("GR", 96 * s + lo, 96 * s + hi)])
 
         ends = []
-        for e, at, jobs in (("a", 0, ajobs), ("v", C_ - 2 * nv + 48, vjobs)):
+        for e, at, jobs in (("a", 0, ajobs), ("v", C_ - 96 * skip - 2 * nv + 48, vjobs)):
             for n, job in enumerate(jobs):
                 at += job[3] - job[2]
                 ends.append((at, e, n))
+        bank = "PF" if kind == W_7 else "PA"
+        if kind != W_7:
+            mask_test(0, skip, kind, bank)
         ajob(0, *ajobs[0])
         start()
         extra()
-        if back:
-            ts(T.GR[:, 0, 0:16 * back], win.indirect(T.VU[:, 0:back]), 0.0, OP.max, ["CH", "VU"], [("GR", 0, back)])
+        if kind == W_7:
+            mask_test(0, skip, kind, bank)
+            mm([(pb("PE", 96), pick(W_OUT, u), T.CS[:, 96 * u:96 * u + 96], u == 0, u == 15) for u in range(16)], ["BW", "CS"], ["PE"])
+        else:
+            early_blocks(2)
         for at, e, n in sorted(ends):
             if e == "a":
                 if n:
                     ajob(n % 3, *ajobs[n])
-                red(n % 3, ajobs[n][0], ajobs[n][1], 0, ajobs[n][3])
+                red(n % 3, *ajobs[n])
+                if n == 2 and late is outputs_late:
+                    owners_now()
                 if n == 2 and kind == W_7:
-                    for j, bank in enumerate(("PA", "PC", "PD")):
-                        inputs_only(512 * j, 512 * j + 512, bank, 1)
+                    for j, bk in enumerate(("PA", "PC", "PD")):
+                        inputs_only(512 * j, 512 * j + 512, bk, 1)
             else:
                 h, j, lo, hi = vjobs[n]
                 vjob(h, j, lo, hi)
                 if j == 3:
                     red(3 + h, "fold", h, lo, hi)
-                if n == 2 and late:
+                    mask_test(2, skip, kind, bank)
+                if n == 0:
+                    mask_test(1, skip, kind, bank)
+                if n == (0 if kind == W_7 else 3) and late:
                     late()
-        s = len(ajobs) % 3
-        ajob(s, "fold", 1, 0, 32)
-        vjob(1, 3, 32, 96, s)
-        red(s, "fold", 1, 0, 96)
-        ajob(3, "fold", 1, 32, 64)
-        vjob(1, 3, 0, 32, 3)
-        red(3, "fold", 1, 0, 64, True)
+        for n, (j, la, lv) in enumerate(((1, 32, 64), (1, 0, 32), (2, 32, 0))):
+            s = (len(ajobs) % 3, 3, (len(ajobs) + 1) % 3)[n]
+            ajob(s, j, 1, la, la + 32)
+            vjob(1, 3, lv, lv + 32, s)
+            red(s, "fold", 1, min(la, lv), min(la, lv) + 64, n == 2)
 
     def stolen_flags():
         mm([(pb("PH", 96), pick(W_7, u), T.CS[:, 96 * u:96 * u + 96], u == 0, False) for u in range(16)], ["BW", "CS"], ["PH"])
 
     def kept_flags():
-        mm([(pb("PH", 96), mt(M_I), T.FK[:], True, False)] +
-           [(pb("PH", 96), pick(W_W, u), T.FLR[:, 96 * u:96 * u + 96], False, False) for u in range(16)],
-           [mn(M_I), "FK", "BW", "FLR"], ["PH"])
+        mm([(pb("PH", 96), mt(M_IB), T.FK[:], False, False)] +
+           [(pb("PH", 96), pick(W_7, u), T.FLR[:, 96 * u:96 * u + 96], False, False) for u in range(16)],
+           [mn(M_IB), "FK", "BW", "FLR"], ["PH"])
 
     def after_steals():
         upd_st()
         ms(T.VB[:, C_:1544], 0, [("VB", C_, 1544)])
-        stale_x(1536, V_, "PE")
         for j, bank in enumerate(("PA", "PC", "PD")):
             inputs_only(512 * j, 512 * j + 512, bank, 0)
-        mm([(pb("PG", 96), pick(W_OUT, u), T.CS[:, 96 * u:96 * u + 96], u == 0, u == 15) for u in range(16)], ["BW", "CS"], ["PG"])
+        stale_x(1536, V_, "PE")
+        for b in range(2, NB):
+            mask_sum(b)
 
     def last_outputs():
-        for j, bank in enumerate(("PA", "PC", "PD")):
+        for j, bank in ((1, "PC"), (2, "PD")):
             inputs_only(512 * j, 512 * j + 512, bank, 2)
-        cp(T.OFF[:], pb("PG", 96), ["PG"], ["OFF"])
+        cp(T.OFF[:], pb("PE", 96), ["PE"], ["OFF"])
         cp(T.OFL[:], T.OFF[:], ["OFF"], ["OFL"])
 
     def after_plan():
-        lose(1)
-        taken("PG", 1)
         taken("PF", 1)
+
+    def updates():
         upd_x()
         upd_st()
 
     def outputs():
         after_plan()
+        updates()
         mm([(pb("PD", 128), pick(W_W, u), T.ST[:, 128 * u:128 * u + 128], u == 0, u == 15) for u in range(16)], ["BW", "ST"], ["PD"])
         ts(T.GW[:, H_:V_], T.XW[:, REPL], 256.0, OP.min, ["XW"], [("GW", H_, V_)])
         dma("s", "y", [(T.y[:], T.GW[:, 0:V_])], ["GW"], [])
         cp(T.GX[:, 0:C_], SG.indirect(T.OFL[:]), ["ST", "OFL"], ["GX"])
 
-    def outputs_late():
+    def owners_now():
         mm([(pb("PC", 96), pick(W_OWN, u), T.GX[:, u:C_:16], u == 0, u == 15) for u in range(16)], ["BW", "GX"], ["PC"])
+
+    def outputs_late():
         cp(T.YWB[:], pb("PD", 128), ["PD"], ["YWB"])
         dma("s", "yw", [(T.yw[:], T.YWB[:])], ["YWB"], [])
         tt(T.YOB[:, 0, :], pb("PC", 96), T.CJ[:, 1, :], OP.not_equal, ["PC", "CJ"], ["YOB"])
@@ -774,7 +875,12 @@ def rank_program(g, core, T, topo):
         dma("s", "yo", [(T.yo[:], T.YOB[:, 1, :])], ["YOB"], [])
 
     upd_ch("PF")
-    lift(SHARE[0], W_7, stolen_flags, after_steals, last_outputs)
+    lift(SHARE[0], W_7, stolen_flags, after_steals, last_outputs, NB)
+    inputs_only(0, 512, "PA", 2)
+
+    def key_mm(lo, hi):
+        mm([(pb("PA", hi - lo, lo), pick(W_W, k), T.GW[:, 16 * lo + k:16 * hi:16], k == 0, k == 15) for k in range(16)],
+           ["BW", ("GW", 16 * lo, 16 * hi)], ["PA"])
 
     def least(lo, hi):
         scan(T.GX[:, 16 * lo:16 * hi], T.RS4[:, 0:16 * (hi - lo)], T.GW[:, 16 * lo:16 * hi], 0.0, OP.max, OP.min,
@@ -797,9 +903,8 @@ def rank_program(g, core, T, topo):
                 (T.PC[:, 0, 1:2], mt(M_LB), tot, True, False), (T.PC[:, 0, 1:2], mt(M_RS), mid, False, True)], ["INC", "MT"], ["PC"])
         else:
             mm([(T.PC[:, 0, 0:1], mt(M_T0 if t == 0 else M_T2), tot, True, True)], ["INC", "MT"], ["PC"])
-        ts(pb("PD", 96), pb("PH", 96), 0.0, OP.is_le, ["PH"], ["PD"])
-        tt(pb("PD", 96), pb("PD", 96), T.CJ[:, 2 + t, :], OP.mult, ["PD", "CJ"], ["PD"])
-        tt(T.RR[:], pb("PD", 96), T.INC[:], OP.add, ["PD", "INC"], ["RR"])
+        tt(pb("PD", 96), T.CJ[:, 2 + t, :], pb("PH", 96), OP.subtract, ["PH", "CJ"], ["PD"])
+        tt(T.RR[:], pb("PD", 96), T.INC[:], OP.max, ["PD", "INC"], ["RR"])
         for lo, hi, hf in (((0, 48, 0), (48, 96, 1)) if t == 1 else ((0, 96, 0),)):
             ts(T.PS[:, lo:hi], T.RR[:, lo:hi], T.PC[:, 0, hf:hf + 1], OP.add, ["RR", "PC"], [("PS", lo, hi)], -1.0, OP.add)
         strew(T.LX[:].indirect(T.PS[:, 46:96]), T.CV[:, 736:C_], ["PS", "CV"], ["LX"])
@@ -837,37 +942,44 @@ def rank_program(g, core, T, topo):
         sum_mm(192, 256, True)
         mm([(pb("PD", 256), T.KM[0:1, 5], T.ONE[0:1, 0:256], True, False)], ["KM", "ONE"], ["PD"])
         act(T.XO[:], XG.indirect(T.OU[:]), ["XW", "OU"], ["XO"])
-        gath("v", "GW", SG, "ST", 0, 56)
-        gath("a", "GW", SG, "ST", 56, 128)
+        gath("v", "GW", SG, "ST", 0, 64)
+        key_mm(0, 64)
+        gath("a", "GW", SG, "ST", 64, 128)
         tt(T.MK[:], pb("PC", 256), T.DGM[:], OP.mult, ["PC", "DGM"], ["MK"])
         scan(T.SC[:], T.M0[:], T.MK[:], 0.0, OP.mult, OP.add, ["M0", "MK"], ["SC"])
         ts(T.NX[:, 0, :], pb("PC", 256), 65536.0, OP.add, ["PC"], [("NX", 0, 1)])
         ts(sm(2), ENDS, WAITS, OP.is_lt, ["SC"], [sn(2)])
         ts(T.NX[:, 1, :], T.NX[:, 0, :], 255, OP.bitwise_and, [("NX", 0, 1)], [("NX", 1, 2)])
         tt(sm(3), sm(2), T.JK[:, 0, :], OP.mult, [sn(2), "JK"], [sn(3)])
+        key_mm(64, 128)
         gath("a", "GW", SG, "ST", 128, 192)
+        key_mm(128, 192)
         tt(sm(3), sm(3), pb("PH", 16), OP.max, [sn(3), "PH"], [sn(3)])
         cp(T.TG[:], sm(3), [sn(3)], ["TG"])
         cp(XG.indirect(T.TG[:]), T.NX[:, 1, :], ["TG", ("NX", 1, 2)], ["XW"])
         send_x(1 + t)
-        gath("a", "GW", SG, "ST", 192, 232)
-        least(0, 64)
-        least(64, 128)
-        gath("a", "GW", SG, "ST", 232, 256)
-        least(128, 192)
-        least(192, 232)
-        least(232, 256)
-        mm([(pb("PD", 256), mt(M_B0), T.GX[:, 15::16], False, True)], ["GX", "MT"], ["PD"])
+        gath("a", "GW", SG, "ST", 192, 230)
+        gath("v", "GW", SG, "ST", 230, 256)
+        tt(T.DF[:], T.NX[:, 1, :], T.XO[:], OP.not_equal, [("NX", 1, 2), "XO"], ["DF"])
+        strew(T.CH[:].indirect(T.TG[:]), T.DF[:], ["TG", "DF"], ["CH"])
+        act(T.CHB[:], T.CH[:, REPL], [CR], ["CHB"])
+        early_blocks(0)
+        tr(T.TT[:, 0:192], pb("PA", 192), ["PA"], ["TT"])
+        scan(T.P2[:, 0:192], T.RS0[:, 0:192], T.TT[:, 0:192], BIG, OP.add, OP.min, ["RS0", "TT"], ["P2"])
+        least(230, 256)
+        least(192, 230)
+        tr(T.P2T[:, 0:192], T.P2[:, 0:192], ["P2"], ["P2T"])
+        mm([(pb("PD", 64, 192), mt(M_B0), T.GX[:, 16 * 192 + 15::16], False, False),
+            (pb("PD", 192), mt(M_B15), T.P2T[:, 0:192], False, True)], ["GX", "P2T", "MT"], ["PD"])
+        mm([(pb("PA", NR), T.ONE[0:1, 0:128], T.TIE[0:1, :], True, False), (pb("PA", NR), mt(M_IB), T.CHB[:], False, False)],
+           ["MT", "CHB"], ["PA"])
+        x_gap(1 + t)
         tt(T.NW[:], pb("PD", 256), T.CSG[:], OP.min, ["PD", "CSG"], ["NW"])
         cp(SG.indirect(T.TG[:]), T.NW[:], ["TG", "NW"], ["ST"])
         send_state(3 + t)
         mine(T.ST[:, REPL], [SR])
-        tt(T.DF[:], T.NX[:, 1, :], T.XO[:], OP.not_equal, [("NX", 1, 2), "XO"], ["DF"])
-        strew(T.CH[:].indirect(T.TG[:]), T.DF[:], ["TG", "DF"], ["CH"])
-        act(T.CHB[:], T.CH[:, REPL], [CR], ["CHB"])
-        x_gap(1 + t)
-        mm([(pb("PA", NR), mt(M_N1), T.ST[:, REPL], True, False), (pb("PA", NR), T.ONE[0:1, 0:128], T.TIE[0:1, :], False, False),
-            (pb("PA", NR), mt(M_IB), T.CHB[:], False, False)], [SR, "MT", "CHB"], ["PA"])
+        mm([(pb("PA", NR), mt(M_N1), T.ST[:, REPL], False, False)], [SR, "MT"], ["PA"])
+        early_blocks(1)
         cp(sm(5), T.LN[:], ["LN"], [sn(5)])
         ts(sm(4), ENDS, NO_OUTPUT, OP.is_lt, ["SC"], [sn(4)])
         ts(T.NF[:], T.PS[:], 255.5, OP.is_gt, ["PS"], ["NF"])
@@ -880,13 +992,16 @@ def rank_program(g, core, T, topo):
         if t == 2:
             ts(T.GW[:, 0:H_], T.XW[:, 0:H_], 256.0, OP.min, ["XW"], [("GW", 0, H_)])
         tt(T.NE[:], pb("PG", NR), T.CH[:, REPL], OP.not_equal, ["PG", CR], ["NE"])
-        for bank, kind in (("PA", P_SCORE), ("PE", P_SCORE), ("PF", P_ST)):
+        for bank, kind in (("PE", P_SCORE), ("PA", P_SCORE), ("PF", P_ST)):
             theirs(3 + t, bank, kind, lambda d: T.LNS[:, 3 + t, d, :])
+        lose(1)
+        taken("PG", 1)
         tt(T.CH[:, REPL], pb("PA", NR), T.NE[:], OP.min, ["PA", "NE"], [CR])
         if t < 2:
-            lift(SHARE[1 + t], W_ALL, kept_flags, after_plan)
+            lift(SHARE[1 + t], W_ALL, kept_flags, after_plan, None, NP)
+            updates()
         else:
-            lift(SHARE[3], W_ALL, kept_flags, outputs, outputs_late)
+            lift(SHARE[3], W_ALL, kept_flags, outputs, outputs_late, NP)
     ts(T.YFB[:], pb("PH", 96), 0.0, OP.is_gt, ["PH"], ["YFB"])
     dma("s", "yf", [(T.yf[:], T.YFB[:])], ["YFB"], [])
     for s in count:

from concourse.bass import DstId, RemoteDMATransfer
from concourse.mybir import AluOpType as OP, ActivationFunctionType as AF

V_, C_, L_, H_, NR = 2048, 1536, 256, 1712, 336
WV, WC = 2320, 1808
DV, DC = 2064, 1552
NB = 4
NP = 2
BIG = float(2 ** 25)
F, B, I, U = "float32", "bfloat16", "int32", "uint16"


def sb(shape, d):
    return ("sbuf", [128] + shape, d)


SCRATCH = {
    "VA": sb([1544], I), "VHI": sb([4, 192], I), "VH": sb([4, 192], U), "VU": sb([768], U), "VB": sb([1544], I), "RS4": sb([1024], B), "XW": sb([WV], B), "ST": sb([WV + C_], B),
    "W0": sb([V_], B), "CS": sb([WC], B), "FLR": sb([WC], B), "KK": sb([1552], B), "CH": sb([WV], F),
    "LW": sb([4688], F), "LX": sb([4688], F), "CV": sb([C_], F), "CV2": sb([C_], B),
    "NLI": sb([16], I), "OVI": sb([96], I), "W32": sb([512], I), "S32": sb([384], I), "S32B": sb([384], B),
    "CI": sb([8], I), "COL": sb([40], F), "EYE": sb([16], F), "GV": sb([128], F), "VV": sb([128], F), "ZV": sb([256], B),
    "Q16": sb([16], F), "JT": sb([2, 16], F), "CJ": sb([5, 96], F), "JK": sb([2, 16], F), "BB": sb([128], B),
    "BW": sb([6, 144], B), "MT": sb([17, 8, 16], B), "CF": sb([WC], F), "KC": sb([512], B), "KM": sb([7, 8, 16], B), "RU": sb([4, 8, 16], B),
    "BD": sb([6, 10, 16], B), "PW": sb([4, 15, 16], B), "TM": sb([128], F), "DGM": sb([256], B), "RS0": sb([256], B),
    "RS1": sb([256], B), "M0": sb([256], B), "ONE": sb([272], B), "D0": sb([2192], B), "DG": sb([32], B), "EL": sb([2], U),
    "TIE": sb([NR], B),
    "LN": sb([16], U), "CO": sb([2, 16], F), "TP": sb([32], F), "TQ": sb([32], F), "ROWS": sb([256], U), "CSG": sb([256], B),
    "GW": sb([4096], B), "GX": sb([4096], B), "SENT": sb([2, 16], F), "TT": sb([256], F),
    "PQ": sb([2, 272], F), "ZZ": sb([256], F), "R1": sb([2, 16], I), "R2": sb([16, 6], I), "TB": sb([16, 16], B),
    "TBT": sb([16, 16], B), "O16": sb([256], U), "OF": sb([16], F), "OU": sb([16], U), "EG": sb([256], B),
    "NW": sb([256], B), "NC": sb([256], F), "CNT": sb([2176], B), "SM": sb([12, 16], F), "TG": sb([16], U), "TC": sb([16], U),
    "MK": sb([256], F), "MX": sb([256], F), "SC": sb([256], F), "SD": sb([272], F),
    "LNX": sb([4, 7, 48], B), "LNS": sb([6, 7, 48], B), "CHB": sb([NR], B),
    "LOSE": sb([2, NR], B), "NE": sb([NR], B), "GR": sb([5, 1536], B), "ACC": sb([1024], B),
    "FL": sb([96], B), "FK": sb([96], B), "INC": sb([96], B), "NF": sb([96], F), "RR": sb([96], F), "PS": sb([96], U),
    "OWN": sb([256], B), "OR": sb([256], F), "P2": sb([256], B), "P2T": sb([256], B), "XO": sb([256], B), "KG": sb([256], B),
    "NX": sb([2, 256], I), "DF": sb([256], F),
    "POW": sb([NR], B), "E16": sb([128], B), "HN": sb([21], F), "HW": sb([2, 21], F), "GB": sb([1536 * NB], B),
    "MI": sb([2, 96 * NB], I), "MS": sb([2, 96 * NB], I), "HB": sb([2, 96 * NB], B),
    "OFF": sb([96], F), "OFL": sb([96], U), "YWB": sb([128], F), "YOB": sb([2, 96], F), "YFB": sb([96], F),
}
for _n in "ABCDEFGH":
    SCRATCH["P" + _n] = ("psum", [128, 32, 16] if _n in "CDH" else [128, 512], F)
DMAS = ["nl", "ovf", "va", "w32", "s32", "xr", "xv", "kc", "vh", "y", "yw", "yo", "yf"]
SEMAPHORES = ["sv", "sa", "sp", "sg", "ls", "lx"] + ["ar%d" % m for m in range(10)] + ["d_" + n for n in DMAS]
M_134, M_N1, M_N2, M_I, M_NI, M_IB, M_SB, M_B0, M_OB, M_T0, M_T2, M_LA, M_LB, M_RS, M_OW, M_NO, M_B15 = range(17)
W_KEY, W_W, W_OWN, W_OUT, W_ALL, W_7 = range(6)
P_X, P_SCORE, P_ST, P_STALE = range(4)
SHARE = (448, 640, 640, 576)
INF = 10 ** 9
NO_OUTPUT = -100000.0
WAITS = -15800.0


def rank_program(g, core, T, topo):
    rank = T.rank_of(core)
    if rank is None:
        return
    Q = {"v": g.vector, "a": g.scalar, "p": g.tensor, "g": g, "s": g.sync}
    SEM = {"v": "sv", "a": "sa", "p": "sp", "g": "sg"}
    count = {}
    seen = {e: {} for e in Q}
    log = {}

    def spec(a):
        return (a, 0, INF) if isinstance(a, str) else a

    def need(e, tok):
        s, n = tok
        if seen[e].get(s, 0) < n:
            Q[e].wait_ge(T.sem[s], n)
            seen[e][s] = n

    def order(e, reads, writes):
        toks = {}
        for kind, lst in (("r", reads), ("w", writes)):
            for a in lst:
                name, lo, hi = spec(a)
                ps = SCRATCH[name][0] == "psum"
                for (l2, h2, k2, e2, tok) in log.get(name, []):
                    if ps:
                        hit = e2 != e or (e != "p" and (k2 == "w" or kind == "w"))
                    elif l2 >= hi or lo >= h2:
                        hit = False
                    else:
                        hit = k2 == "w" or kind == "w"
                    if hit:
                        toks[tok[0]] = max(toks.get(tok[0], 0), tok[1])
        for s in toks:
            need(e, (s, toks[s]))

    def note(e, reads, writes, tok):
        for kind, lst in (("r", reads), ("w", writes)):
            for a in lst:
                name, lo, hi = spec(a)
                old = log.get(name, [])
                if SCRATCH[name][0] == "psum":
                    old = [r for r in old if r[3] == e and r[2] == "w" and kind == "r"]
                    lo, hi = 0, INF
                elif kind == "w":
                    old = [r for r in old if not (lo <= r[0] and r[1] <= hi)]
                else:
                    old = [r for r in old if not (r[2] == "r" and r[3] == e and lo <= r[0] and r[1] <= hi)]
                log[name] = old + [(lo, hi, kind, e, tok)]

    def op(e, fns, reads, writes):
        order(e, reads, writes)
        if not isinstance(fns, list):
            fns = [fns]
        s = SEM[e]
        ins = None
        for f in fns:
            ins = f()
        ins.then_inc(T.sem[s], 1)
        count[s] = count.get(s, 0) + 1
        note(e, reads, writes, (s, count[s]))

    def dma(e, name, pairs, reads, writes):
        order(e, reads, writes)
        s = "d_" + name
        for o, i in pairs:
            Q[e].dma_start(o, i).then_inc(T.sem[s], 16)
        count[s] = 16 * len(pairs)
        note("dma" + name, reads, writes, (s, count[s]))

    v, a, pe = g.vector, g.scalar, g.tensor

    def cp(out, in_, r, w):
        op("v", lambda: v.tensor_copy(out, in_), r, w)

    def tt(out, i0, i1, o, r, w):
        op("v", lambda: v.tensor_tensor(out, i0, i1, o), r, w)

    def ts(out, i0, s1, o0, r, w, s2=None, o1=None):
        if s2 is None:
            op("v", lambda: v.tensor_scalar(out, i0, s1, None, o0), r, w)
        else:
            op("v", lambda: v.tensor_scalar(out, i0, s1, s2, o0, o1), r, w)

    def scan(out, d0, d1, init, o0, o1, r, w):
        op("v", lambda: v.tensor_tensor_scan(out, d0, d1, init, o0, o1), r, w)

    def tr(out, in_, r, w):
        op("v", lambda: v.transpose(out, in_), r, w)

    def ms(out, val, w):
        op("v", lambda: v.memset(out, val), [], w)

    def act(out, in_, r, w, bias=0.0, scale=1.0):
        op("a", lambda: a.activation(out, in_, AF.Identity, bias=bias, scale=scale), r, w)

    def strew(out, in_, r, w):
        op("a", lambda: a.activation(out, in_, AF.Silu), r, w)

    def mm(lst, r, w):
        op("p", [(lambda x=x: pe.matmul(*x)) for x in lst], r, w)

    def iota(out, pat, base, cm, w, fl=True):
        if fl:
            op("g", lambda: g.iota(out, pat, base, cm, allow_small_or_imprecise_dtypes=True), [], w)
        else:
            op("g", lambda: g.iota(out, pat, base, cm), [], w)

    def fill(out, n, val, w):
        iota(out, [[0, n]], val, 0, w)

    def sel(out, in_, pat, cmp, val, base, cm, r, w):
        op("g", lambda: g.affine_select(out, in_, pat, cmp, val, base, cm), r, w)

    def mark(view, name, pat, base, val):
        sel(view, view, pat, OP.not_equal, val, base, 1, [name], [name])

    def col(k):
        return T.COL[:, k:k + 1]

    def cn(k):
        return ("COL", k, k + 1)

    def eye(k):
        return T.EYE[:, k:k + 1]

    def mt(k):
        return T.MT[:, k]

    def mn(k):
        return ("MT", k, k + 1)

    def sm(k):
        return T.SM[:, k, :]

    def sn(k):
        return ("SM", k, k + 1)

    def pb(name, n, at=0):
        return T[name][:, at // 16:(at + n) // 16, :] if len(SCRATCH[name][1]) == 3 else T[name][:, at:at + n]

    def pick(kind, u):
        return T.BW[:, kind, 15 - u:143 - u]

    def to_psum_list(bank, at, kind, src, name, first=True, last=True):
        mm([(pb(bank, 16, at), pick(kind, i), src(i), first and i == 0, last and i == 15) for i in range(16)], ["BW", name], [bank])

    XG, SG = T.XW[:, 0:WV], T.ST[:, 0:WV]
    DGP = pb("PB", 256, 256)
    REPL = slice(H_, V_)
    SR, XR, CR = ("ST", H_, V_), ("XW", H_, V_), ("CH", H_, V_)
    ROW = [[-16, 8], [0, 16]]
    (K_I, K_G, K_96, K_P0, K_P1, K_56, K_DEF, K_KEY, K_OWN, K_OUT, K_BST, K_BCS, K_EL, K_CV, K_CS, K_WRAP) = (
        0, 1, 3, 4, 5, 6, 7, 8, 9, 10, 11, 12, 13, 16, 20, 24)

    dma("s", "ovf", [(T.OVI[:], T.ov[:])], [], ["OVI"])
    dma("a", "w32", [(T.W32[0:32, :], T.wv[:])], [], ["W32"])
    dma("s", "nl", [(T.NLI[:], T.nl[:])], [], ["NLI"])
    dma("s", "va", [(T.VA[:, 0:C_], T.va[:])], [], [("VA", 0, C_)])
    dma("s", "xr", [(T.XW[:, REPL], T.xv[:, REPL])], [], [XR])
    dma("s", "s32", [(T.S32[0:32, :], T.sc[:]), (T.S32[32:64, :], T.ov[:]), (T.S32[64:96, :], T.ov[:])], [], ["S32"])

    iota(T.CI[:, 0:1], [[0, 1]], 0, 1, [("CI", 0, 1)], False)
    iota(T.EYE[:], [[1, 16]], 0, 0, ["EYE"])
    need("g", ("sg", count["sg"]))
    iota(T.KC[64:96, :], [[1, 32], [0, 16]], 0, 0, [("KC", 2, 3)])
    need("g", ("sg", count["sg"]))
    iota(T.KC[96:128, :], [[0, 32], [1, 16]], 0, 0, [("KC", 3, 4)])
    need("g", ("sg", count["sg"]))
    iota(T.CJ[:, 0, :], [[1, 96]], 0, 0, [("CJ", 0, 1)])
    ms(T.ACC[:, 0:1024], 0.0, ["ACC"])
    ms(T.KM[:], 0.0, ["KM"])
    ms(T.RU[:], 0.0, ["RU"])

    def blank(out, n, w, val=0.0):
        act(out, T.ACC[:, 0:n], ["ACC"], w, bias=val)

    blank(T.ST[:, 0:1024], 1024, [("ST", 0, 1024)])
    blank(T.ST[:, 1024:V_], 1024, [("ST", 1024, V_)])
    blank(T.BD[:], 960, ["BD"])
    ts(T.CI[:, 1:2], T.CI[:, 0:1], 15, OP.bitwise_and, ["CI"], [("CI", 1, 2)])
    ts(T.CI[:, 2:3], T.CI[:, 0:1], 4, OP.arith_shift_right, [("CI", 0, 1)], [("CI", 2, 3)])
    ts(T.CI[:, 3:4], T.CI[:, 0:1], 4, OP.arith_shift_right, [("CI", 0, 1)], [("CI", 3, 4)], 1, OP.bitwise_and)
    for view, val in ((T.KM[64:65, 5, :, 4], -1.0), (T.KM[96:97, 5, :, 3], -96.0), (T.KM[64:65, 0:4, :, 5], 16.0),
                      (T.KM[96:97, 0:4, :, 6], 1.0), (T.KM[32:33, 0:4, :, 1], -255.0),
                      (T.KM[32:33, 1, :, 5], 512.0), (T.KM[32:33, 2, :, 5], 1024.0), (T.KM[32:33, 3, :, 5], 1536.0),
                      (T.KM[64:65, 4, :, 3], -16.0), (T.KM[96:97, 4, :, 4], -1.0)):
        op("v", lambda: v.memset(view, val), ["KM"], [("KM", -1, -1)])
    cp(T.COL[:, 0:3], T.CI[:, 1:4], ["CI"], [("COL", 0, 3)])
    ms(T.KM[0:1, 6], 4096.0, ["KM"])
    ms(T.KC[32:64, :], 1.0, [("KC", 1, 2)])
    ts(T.EYE[:], T.EYE[:], col(K_I), OP.is_equal, ["EYE", cn(K_I)], ["EYE"])
    ts(col(K_96), col(K_I), 96.0, OP.mult, [cn(K_I)], [cn(K_96)])
    ts(col(K_DEF), eye(1), 256.0, OP.mult, ["EYE"], [cn(K_DEF)])
    ts(col(K_P0), col(2), -1.0, OP.mult, [cn(2)], [cn(K_P0)], 1.0, OP.add)
    ts(col(K_DEF), eye(3), 1440.0, OP.mult, ["EYE", cn(K_DEF)], [cn(K_DEF)], col(K_DEF), OP.add)
    for u in range(4):
        ts(col(K_CV + u), eye(4), 96.0 - 24 * u, OP.mult, ["EYE", cn(K_DEF)], [cn(K_CV + u)], col(K_DEF), OP.add)
    for u in range(4):
        mark(T.KM[0:32, u, :, 0:2], ("KM", u, u + 1), [[-4, 8], [0, 2]], -u, 1.0)
    mm([(pb("PA", 384), T.KM[64:128, 5], T.KC[64:128, 0:384], True, True)], [("KM", 5, 6), ("KC", 2, 4)], ["PA"])
    for u in range(4):
        act(T.CV2[:, 384 * u:384 * u + 384], pb("PA", 384), ["PA", cn(K_CV + u)], [("CV2", u, u + 1)], bias=col(K_CV + u))
    cp(T.KC[0:32, :], T.W32[0:32, :], ["W32"], [("KC", 0, 1)])
    ts(T.CJ[:, 0, :], T.CJ[:, 0, :], col(K_96), OP.add, [("CJ", 0, 1), cn(K_96)], [("CJ", 0, 1)])
    ts(T.NF[:], T.OVI[:], 2047.5, OP.is_gt, ["OVI"], ["NF"])
    ts(T.CJ[:, 1, :], T.CJ[:, 0, :], float(WV), OP.add, [("CJ", 0, 1)], [("CJ", 1, 2)])
    ts(T.CO[:, 0, :], T.NLI[:], -1.0, OP.mult, ["NLI"], [("CO", 0, 1)], float(C_), OP.add)
    tt(T.NF[:], T.NF[:], T.CJ[:, 1, :], OP.mult, ["NF", ("CJ", 1, 2)], ["NF"])
    ms(T.ST[:, V_:V_ + 1], -1.0, [("ST", V_, V_ + 1)])
    ms(T.ST[:, V_ + 1:DV], 255.0, [("ST", V_ + 1, DV)])
    tt(T.NF[:], T.NF[:], T.OVI[:], OP.max, ["NF", "OVI"], ["NF"])
    ms(T.ST[:, DV:WV], 0.0, [("ST", DV, WV)])
    cp(T.PS[:], T.NF[:], ["NF"], ["PS"])
    wb = ["PE", "PF", "PG", "PH"]

    def state_mm(u, last):
        return [(pb(wb[u], 512), T.KM[:, u], T.KC[:], True, last)]

    for u in range(4):
        mm(state_mm(u, True), [("KM", u, u + 1), "KC"], [wb[u]])
        act(T.W0[:, 512 * u:512 * u + 512], pb(wb[u], 512), [wb[u]], [("W0", u, u + 1)])

    def state_build(u, part):
        piece, nm = T.ST[:, 512 * u:512 * u + 512], ("ST", 512 * u, 512 * u + 512)
        if part == 0:
            mm(state_mm(u, False), ["KM", "KC"], [wb[u]])
        if part == 1:
            mm([(pb(wb[u], 512), mt(M_134), piece, False, True)], [mn(M_134), nm], [wb[u]])
        if part == 2:
            op("a", lambda: a.activation(piece, pb(wb[u], 512), AF.Relu), [wb[u]], [nm])

    def turn_list(k):
        ts(T.TP[:, 0:16], T.CO[:, k, :], col(K_P0), OP.mult, [("CO", k, k + 1), cn(K_P0)], [("TP", 0, 1)])
        ts(T.TP[:, 16:32], T.CO[:, k, :], col(2), OP.mult, [("CO", k, k + 1), cn(2)], [("TP", 1, 2)])
        tr(T.TQ[:], T.TP[:], ["TP"], ["TQ"])
        tt(sm(9), T.TQ[:, 0:16], T.TQ[:, 16:32], OP.add, ["TQ"], [sn(9)])
        ts(T.LN[:], sm(9), -1.0, OP.mult, [sn(9)], ["LN"], float(C_), OP.add)

    def owners(u):
        cp(T.ST[:].indirect(T.PS[:, 24 * u:24 * u + 24]), T.CV2[:, 384 * u:384 * u + 384], ["PS", ("CV2", u, u + 1)], ["ST"])

    def lane_rows():
        cp(T.ROWS[:], T.VA[:].indirect(T.LN[:]), ["VA", "LN"], ["ROWS"])

    ms(T.VA[:, C_:1544], 0, [("VA", C_, 1544)])
    turn_list(0)
    iota(T.GV[:], [[1, 8], [0, 16]], 0, 0, ["GV"])
    iota(T.ZV[:], [[0, 16], [1, 16]], 0, 0, ["ZV"])
    iota(T.Q16[:], [[16, 16]], 0, 0, ["Q16"])
    ms(T.MT[:, 0:3], 0.0, [("MT", 0, 3)])
    for u in range(4):
        mark(T.RU[0:32, u, :, 0:2], ("RU", u, u + 1), [[-4, 8], [0, 2]], -u, 1.0)
        mark(T.RU[0:96, u, :, 8:10], ("RU", u, u + 1), [[-4, 8], [-32, 2]], -u - 32, 1.0)
    mark(T.MT[:, M_134, :, 1], mn(M_134), [[-16, 8]], -1, 1.0)
    mark(T.MT[:, M_134, :, 3:5], mn(M_134), [[-16, 8], [-1, 2]], -3, 1.0)
    lane_rows()
    owners(0)
    ms(T.BW[:], 0.0, ["BW"])
    ts(T.BB[:], T.GV[:], col(K_G), OP.is_equal, ["GV", cn(K_G)], ["BB"])
    ts(col(K_56), eye(5), eye(6), OP.add, ["EYE"], [cn(K_56)])
    ts(col(K_OWN), eye(3), eye(4), OP.add, ["EYE"], [cn(K_OWN)])
    ts(col(K_OUT), eye(8), eye(9), OP.add, ["EYE"], [cn(K_OUT)])
    ts(col(K_KEY), eye(0), 65536.0, OP.mult, ["EYE", cn(K_56)], [cn(K_KEY)], col(K_56), OP.add)
    ts(col(K_CS), eye(3), float(C_), OP.mult, ["EYE"], [cn(K_CS)], eye(1), OP.add)
    ts(col(K_CS), col(K_CS), 64.0, OP.mult, [cn(K_CS)], [cn(K_CS)])
    for kind, wc in ((W_W, eye(0)), (W_OWN, col(K_OWN)), (W_OUT, col(K_OUT)), (W_ALL, 1.0), (W_7, eye(7)), (W_KEY, col(K_KEY))):
        op("v", lambda: v.tensor_scalar(T.BW[:, kind, 15:143:16], T.BB[:, 0::16], wc, 8192.0 if kind in (W_ALL, W_7) else 1.0, OP.mult, OP.mult), ["BB", "COL", "EYE", "BW"],
           ["BW" if kind == W_KEY else ("BW", -1, -1)])

    peers = [T.cores[rank ^ d] for d in range(1, 8)]
    eng = topo.engines(core, peers[0])
    far = [p for p in peers if topo.die(p) != topo.die(core)]
    near = [p for p in peers if topo.die(p) == topo.die(core)]
    masks = {}
    pool = eng[0::2] + eng[1::2]
    per = 2
    for k, p in enumerate(far + near):
        masks[p] = sum(1 << e for e in pool[per * k:per * k + per])

    def send(m, src, dst, reads):
        order("g", reads, [])
        trs = []
        for d in range(7):
            rid, pid, _ = topo.addr(peers[d])
            trs.append(RemoteDMATransfer(dst_ids=[DstId(rid=rid, pnc=pid)], dma_engine_mask=masks[peers[d]],
                                         remote_sem=T.sem["ar%d" % m], src=src(d), dst=dst(d)))
        ls = "ls" if m < 6 else "lx"
        g.remote_dma_fused(trs, local_sem=T.sem[ls])
        count[ls] = count.get(ls, 0) + 7 * per
        note("remote", reads, [], (ls, count[ls]))

    def mine(src, reads):
        mm([(pb("PE", NR), mt(M_N1), src, True, False), (pb("PE", NR), T.ONE[0:1, 0:128], T.TIE[0:1, :], False, False)],
           reads + [mn(M_N1), "ONE", "TIE"], ["PE"])
        mm([(pb("PF", NR), mt(M_N2), src, True, False)], reads + [mn(M_N2)], ["PF"])

    def theirs(m, bank, kind, land, first=False):
        need("p", ("ar%d" % m, 7 * per))
        mm([(pb(bank, 48, 48 * d), T.PW[:, kind, 6 - d:14 - d, :], land(d), first and d == 0, d == 6) for d in range(7)],
           [("PW", kind, kind + 1)], [bank])

    def lose(k):
        ts(T.LOSE[:, k, :], pb("PE", NR), 0.0, OP.is_gt, ["PE"], [("LOSE", k, k + 1)])

    def taken(bank, k):
        tt(pb(bank, NR), pb(bank, NR), T.LOSE[:, k, :], OP.mult, [bank, ("LOSE", k, k + 1)], [bank])

    def upd_st():
        tt(T.ST[:, REPL], T.ST[:, REPL], pb("PF", NR), OP.add, ["PF", SR], [SR])

    def upd_x():
        tt(T.XW[:, REPL], T.XW[:, REPL], pb("PG", NR), OP.add, ["PG", XR], [XR])

    def upd_ch(bank):
        tt(T.CH[:, REPL], pb(bank, NR), T.CH[:, REPL], OP.not_equal, [bank, CR], [CR])

    def rows_consts(k, spec_):
        for qp in range(2):
            for lo, hi, step, s in spec_:
                mark(T.BD[:, 2 * k + qp, 1 + qp:9:2, lo:hi], ("BD", 2 * k + qp, 2 * k + qp + 1), [[-32, 4], [-step, hi - lo]], -16 * qp - s, 1.0)

    def rows_mm(bank, k):
        lst = []
        for qp in range(2):
            for gp in range(2):
                at = 1 + qp - gp
                lst.append((T[bank][:, qp:16:2, :], T.BD[:, 2 * k + qp, at:at + 8, :], T.TBT[:, gp::2, :], gp == 0, gp == 1))
        mm(lst, ["TBT", ("BD", 2 * k, 2 * k + 2)], [bank])

    def partner_consts(kind, lo, hi, step, s, src_step):
        for base in (-112, -240):
            mark(T.PW[:, kind, :, lo:hi:step], ("PW", kind, kind + 1), [[16, 15], [-src_step, len(range(lo, hi, step))]], base - s, 1.0)

    def send_x(m):
        send(6 + m, lambda d: T.XW[:, H_ + 48 * d:H_ + 48 * d + 48], lambda d: T.LNX[:, m, d, :], [XR])

    def send_state(m):
        send(m, lambda d: T.ST[:, H_ + 48 * d:H_ + 48 * d + 48], lambda d: T.LNS[:, m, d, :], [SR])

    def x_gap(m):
        mm([(pb("PG", NR), mt(M_NI), T.XW[:, REPL], True, False)], [XR, mn(M_NI)], ["PG"])
        theirs(6 + m, "PG", P_X, lambda d: T.LNX[:, m, d, :])


    def gath(e, dn, win, wn, lo, hi):
        if hi > lo:
            (cp if e == "v" else act)(T[dn][:, 16 * lo:16 * hi], win.indirect(T.ROWS[:, lo:hi]), [wn, "ROWS"], [(dn, 16 * lo, 16 * hi)])

    def key_start():
        mm([(pb("PA", 256), T.KM[0:1, 6], T.ZV[0:1, :], True, False)], [("KM", 6, 7), "ZV"], ["PA"])

    def key_blocks(lo, hi, last):
        mm([(pb("PA", 256), pick(W_KEY, i), T.GW[:, 256 * i:256 * i + 256], False, last and i == hi - 1) for i in range(lo, hi)],
           ["BW", ("GW", 256 * lo, 256 * hi)], ["PA"])

    def strengths():
        act(T.CSG[:], T.CF[:].indirect(T.LN[:]), ["CF", "LN"], ["CSG"], scale=1.0 / 64)
        to_psum_list("PB", 16, W_KEY, lambda i: T.CSG[:, 16 * i:16 * i + 16], "CSG")

    def lane_fields(k):
        cp(T.R2[:, :, 5], T.CO[:, k, :], [("CO", k, k + 1)], [("R2", 5, 6)])
        for f in range(2):
            tt(T.SENT[:, f, :], pb("PB", 16, 16), T.JT[:, f, :], OP.add, ["PB", "JT"], [("SENT", f, f + 1)])
        ts(T.R2[:, :, 3], T.R2[:, :, 5], 4080, OP.bitwise_and, [("R2", 5, 6)], [("R2", 3, 4)])
        ts(T.R2[:, :, 4], T.R2[:, :, 5], 15, OP.bitwise_and, [("R2", 5, 6)], [("R2", 4, 5)])
        ts(T.TB[:, :, 5], pb("PB", 16, 16), 2.0 ** -16, OP.mult, ["PB"], [("TB", 5, 6)])
        cp(T.TB[:, :, 3:5], T.R2[:, :, 3:5], [("R2", 3, 5)], [("TB", 3, 5)])

    def consts_steal():
        ms(T.TB[:], 0.0, ["TB"])
        ms(T.PQ[:, 0, 0:1], 0.0, ["PQ"])
        ts(T.JK[:, 0, :], T.Q16[:], col(K_I), OP.add, ["Q16", cn(K_I)], [("JK", 0, 1)], float(DV), OP.add)
        ts(T.RS0[:], T.ZV[:], 0.0, OP.is_equal, ["ZV"], ["RS0"], BIG, OP.mult)
        ts(T.JT[:, 0, :], T.JK[:, 0, :], -4096.0, OP.add, ["JK"], [("JT", 0, 1)])
        ts(T.JT[:, 1, :], T.JK[:, 0, :], 0.0, OP.add, ["JK"], [("JT", 1, 2)])
        ts(T.RS1[:], T.ZV[:], 1.0, OP.is_equal, ["ZV"], ["RS1"], BIG, OP.mult)
        ms(T.DG[:, 16:32], 0.0, [("DG", 16, 32)])
        ts(T.DG[:, 0:16], T.EYE[:], float(2 ** 20), OP.mult, ["EYE"], [("DG", 0, 16)], 1.0, OP.max)

    def consts_act():
        ts(col(K_EL), col(K_I), 8.0, OP.mult, [cn(K_I)], [cn(K_EL)], 24.0, OP.add)
        ts(col(K_BST), eye(2), 4096.0, OP.mult, ["EYE"], [cn(K_BST)], eye(1), OP.add)
        ts(col(K_BCS), eye(7), eye(1), OP.add, ["EYE"], [cn(K_BCS)], 64.0, OP.mult)
        ts(T.EL[:, 0:1], col(K_EL), col(K_I), OP.mult, [cn(K_EL), cn(K_I)], ["EL"], 15.0, OP.add)
        ts(T.JK[:, 1, :], T.Q16[:], col(K_I), OP.add, ["Q16", cn(K_I)], [("JK", 1, 2)], float(DC), OP.add)

    def mask_consts():
        fill(T.POW[0:16], NR, 0, ["POW"])
        fill(T.E16[0:16], 128, 0, ["E16"])
        mark(T.E16[0:16], "E16", [[0, 8], [-1, 16]], 0, 1.0)
        for j in range(21):
            mark(T.POW[0:16, j::21], "POW", [[-1, 16]], 0, float(4 ** (10 - j) if j < 11 else 2 * 4 ** (20 - j)))
        fill(T.HN[:], 21, 4, ["HN"])
        fill(T.HN[:, 11:12], 1, 0, ["HN"])

    def mask_table(part):
        if part == 0:
            blank(T.W0[:, 0:1024], 1024, ["W0"])
            blank(T.W0[:, 1024:H_], H_ - 1024, ["W0"])
        else:
            mm([(pb("PG", NR), T.E16[0:16], T.POW[0:16], True, True)], ["E16", "POW"], ["PG"])
            act(T.W0[:, REPL], pb("PG", NR), ["PG"], ["W0"])

    def mask_gather(n):
        lo = 48 * n
        act(T.GB[:, 16 * lo:16 * lo + 768], T.W0[:].indirect(T.VU[:, lo:lo + 48]), ["W0", "VU"], [("GB", n, n + 1)])

    def mask_sum(b):
        mm([(pb("PG", 96, 96 * b), mt(M_I), T.GB[:, 1536 * b + k:1536 * b + 1536:16], k == 0, k == 15) for k in range(16)],
           [("GB", 2 * b, 2 * b + 2), mn(M_I)], ["PG"])

    def mask_test(part, nb, kind, bank):
        n = 96 * nb
        if part == 0:
            op("a", lambda: a.activation(T.CHB[:], T.CH[:, REPL], AF.Relu), [CR], ["CHB"])
            mm([(T[bank][:, 0:21], pick(kind, i), T.CHB[:, 21 * i:21 * i + 21], i == 0, i == 15) for i in range(16)], ["BW", "CHB"], [bank])
            return
        if part == 2:
            mm([(pb("PH", 96), pick(W_ALL, 8 + b), T.HB[:, e, 96 * b:96 * b + 96], False, False) for b in range(nb) for e in range(2)],
               ["BW", "HB"], ["PH"])
            return
        if kind == W_7:
            cp(T.MI[:, 0, :], pb("PG", n), ["PG"], [("MI", 0, 1)])
        ts(T.HW[:, 0, :], T[bank][:, 0:21], 0.0, OP.is_gt, [bank], [("HW", 0, 1)])
        if kind == W_7:
            ts(T.MI[:, 1, :], T.MI[:, 0, :], 1, OP.arith_shift_right, [("MI", 0, 1)], [("MI", 1, 2)], 0x155555, OP.bitwise_and)
        scan(T.HW[:, 1, :], T.HN[:], T.HW[:, 0, :], 0.0, OP.mult, OP.add, ["HN", ("HW", 0, 1)], [("HW", 1, 2)])
        if kind == W_7:
            ts(T.MI[:, 0, :], T.MI[:, 0, :], 0x155555, OP.bitwise_and, [("MI", 0, 1)], [("MI", 0, 1)])
        for e, at in ((0, 10), (1, 20)):
            ts(T.MS[:, e, 0:n], T.MI[:, e, 0:n], T.HW[:, 1, at:at + 1], OP.add, [("MI", e, e + 1), ("HW", 1, 2)], [("MS", e, e + 1)])
        ts(T.MS[:, :, 0:n], T.MS[:, :, 0:n], 0x2AAAAA, OP.bitwise_and, ["MS"], ["MS"])
        cp(T.HB[:, :, 0:n], T.MS[:, :, 0:n], ["MS"], ["HB"])

    def early_blocks(part):
        for b in (range(NP), range(1), range(1, NP))[part]:
            tile, nm = T.GB[:, 1536 * b:1536 * b + 1536], ("GB", 2 * b, 2 * b + 2)
            if part == 0:
                op("a", lambda: a.activation(tile, T.CH[:].indirect(T.VU[:, 96 * b:96 * b + 96]), AF.Relu), ["CH", "VU"], [nm])
            else:
                mm([(pb("PH", 96), pick(W_ALL, 8 + b), T.GB[:, 1536 * b + k:1536 * b + 1536:16], b == 0 and k == 0, False) for k in range(16)],
                   ["BW", nm], ["PH"])

    def cs_sources():
        ts(T.S32[32:64, :], T.S32[32:64, :], 4080, OP.bitwise_and, ["S32"], [("S32", 1, 2)])
        ts(T.S32[64:96, :], T.S32[64:96, :], 15, OP.bitwise_and, [("S32", 2, 3)], [("S32", 2, 3)])
        for u in range(1, 4):
            ts(col(K_CS + u), eye(3), -384.0 * 64 * u, OP.mult, ["EYE", cn(K_CS)], [cn(K_CS + u)], col(K_CS), OP.add)
        cp(T.S32B[0:96, :], T.S32[0:96, :], ["S32"], ["S32B"])
        ms(T.ONE[:], 1.0, ["ONE"])
        for lo, hi in ((1, 2), (2, 4), (4, 8)):
            ms(T.TIE[0:1, 48 * (lo - 1):48 * (hi - 1)], 0.5 if rank > (rank ^ lo) else -0.5, [("TIE", lo, hi)])
        ts(T.CF[:, C_:WC], T.ONE[:], eye(8), OP.mult, ["ONE", "EYE"], [("CF", C_, WC)], 2048.0 * 64, OP.mult)

    def cs_build(u):
        bk = ["PB", "PC", "PD", "PC"][u]
        mm([(pb(bk, 384), T.RU[0:96, u], T.S32B[0:96, :], True, False),
            (pb(bk, 384), T.KM[64:128, 4], T.KC[64:128, 0:384], False, True)], ["RU", "S32B", "KM", "KC"], [bk])
        act(T.CF[:, 384 * u:384 * u + 384], pb(bk, 384), [bk, cn(K_CS + u)], [("CF", 384 * u, 384 * u + 384)], bias=col(K_CS + u), scale=64.0)

    def consts_meet():
        mark(mt(M_N1), mn(M_N1), ROW, -1, -1.0)
        mark(T.MT[:, M_N2, :, 0:5], mn(M_N2), [[-16, 8], [-1, 5]], 0, -1.0)
        mark(T.MT[:, M_N2, :, 7], mn(M_N2), [[-16, 8]], -2, -1.0)
        partner_consts(P_SCORE, 0, 16, 1, 1, 0)
        partner_consts(P_ST, 0, 3, 2, 0, 2)
        partner_consts(P_ST, 7, 8, 1, 2, 0)

    def consts_later_g():
        fill(T.CH[:, REPL], NR, 0, [CR])
        mask_consts()
        partner_consts(P_X, 0, 16, 1, 0, 1)
        mark(mt(M_NI), mn(M_NI), [[-1, 128]], 0, -1.0)
        partner_consts(P_STALE, 0, 16, 1, 2, 0)
        iota(T.RS4[:], [[0, 64], [-256, 16]], 256, 0, ["RS4"])

    def consts_plan_g():
        mark(mt(M_SB), mn(M_SB), ROW, -2, 1.0)
        mark(mt(M_I), mn(M_I), [[-1, 128]], 0, 1.0)
        mark(mt(M_IB), mn(M_IB), [[-1, 128]], 0, BIG)
        mark(T.MT[:, M_B0, :, 0:2], mn(M_B0), [[-16, 8], [0, 2]], 0, 1.0)
        mark(T.MT[:, M_B15, :, 0:2], mn(M_B15), [[-16, 8], [0, 2]], -15, 1.0)
        mark(mt(M_OW), mn(M_OW), ROW, -3, 1.0)
        mark(mt(M_OW), mn(M_OW), ROW, -4, 1.0)
        mark(mt(M_NO), mn(M_NO), [[-1, 128]], 0, -131072.0)
        mark(mt(M_OB), mn(M_OB), ROW, -8, 1.0)
        mark(mt(M_OB), mn(M_OB), ROW, -9, 1.0)
        mark(mt(M_RS), mn(M_RS), ROW, -7, -1.0)
        sel(mt(M_T0), T.BB[:], [[1, 128]], OP.is_gt, 0.0, 0, -1, ["BB"], [mn(M_T0)])
        sel(mt(M_T2), mt(M_T0), ROW, OP.not_equal, 1.0, -15, 1, [mn(M_T0)], [mn(M_T2)])
        sel(mt(M_T2), mt(M_T2), [[0, 8], [1, 16]], OP.not_equal, 0.0, -15, 0, [mn(M_T2)], [mn(M_T2)])
        fill(T.CH[:, 0:H_], H_, 0, [("CH", 0, H_)])
        fill(T.CH[:, V_:WV], WV - V_, 0, [("CH", V_, WV)])

    def consts_lift_g():
        fill(T.KK[:, C_:1552], 16, 0, [("KK", C_, 1552)])
        fill(T.SD[:, 0:16], 16, 0, [("SD", 0, 16)])
        fill(T.LW[:, 0:256], 256, 0, ["LW"])
        fill(T.XW[:, V_:WV], WV - V_, 0, [("XW", V_, WV)])
        iota(T.CV[:], [[-256, 96], [-24576, 16]], 256 * C_, 0, ["CV"])
        for k, s in ((M_LA, 8), (M_LB, 7)):
            sel(T.MT[:, k, :, s:16], T.MT[:, M_T0, :, s:16], [[-16, 8], [0, 16 - s]], OP.is_ge, 0.0, -7, 1, [mn(M_T0)], [mn(k)])
            sel(T.MT[:, k, :, 0:s], T.MT[:, M_T0, :, 0:s], [[16, 8], [0, s]], OP.is_gt, 1.0, 7, -1, [mn(M_T0)], [mn(k)])
            sel(T.MT[:, k, :, 0:s], T.MT[:, k, :, 0:s], [[16, 8], [0, s]], OP.is_ge, 0.0, 15, -1, [mn(k)], [mn(k)])

    def consts_order(part):
        if part == 0:
            for j, s in enumerate((8.0, 7.0, 15.0)):
                ts(col(K_WRAP + j), col(K_I), s, OP.is_lt, [cn(K_I)], [cn(K_WRAP + j)], float(C_), OP.mult)
            ms(T.KM[0:1, 5], BIG, [("KM", 5, 6)])
            ts(T.DGM[:], T.ZV[:], col(K_I), OP.is_equal, ["ZV", cn(K_I)], ["DGM"])
            ms(T.KM[0:1, 5, :, 0], 0.0, [("KM", 5, 6)])
            ms(T.KM[0:1, 5, :, 1], 1.0, [("KM", 5, 6)])
            return
        act(T.CJ[:, 1, :], T.CJ[:, 0, :], [("CJ", 0, 1)], [("CJ", 1, 2)], bias=float(C_), scale=-1.0)
        for t in range(3):
            act(T.CJ[:, 2 + t, :], T.CJ[:, 0, :], [("CJ", 0, 1)], [("CJ", 2 + t, 3 + t)], bias=C_ + 65.0 - 720 * t)
        for j, (t, lo, hi) in enumerate(((1, 0, 48), (1, 48, 96), (2, 0, 96))):
            act(T.CJ[:, 2 + t, lo:hi], T.CJ[:, 2 + t, lo:hi], [("CJ", 2 + t, 3 + t), cn(K_WRAP + j)], [("CJ", 2 + t, 3 + t)], bias=col(K_WRAP + j))
        act(DGP, T.DGM[:], ["DGM"], ["PB"])
        op("a", lambda: a.activation(T.M0[:], T.ZV[:], AF.Sign), ["ZV"], ["M0"])

    def inputs_only(lo, hi, bank, part):
        n = hi - lo
        if part == 0:
            mm([(pb(bank, n), mt(M_OB), T.CS[:, lo:hi], True, True)], ["CS", mn(M_OB)], [bank])
            tt(pb(bank, n), T.VA[:, lo:hi], pb(bank, n), OP.is_equal, ["VA", bank], [bank])
        elif part == 1:
            act(pb(bank, n), pb(bank, n), [bank], [bank], scale=V_ + 1.0)
        else:
            tt(T.VB[:, lo:hi], T.VA[:, lo:hi], pb(bank, n), OP.max, ["VA", bank], [("VB", lo, hi)])

    def stale_x(lo, hi, bank):
        mm([(pb(bank, hi - lo), mt(M_SB), T.ST[:, lo:hi], True, True)], [("ST", lo, hi), mn(M_SB)], [bank])
        tt(T.XW[:, lo:hi], T.XW[:, lo:hi], pb(bank, hi - lo), OP.max, [bank, ("XW", lo, hi)], [("XW", lo, hi)])

    rows_consts(0, [(0, 16, 0, 0), (0, 16, 0, 1)])
    send_x(0)
    rows_consts(1, [(0, 2, 0, 2), (3, 5, 1, 3), (5, 7, 1, 0)])
    fill(T.D0[:], 2192, 1, ["D0"])
    rows_consts(2, [(0, 2, 0, 5), (3, 5, 1, 3), (8, 10, 1, 0)])
    for st in range(3):
        co, cx = st % 2, (st + 1) % 2
        if st == 0:
            for u in range(4):
                state_build(u, 0)
            key_start()
            for lo, hi in ((0, 4), (4, 8), (8, 11), (11, 14), (14, 16)):
                gath("a", "GW", T.W0[:], "W0", 16 * lo, 16 * hi)
                if lo == 14:
                    blank(T.PW[:], 960, ["PW"])
                    consts_meet()
                if lo == 4:
                    for u in range(4):
                        cs_build(u)
                    strengths()
                key_blocks(lo, hi, hi == 16)
                if lo == 0:
                    cs_sources()
                    owners(1)
                    owners(2)
                    owners(3)
                    consts_steal()
                if lo == 4:
                    lane_fields(0)
            for u in range(4):
                state_build(u, 1)
                state_build(u, 2)
            for q in range(16):
                at = 8 * q * (q + 1) + 16 * q
                act(T.D0[:, at:at + 17], T.DG[:, 0:17], ["DG"], [("D0", at, at + 17)])
        else:
            for lo, mid, hi in ((0, 1, 2), (2, 4, 6), (6, 8, 11), (11, 13, 15), (15, 15, 16)):
                gath("v", "GW", SG, "ST", 16 * lo, 16 * mid)
                gath("a", "GW", SG, "ST", 16 * mid, 16 * hi)
                if mid > lo:
                    key_blocks(lo, mid, False)
                key_blocks(mid, hi, hi == 16)
            upd_ch("PF")
            if st == 1:
                cp(T.VU[:], T.VA[:, 768:C_], ["VA"], ["VU"])
                strew(T.CF[:].indirect(T.TC[:]), T.NC[:], ["TC", "NC"], ["CF"])
                mask_table(1)
                mask_gather(0)
            else:
                ts(T.NE[:], pb("PG", NR), 0.0, OP.not_equal, ["PG"], ["NE"])
                upd_x()
                mm([(pb("PE", NR), pick(W_ALL, 7), T.NE[:], True, True)], ["NE", "BW"], ["PE"])
                for n in (3, 4, 5):
                    mask_gather(n)
        scan(T.PQ[:, 0, 1:257], T.RS0[:], pb("PA", 256), BIG, OP.add, OP.min, ["RS0", "PA"], [("PQ", 0, 1)])
        tt(T.ZZ[:], pb("PA", 256), T.PQ[:, 0, 0:256], OP.max, ["PA", ("PQ", 0, 1)], ["ZZ"])
        scan(T.PQ[:, 1, 1:257], T.RS1[:], T.ZZ[:], BIG, OP.add, OP.min, ["RS1", "ZZ"], [("PQ", 1, 2)])
        tt(T.R1[:], T.PQ[:, :, 16:257:16], T.SENT[:], OP.min, ["PQ", "SENT"], ["R1"])
        ts(T.R2[:, :, 0], T.R1[:, 0, :], 4080, OP.bitwise_and, ["R1"], [("R2", 0, 1)])
        ts(T.R2[:, :, 1], T.R1[:, 0, :], 15, OP.bitwise_and, ["R1"], [("R2", 1, 2)])
        ts(T.R2[:, :, 2], T.R1[:, 1, :], 16, OP.arith_shift_right, ["R1"], [("R2", 2, 3)])
        cp(T.TB[:, :, 0:3], T.R2[:, :, 0:3], [("R2", 0, 3)], [("TB", 0, 3)])
        tr(T.TBT[:], T.TB[:], ["TB"], ["TBT"])
        rows_mm("PC", 0)
        rows_mm("PD", 1)
        if st:
            rows_mm("PH", 2)
        if st == 2:
            mask_sum(0)
            mask_sum(1)
        tt(T.OF[:], T.R2[:, :, 0], T.R2[:, :, 1], OP.add, [("R2", 0, 2)], ["OF"])
        if st == 0:
            consts_act()
        if st < 2:
            cp(T.OU[:], T.OF[:], ["OF"], ["OU"])
        else:
            tt(T.CH[:, REPL], pb("PE", NR), T.CH[:, REPL], OP.max, ["PE", CR], [CR])
        cp(T.O16[:], pb("PC", 256), ["PC"], ["O16"])
        act(T.NW[:], pb("PD", 256), ["PD", cn(K_BST)], ["NW"], bias=col(K_BST))
        if st < 2:
            act(T.EG[:], SG.indirect(T.OU[:]), ["ST", "OU"], ["EG"])
        if st == 0:
            rows_mm("PC", 2)
        act(T.NC[:], pb("PH" if st else "PC", 256), ["PH" if st else "PC", cn(K_BCS)], ["NC"], bias=col(K_BCS), scale=64.0)
        if st < 2:
            to_psum_list("PB", 0, W_OWN, lambda i: T.EG[:, i::16], "EG")
        if st == 0:
            act(T.MT[:, 3:17], T.GW[:, 0:1792], ["GW"], [("MT", 3, 17)], scale=0.0)
        act(sm(6), T.CO[:, co, :], [("CO", co, co + 1)], [sn(6)], bias=float(C_), scale=-1.0)
        if st == 1:
            consts_order(1)
            blank(T.LX[:, 0:256], 256, ["LX"])
            mask_gather(1)
        if st == 2:
            mask_gather(6)
            mask_gather(7)
        for q in range(16):
            at, n = 8 * q * (q + 1), 16 * (q + 1)
            ts(T.GX[:, at:at + n], T.O16[:, 0:n], T.OF[:, q:q + 1], OP.is_equal, ["O16", "OF"], [("GX", at, at + n)], 2.0 ** -8, OP.mult)
        scan(T.CNT[:], T.D0[:, 0:2176], T.GX[:, 0:2176], 0.0, OP.mult, OP.add, ["D0", "GX"], ["CNT"])
        tt(sm(0), T.CNT[:].indirect(T.EL[:, 0:1]), T.JK[:, 0, :], OP.min, ["CNT", "EL", "JK"], [sn(0)])
        tt(sm(1), sm(0), T.OF[:], OP.max, [sn(0), "OF"], [sn(1)])
        cp(T.TG[:], sm(1), [sn(1)], ["TG"])
        cp(SG.indirect(T.TG[:]), T.NW[:], ["TG", "NW"], ["ST"])
        send_state(st)
        mine(T.ST[:, REPL], [SR])
        if st == 0:
            consts_later_g()
        if st == 1:
            x_gap(0)
            theirs(0, "PH", P_STALE, lambda d: T.LNS[:, 0, d, :], True)
            consts_plan_g()
        if st == 2:
            consts_lift_g()
        if st < 2:
            ts(sm(3), sm(1), 2047.5, OP.is_lt, [sn(1)], [sn(3)])
            ts(sm(4), T.OF[:], 2047.5, OP.is_lt, ["OF"], [sn(4)])
            tt(sm(5), sm(3), pb("PB", 16), OP.mult, [sn(3), "PB"], [sn(5)])
            tt(sm(4), sm(4), sm(3), OP.subtract, [sn(3), sn(4)], [sn(4)])
        ts(sm(2), sm(1), 2047.5, OP.is_gt, [sn(1)], [sn(2)])
        if st < 2:
            tt(sm(4), sm(4), T.CO[:, co, :], OP.mult, [sn(4), ("CO", co, co + 1)], [sn(4)])
        tt(sm(2), sm(2), T.JK[:, 1, :], OP.mult, [sn(2), "JK"], [sn(2)])
        if st < 2:
            tt(T.CO[:, cx, :], sm(4), sm(5), OP.add, [sn(4), sn(5)], [("CO", cx, cx + 1)])
        tt(sm(2), sm(2), sm(6), OP.max, [sn(2), sn(6)], [sn(2)])
        if st < 2:
            turn_list(cx)
            lane_rows()
            strengths()
            key_start()
        cp(T.TC[:], sm(2), [sn(2)], ["TC"])
        if st == 0:
            mask_table(0)
            consts_order(0)
        else:
            strew(T.CF[:].indirect(T.TC[:]), T.NC[:], ["TC", "NC"], ["CF"])
        if st == 1:
            mask_gather(2)
            tt(T.LOSE[:, 0, :], T.LOSE[:, 0, :], pb("PH", NR), OP.is_gt, ["PH", ("LOSE", 0, 1)], [("LOSE", 0, 1)])
            taken("PG", 0)
        if st < 2:
            lane_fields(cx)
        if st == 2:
            act(T.CS[:], T.CF[:], ["CF"], ["CS"], scale=1.0 / 64)
            cp(T.VH[:], T.VHI[:], ["VHI"], ["VH"])
            for j, bank in enumerate(("PA", "PC", "PD")):
                stale_x(512 * j, 512 * j + 512, bank)
        k = min(st, 1)
        theirs(st, "PE", P_SCORE, lambda d: T.LNS[:, st, d, :])
        theirs(st, "PF", P_ST, lambda d: T.LNS[:, st, d, :])
        lose(k)
        taken("PF", k)
        if st < 2:
            upd_st()
        if st == 0:
            dma("s", "vh", [(T.VHI[j % 4::4, j // 4, :], T.va[j::16, 0:768]) for j in range(16)], ["LOSE"], ["VHI"])
        if st == 1:
            dma("s", "xv", [(T.XW[:, 0:H_], T.xv[:, 0:H_])], ["LOSE"], [("XW", 0, H_)])
            dma("s", "kc", [(T.KK[:, 0:C_], T.kc[:])], [], [("KK", 0, C_)])

    def lift(nv, kind, start, extra, late=None, skip=0):
        win = T.CH[:]
        over = 768 - nv
        left, ajobs, rest = over - 96, [], []
        for h, j, lo, hi in ((0, 1, 0, 96), (0, 2, 0, 96), (1, 2, 0, 32), (1, 2, 64, 96), (1, 1, 64, 96)):
            mid = lo + min(hi - lo, left)
            left -= mid - lo
            ajobs += [(j, h, lo, mid)] if mid > lo else []
            rest += [(h, j, mid, hi)] if hi > mid else []
        ajobs += [("plain", u, 0, 96) for u in range(8 + skip, 16)]
        vjobs = sorted([(0, 0, 0, 96), (0, 3, 0, 96), (1, 0, 0, 96)] + rest)

        def red(s, form, u, lo, hi, last=False):
            mm([(pb("PH", hi - lo, lo), pick(kind, u if form == "plain" else 2 * (k // 4) + u), T.GR[:, s, 16 * lo + k:16 * hi:16],
                 False, last and k == 15) for k in range(16)], ["BW", ("GR", 96 * s + lo, 96 * s + hi)], ["PH"])

        def ajob(s, form, u, lo, hi):
            ls = T.VU[:, 96 * (u - 8) + lo:96 * (u - 8) + hi] if form == "plain" else T.VH[:, form, 96 * u + lo:96 * u + hi]
            op("a", lambda: a.activation(T.GR[:, s, 16 * lo:16 * hi], win.indirect(ls), AF.Relu), ["CH", "VU", "VH"],
               [("GR", 96 * s + lo, 96 * s + hi)])

        def vjob(h, j, lo, hi, s=None):
            acc, nm = T.GR[:, 3 + h, 16 * lo:16 * hi], ("GR", 96 * (3 + h) + lo, 96 * (3 + h) + hi)
            src = win.indirect(T.VH[:, j, 96 * h + lo:96 * h + hi])
            if j == 0:
                ts(acc, src, 0.0, OP.max, ["CH", "VH"], [nm])
            elif s is None:
                tt(acc, src, acc, OP.max, ["CH", "VH", nm], [nm])
            else:
                tt(T.GR[:, s, 16 * lo:16 * hi], src, acc, OP.max, ["CH", "VH", nm], [("GR", 96 * s + lo, 96 * s + hi)])

        ends = []
        for e, at, jobs in (("a", 0, ajobs), ("v", C_ - 96 * skip - 2 * nv + 48, vjobs)):
            for n, job in enumerate(jobs):
                at += job[3] - job[2]
                ends.append((at, e, n))
        bank = "PF" if kind == W_7 else "PA"
        if kind != W_7:
            mask_test(0, skip, kind, bank)
        ajob(0, *ajobs[0])
        start()
        extra()
        if kind == W_7:
            mask_test(0, skip, kind, bank)
            mm([(pb("PE", 96), pick(W_OUT, u), T.CS[:, 96 * u:96 * u + 96], u == 0, u == 15) for u in range(16)], ["BW", "CS"], ["PE"])
        else:
            early_blocks(2)
        for at, e, n in sorted(ends):
            if e == "a":
                if n:
                    ajob(n % 3, *ajobs[n])
                red(n % 3, *ajobs[n])
                if n == 2 and late is outputs_late:
                    owners_now()
                if n == 2 and kind == W_7:
                    for j, bk in enumerate(("PA", "PC", "PD")):
                        inputs_only(512 * j, 512 * j + 512, bk, 1)
            else:
                h, j, lo, hi = vjobs[n]
                vjob(h, j, lo, hi)
                if j == 3:
                    red(3 + h, "fold", h, lo, hi)
                    mask_test(2, skip, kind, bank)
                if n == 0:
                    mask_test(1, skip, kind, bank)
                if n == (0 if kind == W_7 else 3) and late:
                    late()
        for n, (j, la, lv) in enumerate(((1, 32, 64), (1, 0, 32), (2, 32, 0))):
            s = (len(ajobs) % 3, 3, (len(ajobs) + 1) % 3)[n]
            ajob(s, j, 1, la, la + 32)
            vjob(1, 3, lv, lv + 32, s)
            red(s, "fold", 1, min(la, lv), min(la, lv) + 64, n == 2)

    def stolen_flags():
        mm([(pb("PH", 96), pick(W_7, u), T.CS[:, 96 * u:96 * u + 96], u == 0, False) for u in range(16)], ["BW", "CS"], ["PH"])

    def kept_flags():
        mm([(pb("PH", 96), mt(M_IB), T.FK[:], False, False)] +
           [(pb("PH", 96), pick(W_7, u), T.FLR[:, 96 * u:96 * u + 96], False, False) for u in range(16)],
           [mn(M_IB), "FK", "BW", "FLR"], ["PH"])

    def after_steals():
        upd_st()
        ms(T.VB[:, C_:1544], 0, [("VB", C_, 1544)])
        for j, bank in enumerate(("PA", "PC", "PD")):
            inputs_only(512 * j, 512 * j + 512, bank, 0)
        stale_x(1536, V_, "PE")
        for b in range(2, NB):
            mask_sum(b)

    def last_outputs():
        for j, bank in ((1, "PC"), (2, "PD")):
            inputs_only(512 * j, 512 * j + 512, bank, 2)
        cp(T.OFF[:], pb("PE", 96), ["PE"], ["OFF"])
        cp(T.OFL[:], T.OFF[:], ["OFF"], ["OFL"])

    def after_plan():
        taken("PF", 1)

    def updates():
        upd_x()
        upd_st()

    def outputs():
        after_plan()
        updates()
        mm([(pb("PD", 128), pick(W_W, u), T.ST[:, 128 * u:128 * u + 128], u == 0, u == 15) for u in range(16)], ["BW", "ST"], ["PD"])
        ts(T.GW[:, H_:V_], T.XW[:, REPL], 256.0, OP.min, ["XW"], [("GW", H_, V_)])
        dma("s", "y", [(T.y[:], T.GW[:, 0:V_])], ["GW"], [])
        cp(T.GX[:, 0:C_], SG.indirect(T.OFL[:]), ["ST", "OFL"], ["GX"])

    def owners_now():
        mm([(pb("PC", 96), pick(W_OWN, u), T.GX[:, u:C_:16], u == 0, u == 15) for u in range(16)], ["BW", "GX"], ["PC"])

    def outputs_late():
        cp(T.YWB[:], pb("PD", 128), ["PD"], ["YWB"])
        dma("s", "yw", [(T.yw[:], T.YWB[:])], ["YWB"], [])
        tt(T.YOB[:, 0, :], pb("PC", 96), T.CJ[:, 1, :], OP.not_equal, ["PC", "CJ"], ["YOB"])
        ts(T.YOB[:, 0, :], T.YOB[:, 0, :], 2048.0, OP.mult, ["YOB"], ["YOB"])
        tt(T.YOB[:, 1, :], T.YOB[:, 0, :], T.OFF[:], OP.max, ["YOB", "OFF"], ["YOB"])
        dma("s", "yo", [(T.yo[:], T.YOB[:, 1, :])], ["YOB"], [])

    upd_ch("PF")
    lift(SHARE[0], W_7, stolen_flags, after_steals, last_outputs, NB)
    inputs_only(0, 512, "PA", 2)

    def key_mm(lo, hi):
        mm([(pb("PA", hi - lo, lo), pick(W_W, k), T.GW[:, 16 * lo + k:16 * hi:16], k == 0, k == 15) for k in range(16)],
           ["BW", ("GW", 16 * lo, 16 * hi)], ["PA"])

    def least(lo, hi):
        scan(T.GX[:, 16 * lo:16 * hi], T.RS4[:, 0:16 * (hi - lo)], T.GW[:, 16 * lo:16 * hi], 0.0, OP.max, OP.min,
             ["RS4", ("GW", 16 * lo, 16 * hi)], [("GX", 16 * lo, 16 * hi)])

    def sum_mm(lo, hi, last):
        mm([(pb("PC", hi - lo, lo), mt(M_NI), T.GX[:, 16 * lo + k:16 * hi:16], False, last and k == 15) for k in range(16)],
           [("GX", 16 * lo, 16 * hi)], ["PC"])

    ENDS = T.SC[:, 15::16]

    for t in range(3):
        fill(T.FLR[:], WC, 0, ["FLR"])
        fill(T.CH[:], WV, 0, ["CH"])
        ts(T.FL[:], pb("PH", 96), 0.0, OP.is_gt, ["PH"], ["FL"])
        scan(T.INC[:], T.ONE[:, 0:96], T.FL[:], 0.0, OP.mult, OP.add, ["ONE", "FL"], ["INC"])
        tot, mid = T.INC[:, 95:96], T.INC[:, 47:48]
        if t == 1:
            mm([(T.PC[:, 0, 0:1], mt(M_LA), tot, True, False), (T.PC[:, 0, 0:1], mt(M_RS), mid, False, True),
                (T.PC[:, 0, 1:2], mt(M_LB), tot, True, False), (T.PC[:, 0, 1:2], mt(M_RS), mid, False, True)], ["INC", "MT"], ["PC"])
        else:
            mm([(T.PC[:, 0, 0:1], mt(M_T0 if t == 0 else M_T2), tot, True, True)], ["INC", "MT"], ["PC"])
        tt(pb("PD", 96), T.CJ[:, 2 + t, :], pb("PH", 96), OP.subtract, ["PH", "CJ"], ["PD"])
        tt(T.RR[:], pb("PD", 96), T.INC[:], OP.max, ["PD", "INC"], ["RR"])
        for lo, hi, hf in (((0, 48, 0), (48, 96, 1)) if t == 1 else ((0, 96, 0),)):
            ts(T.PS[:, lo:hi], T.RR[:, lo:hi], T.PC[:, 0, hf:hf + 1], OP.add, ["RR", "PC"], [("PS", lo, hi)], -1.0, OP.add)
        strew(T.LX[:].indirect(T.PS[:, 46:96]), T.CV[:, 736:C_], ["PS", "CV"], ["LX"])
        cp(T.LW[:].indirect(T.PS[:, 0:46]), T.CV[:, 0:736], ["PS", "CV"], ["LW"])
        tt(T.MK[:], T.LW[:, 0:256], DGP, OP.mult, ["LW", "PB"], ["MK"])
        tt(T.MX[:], T.LX[:, 0:256], DGP, OP.mult, ["LX", "PB"], ["MX"])
        scan(T.SD[:, 16:272], T.MK[:], T.MX[:], 0.0, OP.add, OP.add, ["MK", "MX"], [("SD", 16, 272)])
        tt(sm(0), T.SD[:, 31::16], T.SD[:, 15:256:16], OP.subtract, ["SD"], [sn(0)])
        ts(T.LN[:], sm(0), -1.0 / 256, OP.mult, [sn(0)], ["LN"], C_ + 0.25, OP.add)
        if t < 2:
            fill(T.LW[:, 0:256], 256, 0, ["LW"])
            fill(T.LX[:, 0:256], 256, 0, ["LX"])
        cp(T.ROWS[:], T.VB[:].indirect(T.LN[:]), ["VB", "LN"], ["ROWS"])
        act(T.CSG[:], T.CS[:].indirect(T.LN[:]), ["CS", "LN"], ["CSG"])
        to_psum_list("PH", 0, W_OUT, lambda i: T.CSG[:, i::16], "CSG")
        act(T.KG[:], T.KK[:].indirect(T.LN[:]), ["KK", "LN"], ["KG"])
        mm([(pb("PC", 256), mt(M_I), T.KG[:], True, False)], ["KG", "MT"], ["PC"])
        mm([(pb("PE", 256), mt(M_OW), T.CSG[:], True, False)], ["CSG", "MT"], ["PE"])
        gath("v", "GX", XG, "XW", 0, 40)
        cp(T.OU[:], pb("PH", 16), ["PH"], ["OU"])
        gath("a", "GX", XG, "XW", 40, 64)
        sum_mm(0, 64, False)
        act(T.EG[:], SG.indirect(T.OU[:]), ["ST", "OU"], ["EG"], scale=-1.0)
        mm([(pb("PE", 256), mt(M_OW), T.EG[:], False, True)], ["EG", "MT"], ["PE"])
        gath("v", "GX", XG, "XW", 64, 104)
        gath("a", "GX", XG, "XW", 104, 128)
        op("a", lambda: a.activation(T.OWN[:], pb("PE", 256), AF.Abs), ["PE"], ["OWN"])
        sum_mm(64, 128, False)
        gath("v", "GX", XG, "XW", 128, 160)
        gath("a", "GX", XG, "XW", 160, 192)
        mm([(pb("PC", 256), mt(M_NO), T.OWN[:], False, False)], ["OWN", "MT"], ["PC"])
        sum_mm(128, 192, False)
        gath("v", "GX", XG, "XW", 192, 224)
        gath("a", "GX", XG, "XW", 224, 256)
        sum_mm(192, 256, True)
        mm([(pb("PD", 256), T.KM[0:1, 5], T.ONE[0:1, 0:256], True, False)], ["KM", "ONE"], ["PD"])
        act(T.XO[:], XG.indirect(T.OU[:]), ["XW", "OU"], ["XO"])
        gath("v", "GW", SG, "ST", 0, 64)
        key_mm(0, 64)
        gath("a", "GW", SG, "ST", 64, 128)
        tt(T.MK[:], pb("PC", 256), T.DGM[:], OP.mult, ["PC", "DGM"], ["MK"])
        scan(T.SC[:], T.M0[:], T.MK[:], 0.0, OP.mult, OP.add, ["M0", "MK"], ["SC"])
        ts(T.NX[:, 0, :], pb("PC", 256), 65536.0, OP.add, ["PC"], [("NX", 0, 1)])
        ts(sm(2), ENDS, WAITS, OP.is_lt, ["SC"], [sn(2)])
        ts(T.NX[:, 1, :], T.NX[:, 0, :], 255, OP.bitwise_and, [("NX", 0, 1)], [("NX", 1, 2)])
        tt(sm(3), sm(2), T.JK[:, 0, :], OP.mult, [sn(2), "JK"], [sn(3)])
        key_mm(64, 128)
        gath("a", "GW", SG, "ST", 128, 192)
        key_mm(128, 192)
        tt(sm(3), sm(3), pb("PH", 16), OP.max, [sn(3), "PH"], [sn(3)])
        cp(T.TG[:], sm(3), [sn(3)], ["TG"])
        cp(XG.indirect(T.TG[:]), T.NX[:, 1, :], ["TG", ("NX", 1, 2)], ["XW"])
        send_x(1 + t)
        gath("a", "GW", SG, "ST", 192, 230)
        gath("v", "GW", SG, "ST", 230, 256)
        tt(T.DF[:], T.NX[:, 1, :], T.XO[:], OP.not_equal, [("NX", 1, 2), "XO"], ["DF"])
        strew(T.CH[:].indirect(T.TG[:]), T.DF[:], ["TG", "DF"], ["CH"])
        act(T.CHB[:], T.CH[:, REPL], [CR], ["CHB"])
        early_blocks(0)
        tr(T.TT[:, 0:192], pb("PA", 192), ["PA"], ["TT"])
        scan(T.P2[:, 0:192], T.RS0[:, 0:192], T.TT[:, 0:192], BIG, OP.add, OP.min, ["RS0", "TT"], ["P2"])
        least(230, 256)
        least(192, 230)
        tr(T.P2T[:, 0:192], T.P2[:, 0:192], ["P2"], ["P2T"])
        mm([(pb("PD", 64, 192), mt(M_B0), T.GX[:, 16 * 192 + 15::16], False, False),
            (pb("PD", 192), mt(M_B15), T.P2T[:, 0:192], False, True)], ["GX", "P2T", "MT"], ["PD"])
        mm([(pb("PA", NR), T.ONE[0:1, 0:128], T.TIE[0:1, :], True, False), (pb("PA", NR), mt(M_IB), T.CHB[:], False, False)],
           ["MT", "CHB"], ["PA"])
        x_gap(1 + t)
        tt(T.NW[:], pb("PD", 256), T.CSG[:], OP.min, ["PD", "CSG"], ["NW"])
        cp(SG.indirect(T.TG[:]), T.NW[:], ["TG", "NW"], ["ST"])
        send_state(3 + t)
        mine(T.ST[:, REPL], [SR])
        mm([(pb("PA", NR), mt(M_N1), T.ST[:, REPL], False, False)], [SR, "MT"], ["PA"])
        early_blocks(1)
        cp(sm(5), T.LN[:], ["LN"], [sn(5)])
        ts(sm(4), ENDS, NO_OUTPUT, OP.is_lt, ["SC"], [sn(4)])
        ts(T.NF[:], T.PS[:], 255.5, OP.is_gt, ["PS"], ["NF"])
        tt(sm(4), sm(2), sm(4), OP.is_equal, [sn(2), sn(4)], [sn(4)])
        tt(sm(4), sm(4), T.JK[:, 1, :], OP.mult, [sn(4), "JK"], [sn(4)])
        tt(T.FK[:], T.NF[:], T.FL[:], OP.mult, ["NF", "FL"], ["FK"])
        tt(sm(4), sm(4), sm(5), OP.max, [sn(4), sn(5)], [sn(4)])
        cp(T.TC[:], sm(4), [sn(4)], ["TC"])
        cp(T.FLR[:].indirect(T.TC[:]), T.ONE[:, 0:256], ["TC", "ONE"], ["FLR"])
        if t == 2:
            ts(T.GW[:, 0:H_], T.XW[:, 0:H_], 256.0, OP.min, ["XW"], [("GW", 0, H_)])
        tt(T.NE[:], pb("PG", NR), T.CH[:, REPL], OP.not_equal, ["PG", CR], ["NE"])
        for bank, kind in (("PE", P_SCORE), ("PA", P_SCORE), ("PF", P_ST)):
            theirs(3 + t, bank, kind, lambda d: T.LNS[:, 3 + t, d, :])
        lose(1)
        taken("PG", 1)
        tt(T.CH[:, REPL], pb("PA", NR), T.NE[:], OP.min, ["PA", "NE"], [CR])
        if t < 2:
            lift(SHARE[1 + t], W_ALL, kept_flags, after_plan, None, NP)
            updates()
        else:
            lift(SHARE[3], W_ALL, kept_flags, outputs, outputs_late, NP)
    ts(T.YFB[:], pb("PH", 96), 0.0, OP.is_gt, ["PH"], ["YFB"])
    dma("s", "yf", [(T.yf[:], T.YFB[:])], ["YFB"], [])
    for s in count:
        need("g", (s, count[s]))
